import numpy as np, ml_dtypes
CORES = [40,64,80,88,96,104,120,144]
N = 8
BF = ml_dtypes.bfloat16
L, H, M, E, HO, RO, C, R, ST, QO = 4096, 2048, 256, 16, 4, 4, 16, 112, 341, 2048
def parts(rng):
    v = rng.integers(0, 256, (N, 8, 16, L)); m = np.argsort(rng.random((N, 8, H)), axis=-1) + H
    return v, m, rng.integers(0, 1024, (N, 8, 16, 1)), rng.integers(0, 2048, (N, 8, 16, E // 16)), rng.integers(780, 1081, (N, 8, 1))
def joined(rng, n):
    p = np.tile(np.arange(L), (N, 8, 1))
    for r in range(N):
        for g in range(8):
            o = rng.permutation(L); s = int(n[r, g]); p[r, g, o[:s]] = o[s:2 * s]; p[r, g, o[s:2 * s]] = o[:s]
    return p
def left(rng, n):
    p = np.tile(np.arange(L), (N, 8, 1))
    for r in range(N):
        for g in range(8):
            s = int(n[r, g]); a, b = rng.permutation(H)[s:], H + rng.permutation(H)[s:]; p[r, g, a] = b; p[r, g, b] = a
    return p
def shares(rng):
    return (rng.choice(np.array([0.0, 0.1, 0.25, 0.4, 0.475]), (N, 8)) * L).astype(np.int64)
def first_hop(v, w, k):
    u = np.add.reduce(w[:, None] * np.roll(v, 8, axis=0), axis=0) & (L - 1)
    return (((u * u) >> 5)[:, None] + u[:, None] * np.ascontiguousarray(k.T).reshape(1, -1)) & (L - 1)
def plant(rng, v, w, k, a, ok):
    pool = rng.integers(0, 256, (16, H)); src, to = [], []
    for j, cs in enumerate(first_hop(pool, w, k).tolist()):
        if len(to) == len(a): break
        for c in cs:
            if ok[c]:
                ok[c] = False; src.append(j); to.append(c); break
    x = pool[:, src]; v[:, a[:len(to)]] = x
    v[:, to] = np.clip(np.roll(x, 8, axis=0) + rng.integers(-2, 3, x.shape), 0, 255)
    return np.array(to, np.int64)
def pack(v, p, m, w, k, t):
    return {"rec": np.ascontiguousarray(v.reshape(N, 128, L)).astype(np.float32).astype(BF), "pr": p.astype(np.int32), "mt": m.astype(np.int32),
            "w": w.reshape(N, 128, 1).astype(np.int32), "kk": np.ascontiguousarray(k.reshape(N, 128, E // 16)).astype(np.int32), "th": t.astype(np.int32)}
def setup_inputs(rng):
    v, m, w, k, t = parts(rng)
    return pack(v, joined(rng, shares(rng)), m, w, k, t)
def setup_inputs_room(rng):
    v, m, w, k, t0 = parts(rng)
    n = rng.choice(np.array([0, 1, C - 1, C, R - 1, R, R + 1, M - 1, M, M + 1, H]), (N, 8))
    n[0] = R; n[0, 6:] = np.array([1, M - 1]); n[1] = np.array([R, R + 1, R - 1, R, C, M, M + 1, 0]); n[N - 1] = R; n[N - 1, 6:] = np.array([C - 1, H])
    n[2] = rng.choice(np.array([M, M + 1, 2 * M]), 8); n[2, :2] = np.array([M, M + 1])
    t = np.where(rng.random((N, 8, 1)) < 0.5, 0, t0); t[0, :6] = 0; t[1, :4] = 0; t[N - 1, :6] = 0; t[2] = t0[2]; t[1, 5] = t0[1, 5]
    p = left(rng, n); every = np.arange(L)
    for g in range(8):
        a = np.nonzero(p[2, g, :H] == every[:H])[0][:M]
        plant(rng, v[2, g], w[2, g, :, 0], k[2, g], a, ((every >= H) & (p[2, g] != every)).tolist())
    o = rng.permutation(H); a = o[:M // 2]; ok = np.zeros(L, bool); ok[o[M // 2:]] = True
    s = np.concatenate([a, plant(rng, v[1, 5], w[1, 5, :, 0], k[1, 5], a, ok.tolist())])
    rest = np.setdiff1d(every[:H], s); b = H + rng.permutation(H)[:len(rest)]
    p[1, 5] = every; p[1, 5, rest] = b; p[1, 5, b] = rest
    return pack(v, p, m, w, k, t)
def setup_inputs_ties(rng):
    v, m, w, k, t = parts(rng); v = 64 * rng.integers(0, 4, v.shape); t = 64 * rng.integers(10, 17, t.shape)
    v[:, 1::2] = v[:, 1::2][..., rng.integers(0, 64, L)]
    return pack(v, joined(rng, shares(rng)), m, w, k, t)
def setup_inputs_alike(rng):
    v, m, w, k, t = parts(rng); n = shares(rng); n[:, 0] = 0; p = joined(rng, n)
    w[:, 0] = 0; t[:, 0] = 1600
    for r in range(1, N):
        t[r, 0] = 4095; v[r, 0] = rng.integers(0, 40 if r % 2 == 0 else 120, (16, L))
        v[r, 0, :, 0] = 255; v[r, 0, :, 1] = 0
    v[1, 0, :, 1:] = 0
    k[:, 1] = k[:, 1, :1, :1]; t[:, 1] = 1200
    v[:, 2] = rng.integers(0, 256, (N, 1, 1)); v[::2, 2] = rng.integers(0, 256, (v[::2, 2].shape[0], 16, 1)); t[:, 2] = 1
    v[:, 3] = v[:, 3][..., rng.integers(0, 8, L)]
    m[:, 4] = H + np.arange(H); p[:, 4] = np.arange(L); o = rng.permutation(H)[:H // 2]; p[:, 4, o] = o + H; p[:, 4, o + H] = o
    for z in (v, m, w, k, t, p): z[:, 5] = z[:1, 5]
    k[:, 6] = 0; t[:, 6] = 1300
    for r in range(N):
        old = v[r, 6].copy(); c, j = np.unique(first_hop(old, w[r, 6, :, 0], k[r, 6])[:, 0], return_index=True); v[r, 6][:, c] = old[:, j]
    o = np.arange(20, H - 20); p[:, 7] = np.arange(L)
    for r in range(N):
        b = H + rng.permutation(H)[:H - 40]; p[r, 7, o] = b; p[r, 7, b] = o
    return pack(v, p, m, w, k, t)
def setup_inputs_ends(rng):
    v, m, w, k, t = parts(rng)
    v = np.where(rng.random((N, 8, 1, L)) < 0.5, rng.choice(np.array([0, 0, 1, 254, 255, 255]), v.shape), v)
    w[:, ::2] = rng.choice(np.array([1, 1022, 1023]), (N, 4, 16, 1)); k[:, 1::2] = rng.choice(np.array([0, 1, 2046, 2047]), (N, 4, 16, E // 16))
    t = rng.choice(np.array([1, 4080, 4081, 4094, 4095]), t.shape); t[0, 0] = 4095; t[N - 1, 1] = 4095
    v[:, 3, :, ::7] = 255; v[:, 3, :, 1::7] = 0
    v[:, 4] = rng.integers(240, 256, (N, 16, L)); v[:, 4, :, ::9] = 255; t[:, 4] = 4080
    w[:, 4] = rng.integers(1022, 1024, (N, 16, 1)); w[::2, 4] = 1023
    return pack(v, joined(rng, shares(rng)), m, w, k, t)
def setup_inputs_spread(rng):
    v, m, w, k, t = parts(rng)
    v = (rng.random((N, 8, 16, L)) * np.exp2(8 * rng.random((N, 8, 1, L)))).astype(np.int64); w = np.exp2(10 * rng.random(w.shape)).astype(np.int64)
    k = np.exp2(11 * rng.random(k.shape)).astype(np.int64); t = np.minimum(np.exp2(7 + 5 * rng.random(t.shape)).astype(np.int64), 4095)
    return pack(np.minimum(v, 255), joined(rng, shares(rng)), m, np.minimum(w, 1023), np.minimum(k, 2047), t)
def check_inputs(d):
    bad = []; v = np.asarray(d["rec"]).astype(np.float32)
    if not np.all((v >= 0) & (v <= 255) & (v == np.floor(v))): bad.append("rec: whole numbers from 0 to 255")
    for k, lo, hi in (("pr", 0, L - 1), ("mt", H, L - 1), ("w", 0, 1023), ("kk", 0, 2047), ("th", 0, 4095)):
        if np.min(d[k]) < lo or np.max(d[k]) > hi: bad.append("range of " + k)
    p = np.clip(np.asarray(d["pr"]).astype(np.int64), 0, L - 1)
    if not np.all(np.take_along_axis(p, p, -1) == np.arange(L)): bad.append("pr: a partner's partner is the leaf itself")
    if not np.all(np.sort(np.asarray(d["mt"]), axis=-1) == np.arange(H, L)): bad.append("mt: each leaf of the second half once")
    return bad
def reference(rec, pr, mt, w, kk, th):
    G = N * 8; g = np.arange(G)[:, None]; X = (np.arange(16) + 8) & 15
    q = np.ascontiguousarray(np.asarray(rec).astype(np.float32).astype(np.int32).reshape(G, 16, L).transpose(0, 2, 1))
    p = pr.astype(np.int64).reshape(G, L); first = mt.astype(np.int64).reshape(G, H)
    m = np.zeros((G, L), np.int64); m[:, :H] = first; m[g, first] = np.arange(H)
    wv = w.astype(np.int64).reshape(G, 1, 16); kv = np.ascontiguousarray(kk.astype(np.int64).reshape(G, 16, E // 16).transpose(0, 2, 1)).reshape(G, 1, E)
    t0 = th.astype(np.int64).reshape(G); J = np.repeat(t0[:, None], L, axis=1); lane = np.arange(M)
    for t in range(RO):
        order = (ST * t + np.arange(H)) & (H - 1)
        loose = (p[:, order] == order).astype(np.int64); place = np.add.accumulate(loose, axis=1) - 1
        gi, ci = np.nonzero((loose == 1) & (place < M))
        a = np.zeros((G, M), np.int64); live = np.zeros((G, M), bool); a[gi, place[gi, ci]] = order[ci]; live[gi, place[gi, ci]] = True
        A = q[g, a][:, :, X]; y = A; bd = np.full((G, M), 1 << 20); bc = np.zeros((G, M), np.int64)
        for h in range(HO):
            u = np.add.reduce(wv * y, axis=2) & (L - 1)
            c = (((u * u) >> 5)[:, :, None] + kv * u[:, :, None]) & (L - 1)
            D = np.add.reduce(np.abs(q[g[:, :, None], c] - A[:, :, None, :]), axis=3)
            D = np.where(c == a[:, :, None], 4095, D)
            e = np.argmin(D, axis=2)[:, :, None]
            D = np.take_along_axis(D, e, 2)[:, :, 0]; c = np.take_along_axis(c, e, 2)[:, :, 0]
            bc = np.where(D < bd, c, bc); bd = np.where(D < bd, D, bd)
            y = (A + q[g, m[g, p[g, c]]]) >> 1
        prop = live & (bd < J[g, bc]); key = M * bd + lane
        least = np.full((G, L), 1 << 30); gi, li = np.nonzero(prop)
        np.minimum.at(least, (gi, a[gi, li]), key[gi, li]); np.minimum.at(least, (gi, bc[gi, li]), key[gi, li])
        stand = prop & (least[g, a] == key) & (least[g, bc] == key)
        gi, li = np.nonzero(stand); sa, sc, sd = a[gi, li], bc[gi, li], bd[gi, li]
        old = p[gi, sc]; p[gi, old] = old; J[gi, old] = t0[gi]
        p[gi, sa] = sc; p[gi, sc] = sa; J[gi, sa] = sd; J[gi, sc] = sd
        va, vc = q[gi, sa], q[gi, sc]
        q[gi, sa] = va + np.clip(vc[:, X] - va, -1, 1); q[gi, sc] = vc + np.clip(va[:, X] - vc, -1, 1)
        no = live & (p[g, a] == a); place = np.add.accumulate(no.astype(np.int64), axis=1) - 1
        gi, li = np.nonzero(no & (place < R)); s = np.zeros((G, R), np.int64); has = np.zeros((G, R), bool)
        s[gi, place[gi, li]] = a[gi, li]; has[gi, place[gi, li]] = True
        v = q[g, s]; come = np.zeros_like(v); there = np.zeros_like(has); i = np.arange(G)
        for d in range(1, N):
            src = ((i // 8 - d) % N) * 8 + ((i - d) & 7); b = slice((d - 1) * C, d * C)
            come[:, b] = v[src, b]; there[:, b] = has[src, b]
        gi, k = np.nonzero(has & there); q[gi, s[gi, k]] = come[gi, k]
        gi, k = np.nonzero(has[:, 1::2]); x, z = s[gi, 2 * k], s[gi, 2 * k + 1]; mx, mz = m[gi, x], m[gi, z]
        m[gi, x] = mz; m[gi, z] = mx; m[gi, mx] = z; m[gi, mz] = x
        hx, hz, hmx, hmz = q[gi, x, 8:], q[gi, z, 8:], q[gi, mx, 8:], q[gi, mz, 8:]
        q[gi, x, 8:] = hz; q[gi, z, 8:] = hx; q[gi, mx, 8:] = hmz; q[gi, mz, 8:] = hmx
    yq = np.ascontiguousarray(q[:, :QO].transpose(0, 2, 1)).reshape(N, 128, QO)
    return {"yq": yq.astype(np.float32).astype(BF), "yp": p.reshape(N, 8, L).astype(np.float32), "ym": np.ascontiguousarray(m[:, :H]).reshape(N, 8, H).astype(np.float32)}

@@ -1,0 +1,541 @@
+import numpy as np
+from concourse.bass import DstId, RemoteDMATransfer
+from concourse.mybir import AluOpType as O, AxisListType, ActivationFunctionType as F
+
+TW, D1, D2 = 4608, 4096, 4352
+B, H16, F4, I4, U2 = "bfloat16", "float16", "float32", "int32", "uint16"
+_S = dict(
+    Q=(TW, B), S1=(TW, B), S2=(TW, B), BITS=(TW, B), CT=(4096, F4), MPT=(4096, B), VT=(2048, B), UR=(4096, H16),
+    X0=(2048, B), X1=(2048, B), M0=(2048, B), M1=(2048, B), IND=(2048, B), SB=(2048, B), SA=(2048, B), RB=(448, B), HB=(64, B),
+    CF=(64, F4), CI=(32, I4), OH=(16, F4), DD=(16, F4), IO=(160, F4), IW=(160, B), WB=(144, B), Wp=(144, B), Wmp=(144, B), Wix=(144, B),
+    Wf=(144, B), Wg=(144, B), Ww=(144, H16), Wv=(144, H16), MAT=(2304, B), I32=(128, F4), I16=(256, H16), PI2=(256, B), HI2=(256, B), GM=(128, B),
+    I16c=(256, B), MASK=(256, B), MNG=(256, B), CS=(256, B), RK=(256, F4), RS=(256, B), IL=(256, B), ONE=(256, B), LW=(16, F4), KC=(16, H16), KL=(128, H16),
+    CO=(256, F4), UL=(64, U2), TI=(256, I4), TJ=(512, I4), TF=(512, F4), TG=(512, F4), TB=(2048, B), TM=(512, B), TU=(256, H16), BT=(512, B),
+    PLi=(256, I4), MTi=(128, I4), MTu=(128, U2), PWu=(256, U2), NB=(1024, B), LP=(512, B), LM=(512, B), YO=(768, F4),
+    FWb=(128, B), CE=(128, F4), C3=(136, F4), SM=(256, F4), SS=(256, F4), SW=(128, F4), cu=(16, U2), aW=(16, U2), dR=(256, B), XI=(256, B),
+    va=(256, B), y=(256, H16), AO=(256, F4), AB=(256, B), aR=(256, F4), SAT=(32, F4), S1a=(256, B), S1c=(256, B), S2c=(256, B), vc=(256, B),
+    BB=(512, B), BL=(512, B), ui=(32, I4), uo=(16, U2), co=(256, U2), cF=(256, F4), hB=(256, B), eq=(256, B), SC=(512, F4), KI=(128, I4),
+    KJ=(128, I4), lo=(32, I4), E=(512, B), cw=(16, U2), mg=(256, B), mo=(16, U2), DW=(104, I4), Di=(64, I4), TH=(32, F4), MN=(32, F4), LS=(32, F4),
+    st=(64, F4), E2=(256, B), RE=(512, B), RO=(512, B), JK=(1536, B), BA=(48, F4), DF=(48, F4), OT=(128, F4), OF=(48, U2),
+    no=(512, B), po=(16, U2), VAL=(768, B), QV=(512, B), dn=(256, B), P6=(96, F4), O2=(40, U2), V2=(384, B), G6=(768, B), R6=(768, B))
+SCRATCH = {k: ("sbuf", [128, n], d) for k, (n, d) in _S.items()}
+SCRATCH["PS"] = ("psum", [128, 4096], F4)
+NDMA = 60
+SEMAPHORES = ["pe", "dve", "act", "pool", "snt"] + ["arr%d" % t for t in range(4)] + ["hin%d" % t for t in range(4)] + ["d%d" % i for i in range(NDMA)]
+INFO = {}
+GA, SCA, FIX, GAP, PEC, WAY = 1.56, 3.8, 0.06, 0.15, 0.5e-3, 7.0
+LOOK, ITER, NOISE, NACT = 0.1, 24, 1.0, 8
+SUB = ((0, 32), (32, 64), (64, 96), (96, 128))
+
+
+def routes(T, topo, r):
+    me = T.cores[r]; n = len(T.cores); direct = []; far = []
+    for d in range(1, n):
+        c = T.cores[(r + d) % n]
+        (direct if topo.may_write(me, c) else far).append((d, c))
+    off = topo.engines(me, direct[0][1])
+    hs = [h for h in topo.cores_of(me) if h != me and all(topo.may_write(h, c) for _, c in far)]
+    hs.sort(key=lambda h: topo.die(h) != topo.die(me))
+    on = [e for e in topo.engines(me, hs[0]) if e not in off]
+
+    def deal(es, k):
+        sz = [1] * k
+        while sum(sz) + min(sz) <= len(es):
+            j = sz.index(min(sz)); sz[j] *= 2
+        out = []; p = 0
+        for z in sorted(sz, reverse=True):
+            out.append(sum(1 << e for e in es[p:p + z])); p += z
+        return out
+    return ([(d, c, None, m) for (d, c), m in zip(direct, deal(off, len(direct)))]
+            + [(d, c, h, m) for (d, c), h, m in zip(far, hs, deal(on, len(far)))])
+
+
+def relay(g, core, T, topo):
+    for r in range(len(T.cores)):
+        for d, c, h, m in routes(T, topo, r):
+            if h == core:
+                rid, pid = topo.addr(c, core); mk = topo.mask(core, c)
+                for t in range(4):
+                    g.wait_ge(T.sem["hin%d" % t], bin(m).count("1"))
+                    k = 112 * t + 16 * (d - 1)
+                    g.remote_dma_fused([RemoteDMATransfer(dst_ids=[DstId(rid=rid, pnc=pid)], dma_engine_mask=mk, remote_sem=T.sem["arr%d" % t],
+                                                          src=T.HB[:, 16 * t:16 * t + 16], dst=T.RB[:, k:k + 16])], local_sem=T.sem.snt)
+                g.wait_ge(T.sem.snt, 4 * bin(mk).count("1"))
+
+
+def rank_program(g, core, T, topo):
+    r = T.rank_of(core)
+    if r is None:
+        relay(g, core, T, topo)
+        return
+    ops = []; hist = {}
+
+    def A(n, a, b, s=1, p=(0, 128), reg=None):
+        ap = T[n][p[0]:p[1], a:b:s] if s > 1 else T[n][p[0]:p[1], a:b]
+        if n == "PS":
+            return (ap, [(n, a // 512 * 512, (b + 511) // 512 * 512)], [], len(range(a, b, s)), False, True)
+        return (ap, [(reg or n, a, b)], [], len(range(a, b, s)), _S[n][1] in (B, H16, U2), False)
+
+    def IX(w, o):
+        return (w[0].indirect(o[0]), w[1], o[1], 16 * o[3], False, False)
+
+    def X(ap):
+        return (ap, [], [], 0, False, False)
+    isop = lambda v: isinstance(v, tuple)
+    ap = lambda v: v[0] if isop(v) else v
+
+    def op(q, fn, outs, ins, cost, lat=0.0, kind="c", tag=None, ext=None, after=()):
+        i = len(ops); deps = {}
+        acc = []
+        for v in outs:
+            acc += [(x, True) for x in v[1]] + [(x, False) for x in v[2]]
+        for v in ins:
+            if isop(v):
+                acc += [(x, False) for x in v[1] + v[2]]
+        for (n, a, b), w in acc:
+            for (a2, b2, j, w2) in hist.get(n, []):
+                if a < b2 and a2 < b and (w or w2 or n == "PS"):
+                    o = ops[j]
+                    if tag is not None and o["tag"] == tag:
+                        continue
+                    sem = o["kind"] != "c" or o["q"] != q or (q != "pe" and n != "PS")
+                    deps[j] = deps.get(j, False) or sem
+        for (n, a, b), w in acc:
+            h = hist.setdefault(n, [])
+            if (w and tag is None) or n == "PS":
+                h[:] = [e for e in h if not (a <= e[0] and e[1] <= b)]
+            h.append((a, b, i, w))
+        for j in after:
+            deps.setdefault(j, False)
+        ops.append(dict(q=q, fn=fn, deps=deps, cost=cost, lat=lat, kind=kind, tag=tag, ext=ext))
+        return i
+
+    def vc_(o, ins, base):
+        if o[2]:
+            return FIX + o[3] * SCA * 1e-3
+        if any(isop(v) and v[2] for v in ins):
+            return FIX + o[3] * GA * 1e-3
+        return FIX + max(64, max(v[3] for v in ins + [o] if isop(v)) * base) * 1e-3
+    half = lambda *v: 0.5 if all(x[4] for x in v) else 1.0
+
+    def tc(o, a, **k): return op("dve", lambda e: e.tensor_copy(o[0], a[0]), [o], [a], vc_(o, [a], half(o, a)), **k)
+    def tt(o, a, b, f, **k): return op("dve", lambda e: e.tensor_tensor(o[0], a[0], b[0], f), [o], [a, b], vc_(o, [a, b], 1 if a[5] or b[5] else 2 * half(o, a, b)), **k)
+
+    def ts(o, a, s1, f0, s2=None, f1=None, **k):
+        fn = (lambda e: e.tensor_scalar(o[0], a[0], ap(s1), None, f0)) if f1 is None else (lambda e: e.tensor_scalar(o[0], a[0], ap(s1), ap(s2), f0, f1))
+        return op("dve", fn, [o], [a, s1, s2], vc_(o, [a], half(o, a)), **k)
+    def scan(o, a, b, f0, f1, init=0.0): return op("dve", lambda e: e.tensor_tensor_scan(o[0], a[0], b[0], init, f0, f1), [o], [a, b], vc_(o, [a], half(o, a, b)))
+    def red(o, a, f): return op("dve", lambda e: e.tensor_reduce(o[0], a[0], AxisListType.X, f), [o], [a], vc_(o, [a], 1))
+    def ms(o, c): return op("dve", lambda e: e.memset(o[0], c), [o], [], vc_(o, [], half(o)))
+
+    def act(o, a, bias=0.0, scale=1.0, f=F.Identity, acc=None, **k):
+        fn = ((lambda e: e.activation(o[0], a[0], f, bias=ap(bias), scale=ap(scale))) if acc is None else
+              (lambda e: e.activation(o[0], a[0], f, bias=ap(bias), scale=ap(scale), accum_out=acc[0])))
+        return op("act", fn, [o] + ([acc] if acc else []), [a, bias, scale], vc_(o, [a], 1), **k)
+
+    def mm(lst):
+        def fn(e):
+            for o, l, rr, s0, s1 in lst:
+                i = e.matmul(o[0], l[0], rr[0], s0, s1)
+            return i
+        c = sum(max(min(64, l[3]), rr[3]) * (1 if l[4] else 4) for o, l, rr, s0, s1 in lst) * PEC + FIX
+        return op("pe", fn, [x[0] for x in lst], [x[1] for x in lst] + [x[2] for x in lst], c)
+    grp = lambda o, prs: [(o, l, rr, i == 0, i == len(prs) - 1) for i, (l, rr) in enumerate(prs)]
+
+    def wrap(o, W, n, a, b, odd=False):
+        return mm(grp(o, [(A(W, 15 - x, 143 - x), A(n, a + ((x | 1) if odd else x), b, 16)) for x in range(16)]))
+
+    def iota(o, pat, base, cm):
+        fl = _S[o[1][0][0]][1] != I4
+        fn = (lambda e: e.iota(o[0], pat, base, cm, allow_small_or_imprecise_dtypes=True)) if fl else (lambda e: e.iota(o[0], pat, base, cm))
+        return op("pool", fn, [o], [], 0.25 + o[3] * 2e-3)
+
+    def dma(o, a, q="sync", tag=None, lat=2.5): return op(q, lambda e: e.dma_start(o[0], a[0]), [o], [a], 0.1, lat, "dma", tag)
+
+    def load(n, a, b, src, dr, sr, q):
+        dma(A(n, a, b, p=(0, dr * (8 - r))), X(src[sr * r:sr * 8, :]), q, "ld" + n)
+        if r:
+            dma(A(n, a, b, p=(dr * (8 - r), dr * 8)), X(src[0:sr * r, :]), q, "ld" + n)
+    rowsof = lambda n, row, a, b: (T[n][row:128:16, a:b], [(n, a, b)], [], 0, False, False)
+    PS = lambda bank, a, b, s=1, p=(0, 128): A("PS", 512 * bank + a, 512 * bank + b, s, p)
+    cn = {}
+    def c(n): return A("CF", cn.setdefault(n, len(cn)), cn[n] + 1)
+    mn = {}
+    def M(n): return A("MAT", 128 * mn.setdefault(n, len(mn)), 128 * mn[n] + 128)
+    ci = lambda k: A("CI", k, k + 1)
+    oh = lambda k: A("OH", k, k + 1)
+    dd = lambda k: A("DD", k, k + 1)
+    cut = sorted({0, 64, 128 - 16 * r, 128})
+
+    load("PLi", 0, 256, T.pr, 16, 1, "sync"); load("MTi", 0, 128, T.mt, 16, 1, "act")
+    load("CI", 16, 17, T.kk, 16, 16, "sync"); load("CI", 20, 21, T.w, 16, 16, "act"); load("CI", 24, 25, T.th, 1, 1, "sync")
+    for k in range(len(cut) - 1):
+        a, b = cut[k], cut[k + 1]; ra = (a + 16 * r) % 128
+        dma(A("Q", 0, 4096, p=(a, b)), X(T.rec[ra:ra + b - a, :]), "act" if k % 2 else "sync", "ldQ", 6.0)
+    ms(A("S1", 0, TW), 0.0)
+    iota(ci(0), [[0, 1]], 0, 1); iota(A("IO", 0, 160), [[1, 160]], 0, 0); iota(A("I16c", 0, 256), [[0, 16], [1, 16]], 0, 0)
+    iota(A("IL", 0, 256), [[1, 256]], 0, 0); iota(A("ONE", 0, 256), [[0, 256]], 1, 0)
+    ts(ci(1), ci(0), 15, O.bitwise_and); ts(ci(2), ci(0), 4, O.arith_shift_right); ts(ci(3), ci(0), 1, O.bitwise_and)
+    ts(ci(4), ci(0), 4, O.arith_shift_right, 1, O.bitwise_and); ts(ci(5), ci(0), 3, O.arith_shift_right); ts(ci(6), ci(0), 7, O.bitwise_and)
+    tc(A("CF", 0, 7), A("CI", 0, 7))
+    for n in ("p", "x", "b", "p1", "odd", "r8", "p7"):
+        c(n)
+    ts(A("OH", 0, 16), A("IO", 0, 16), c("x"), O.is_equal)
+    act(A("DD", 0, 15), A("OH", 0, 15), scale=64.0); tt(A("DD", 0, 15), A("DD", 0, 15), A("OH", 1, 16), O.add)
+    act(c("b15"), c("b"), bias=15.0, scale=16.0); act(c("p16"), c("p"), bias=16.0)
+    ts(A("WB", 0, 144), A("IO", 0, 144), c("b15"), O.is_equal); ts(A("IW", 0, 160), A("IO", 0, 160), c("p16"), O.is_equal)
+    act(c("wg"), oh(7), bias=oh(4), scale=512.0); act(c("f47"), oh(7), bias=oh(4))
+    for n, s in (("Wf", oh(4)), ("Wp", dd(0)), ("Wmp", dd(5)), ("Wix", dd(12)), ("Wg", c("wg"))):
+        act(A(n, 0, 144), A("WB", 0, 144), scale=s)
+    sh = lambda k: A("IW", 16 - k, 144 - k)
+    ts(c("hi"), c("x"), 8.0, O.is_ge); act(c("lo"), c("hi"), bias=1.0, scale=-1.0); ts(c("l12"), c("x"), 12.0, O.is_lt)
+    ts(A("MASK", 0, 256), A("I16c", 0, 256), c("x"), O.is_equal); act(A("RS", 0, 256), A("I16c", 0, 256), f=F.Sign)
+    act(A("RK", 0, 256), A("RS", 0, 256), bias=33554432.0, scale=-33554496.0)
+    act(A("MNG", 0, 256), A("MASK", 0, 256), bias=-2.0 ** 30, scale=2.0 ** 30); act(A("CS", 0, 256), A("ONE", 0, 256), scale=oh(4))
+    iota(M("Z"), [[0, 128]], 0, 0); iota(M("t0"), [[1, 8], [0, 16]], 0, 0); ts(M("BD"), M("t0"), c("b"), O.is_equal)
+    ts(M("t1"), A("IO", 0, 128), c("p"), O.is_ge); tt(M("TRI"), M("t1"), M("BD"), O.mult)
+    act(M("t0"), sh(8), scale=c("lo")); act(M("t1"), sh(-8), scale=c("hi")); tt(M("PERM"), M("t0"), M("t1"), O.add)
+    act(M("PERMn"), M("PERM"), scale=-1.0); act(M("N4096"), sh(0), scale=-4096.0); act(M("BDi"), M("BD"), scale=dd(12)); act(M("In"), sh(0), scale=-1.0)
+    act(A("I32", 0, 128), sh(0)); tc(A("I16", 0, 128), sh(0)); tc(A("I16", 128, 256), M("PERM"))
+    act(A("PI2", 0, 128), sh(0), scale=8388608.0); act(A("PI2", 128, 256), sh(0), scale=8388608.0)
+    act(A("HI2", 0, 128), sh(0), scale=-64.0); act(A("HI2", 128, 256), sh(0))
+    act(c("m01"), oh(0), bias=oh(1)); act(c("m56"), oh(5), bias=oh(6)); act(c("mk"), oh(12), bias=oh(13)); act(c("m4"), c("m01"), bias=c("m56"))
+    act(c("keep"), c("m56"), bias=1.0, scale=-1.0); act(c("md"), oh(13), bias=oh(14), scale=1.0 / 64)
+    for n, k, s in (("MI", 0, "m4"), ("Mup", 12, "m01"), ("Mdn", -12, "mk"), ("Mk", 0, "mk"), ("M56", 0, "m56"), ("Md", -11, "md"), ("M7", -7, "mk")):
+        act(M(n), sh(k), scale=c(s))
+    act(M("t0"), sh(0), scale=c("l12")); I12 = M("t0"); Ib = sh(0)
+    GG, GN, GP, GJ, GD, G64 = (A("GM", 16 * k, 16 * k + 16) for k in range(6))
+    ts(A("GM", 0, 8), A("IO", 0, 8), c("b"), O.is_equal); act(A("GM", 8, 16), A("GM", 0, 8))
+    act(GN, GG, scale=-1024.0); act(GP, GG, scale=2048.0); act(GJ, GG, scale=dd(2)); act(GD, GG, scale=-512.0); act(G64, GG, scale=64.0)
+    G1 = A("GM", 0, 8); G64 = A("GM", 80, 88)
+    act(c("pd"), c("p1"), bias=1.0, scale=-2.0); act(c("off"), c("pd"), bias=-0.5, scale=3072.0); act(c("even"), c("odd"), bias=1.0, scale=-1.0)
+    act(c("s1"), c("l12"), scale=-1048576.0); act(c("s4"), oh(13), bias=oh(14)); act(c("s3"), c("s4"), bias=oh(12), scale=256.0)
+    act(c("s2"), oh(15), bias=c("s3"), scale=2097152.0); act(c("nlo"), c("lo"), scale=-512.0); act(c("nhi"), c("hi"), scale=-512.0)
+    iota(A("CO", 208, 224), [[16, 16]], 0, 0); act(A("LW", 0, 16), A("CO", 208, 224), bias=c("x"))
+    DU1, DU2, L257 = A("BA", 0, 16), A("BA", 32, 48), A("CO", 32, 48)
+    act(L257, A("LW", 0, 16), bias=257.0)
+    TL = A("CO", 64, 96); iota(TL, [[128, 2], [0, 16]], -12582912, 1)
+    OB = A("CO", 96, 128)
+    for k, bs in enumerate((D1, 0, D2, D1)):
+        act(A("CO", 96 + 8 * k, 104 + 8 * k), A("LW", 0, 8), bias=float(bs))
+    DB = A("CO", 128, 144); act(A("CO", 128, 136), A("LW", 0, 8), bias=float(D1)); act(A("CO", 136, 144), A("LW", 0, 8), bias=float(D2))
+    for k in range(3):
+        act(A("BA", 16 * k, 16 * k + 16), A("LW", 0, 16), bias=float(D2 if k == 2 else D1))
+    iota(A("CO", 144, 160), [[16, 2], [1, 8]], 0, 0); iota(A("CO", 160, 176), [[1, 2], [0, 8]], 0, 0)
+    EL, EH, E2L = A("UL", 0, 16), A("UL", 16, 32), A("UL", 32, 48)
+    tc(EL, A("IO", 0, 16)); tc(EH, A("CO", 144, 160))
+    ts(c("c1"), c("x"), 13.0, O.is_ge); act(c("c4"), oh(14), scale=32.0); act(c("c2"), oh(15), bias=c("c4"), scale=64.0)
+    act(c("c3"), oh(12), bias=c("c2"), scale=96.0); act(c("c5"), c("l12"), bias=c("c3"), scale=98.0)
+    act(A("CO", 176, 192), A("CO", 144, 160), bias=c("c5"), scale=c("c1")); act(A("CO", 192, 208), A("CO", 160, 176), scale=oh(12))
+    tt(A("CO", 176, 192), A("CO", 176, 192), A("CO", 192, 208), O.add); tc(E2L, A("CO", 176, 192))
+    iota(A("DW", 96, 98), [[128, 2]], 0, 1); iota(A("DW", 98, 104), [[0, 6]], 0, 0)
+    HC = A("TJ", 384, 480); iota(HC, [[64, 3], [0, 32]], -192, 0)
+    for n, a, b, v in (("MN", 0, 32, 8000000), ("LS", 0, 32, 0), ("C3", 128, 136, 0), ("Q", 4096, TW, 0), ("BITS", 4096, TW, 0), ("S2", 4096, TW, 0)):
+        iota(A(n, a, b), [[0, b - a]], v, 0)
+    ms(A("S2", 0, 2048), 0.0); ms(A("VT", 0, 2048), 0.0)
+    for t in range(4):
+        iota(A("SB", 512 * t + 256, 512 * t + 384), [[0, 128]], -1, 0); iota(A("SA", 512 * t + 256, 512 * t + 384), [[0, 128]], 0, 0)
+    p8 = (0, 8)
+    ts(A("CI", 25, 26, p=p8), A("CI", 24, 25, p=p8), 6, O.arith_shift_right); ts(A("CI", 26, 27, p=p8), A("CI", 24, 25, p=p8), 63, O.bitwise_and)
+    tc(A("TM", 384, 386, p=p8), A("CI", 25, 27, p=p8)); iota(A("TM", 256, 384, p=p8), [[1, 8], [0, 16]], 0, -1)
+    ts(A("TM", 256, 384, p=p8), A("TM", 256, 384, p=p8), 0.0, O.is_equal)
+    mm(grp(PS(7, 0, 2), [(A("TM", 256, 384, p=p8), A("TM", 384, 386, p=p8))])); c("th0"); c("th1")
+    act(A("CF", cn["th0"], cn["th1"] + 1), PS(7, 0, 2))
+    act(c("t2"), oh(2), bias=c("f47"), scale=c("th0")); act(c("thb"), oh(3), bias=c("t2"), scale=c("th1"))
+    tb = lambda k: A("TB", 256 * k, 256 * k + 256)
+    act(c("x256"), c("x"), scale=256.0); act(c("x4"), c("x"), scale=4.0); act(A("TF", 0, 256), A("IL", 0, 256), bias=c("x256"))
+    tt(tb(4), A("PLi", 0, 256), A("TF", 0, 256), O.is_equal); dma(rowsof("S1", 4, 0, 4096), tb(4), "sync", "s1")
+    ts(A("TJ", 0, 256), A("PLi", 0, 256), 6, O.arith_shift_right); tc(tb(0), A("TJ", 0, 256))
+    ts(A("TI", 0, 256), A("PLi", 0, 256), 63, O.bitwise_and); tc(tb(1), A("TI", 0, 256))
+    iota(tb(2), [[1, 4], [0, 64]], 0, 0); act(tb(5), tb(2), bias=c("x4")); iota(tb(6), [[0, 4], [1, 64]], 0, 0)
+    act(tb(2), A("ONE", 0, 256), scale=c("th0")); act(tb(3), A("ONE", 0, 256), scale=c("th1"))
+    for k, row in ((0, 0), (1, 1), (5, 12), (6, 13), (2, 2), (3, 3), (4, 7)):
+        dma(rowsof("S1", row, 0, 4096), tb(k), "sync", "s1")
+    ts(A("MTu", 0, 128), A("MTi", 0, 128), -2048.0, O.add)
+    iota(A("TM", 0, 128), [[0, 8], [2, 16]], 0, 0); act(A("TM", 0, 128), A("TM", 0, 128), bias=c("hi"))
+    iota(A("TM", 128, 256), [[1, 8], [0, 16]], 0, 0); act(c("x8"), c("p7"), scale=8.0); act(A("TM", 128, 256), A("TM", 128, 256), bias=c("x8"))
+    dma(rowsof("VT", 5, 0, 2048), A("TM", 0, 128), "sync", "VT"); dma(rowsof("VT", 6, 0, 2048), A("TM", 128, 256), "sync", "VT")
+    ts(A("TJ", 256, 384), A("MTi", 0, 128), 6, O.arith_shift_right); tc(A("TB", 1792, 1920), A("TJ", 256, 384))
+    ts(A("TJ", 256, 384), A("MTi", 0, 128), 63, O.bitwise_and); tc(A("TB", 1920, 2048), A("TJ", 256, 384))
+    dma(rowsof("S2", 5, 0, 2048), A("TB", 1792, 1920), "sync", "S2"); dma(rowsof("S2", 6, 0, 2048), A("TB", 1920, 2048), "sync", "S2")
+    for k in range(8):
+        tc(IX(A("S2", 2048, 4096), A("MTu", 16 * k, 16 * k + 16)), A("VT", 256 * k, 256 * k + 256))
+    kj = lambda a, b: A("KJ", 0, 128, p=(a, b))
+    iota(kj(0, 32), [[1, 2], [0, 64]], 0, 2); iota(kj(32, 64), [[0, 2], [1, 64]], 0, 0); iota(kj(64, 96), [[1, 128]], 0, 128); iota(kj(96, 128), [[1, 128]], 0, 128)
+    tt(kj(64, 128), kj(64, 128), kj(64, 128), O.mult)
+    ts(kj(64, 96), kj(64, 96), 11, O.arith_shift_right, 63, O.bitwise_and); ts(kj(96, 128), kj(96, 128), 5, O.arith_shift_right, 63, O.bitwise_and)
+    tc(A("TU", 0, 128), kj(0, 128)); dma(A("UR", 0, 4096, p=(0, 4)), A("TU", 0, 128), "sync")
+    ts(ci(8), ci(16), 63, O.bitwise_and); ts(A("KC", 0, 1), ci(8), 64.0, O.mult); tc(A("KC", 1, 2), ci(16))
+    ts(A("KC", 2, 3), A("ONE", 0, 1), 64.0, O.mult); tc(A("KC", 3, 4), A("ONE", 0, 1))
+    mm(grp(PS(6, 0, 128, p=(0, 4)), [(A("KC", 0, 4), A("I16", 0, 128))])); tc(A("KL", 0, 128, p=(0, 4)), PS(6, 0, 128, p=(0, 4)))
+    for k in range(8):
+        pr = (A("KL", 0, 128, p=(0, 4)), A("UR", 512 * k, 512 * k + 512, p=(0, 4))); nb = A("NB", 512 * (k % 2), 512 * (k % 2) + 512)
+        mm(grp(PS(k % 2, 0, 512), [pr])); act(nb, PS(k % 2, 0, 512), bias=129.0 - 4095.0 / 8192, scale=1.0 / 4096)
+        mm(grp(PS(2 + k % 2, 0, 512), [pr, (M("N4096"), nb)]))
+        if k % 2:
+            ts(A("CT", 512 * k, 512 * k + 512), PS(2 + k % 2, 0, 512), 528384.0, O.add)
+        else:
+            act(A("CT", 512 * k, 512 * k + 512), PS(2 + k % 2, 0, 512), bias=528384.0)
+    tc(A("KC", 4, 5), ci(20)); ts(c("w2"), ci(20), 0.5, O.mult); ts(A("Ww", 0, 144), A("WB", 0, 144), c("w2"), O.mult)
+    ts(A("KC", 6, 7), ci(20), c("pd"), O.mult); tc(A("TU", 128, 256), M("BD"))
+    mm(grp(PS(7, 8, 9), [(A("I16", 128, 256), A("KC", 4, 5))]) + grp(PS(7, 9, 10), [(A("TU", 128, 256), A("KC", 6, 7))]))
+    act(c("wv"), PS(7, 8, 9)); act(c("cw"), PS(7, 9, 10), scale=-1536.0); ts(A("Wv", 0, 144), A("WB", 0, 144), c("wv"), O.mult)
+
+    def lanes(t):
+        s = (341 * t) % 2048; lst = [(PS(6, 0, 128), M("Z"), Ib, True, False)]
+        for x in range(16):
+            f = s + x; n1 = min(128, (2048 - f + 15) // 16); W = A("Wf", 15 - x, 143 - x)
+            lst.append((PS(6, 0, n1), W, A("S1", f, 2048, 16), False, x == 15 and n1 == 128))
+            if n1 < 128:
+                f2 = f + 16 * n1 - 2048
+                lst.append((PS(6, n1, 128), W, A("S1", f2, f2 + 16 * (128 - n1), 16), False, x == 15))
+            if x % 4 == 3:
+                mm(lst); lst = []
+        act(A("FWb", 0, 128), PS(6, 0, 128))
+        mm(grp(PS(7, 128, 256), [(M("BD"), A("FWb", 0, 128))]) + grp(PS(7, 0, 128), [(M("TRI"), A("FWb", 0, 128))]))
+        scan(A("CE", 0, 128), A("ONE", 0, 128), PS(7, 128, 256), O.mult, O.add)
+        tt(A("SM", 0, 128), A("CE", 0, 128), A("MASK", 0, 128), O.mult); scan(A("SS", 0, 128), A("RS", 0, 128), A("SM", 0, 128), O.mult, O.add)
+        act(A("SW", 112, 116), A("SS", 15, 64, 16), bias=0.5, scale=-1.0)
+        tt(A("SM", 128, 256), A("CE", 0, 128), PS(7, 128, 256), O.subtract); tt(A("C3", 0, 128), A("SM", 128, 256), PS(7, 0, 128), O.add)
+        for j in (4, 0, 5, 1, 6, 2, 7, 3):
+            if j < 4:
+                act(A("IND", 256 * j, 256 * j + 256), A("IL", 0, 256), bias=A("SW", 112 + j, 113 + j), f=F.Sign)
+            else:
+                ts(A("IND", 256 * j, 256 * j + 256), A("IL", 0, 256), A("SS", 16 * j + 15, 16 * j + 16), O.is_ge, 2.0, O.mult)
+            mm([(PS(6, 256, 512), M("BD"), A("IND", 256 * j, 256 * j + 256), j == 4, j == 3)])
+        tt(A("SM", 0, 256), PS(6, 256, 512), A("MASK", 0, 256), O.mult); scan(A("SS", 0, 256), A("RS", 0, 256), A("SM", 0, 256), O.mult, O.add)
+        cw = A("SS", 15, 256, 16); w = lambda k: A("SW", 16 * k, 16 * k + 16)
+        ts(A("cu", 0, 16), cw, 0.5, O.mult, 32.0, O.add); tt(A("XI", 0, 256), IX(A("C3", 0, 136), A("cu", 0, 16)), A("IL", 0, 256), O.is_le)
+        wrap(PS(7, 256, 272), "WB", "XI", 0, 256)
+        act(w(0), cw, bias=512.0 + s, scale=8.0); act(w(1), cw, bias=-191.0, f=F.Relu); act(A("dR", 0, 256), PS(6, 256, 512), bias=-191.0, f=F.Relu)
+        tt(w(2), w(1), DU1, O.mult)
+        tt(w(3), w(0), PS(7, 256, 272), O.add); ts(w(4), w(3), 2048.0, O.is_ge, -2048.0, O.mult); tt(w(3), w(3), w(4), O.add)
+        tt(w(5), w(3), w(2), O.max); tc(A("aW", 0, 16), w(5)); tt(A("DF", 16, 32), w(5), DU1, O.subtract)
+
+    lanes(0); act(A("no", 0, 256), IX(A("S1", 0, TW), A("aW", 0, 16)))
+    wrap(PS(4, 0, 256), "Wp", "S1", 0, 4096); tc(A("PWu", 0, 256), PS(4, 0, 256))
+    for k in range(8):
+        act(A("MPT", 512 * k, 512 * k + 512), IX(A("S2", 0, 4096), A("PWu", 32 * k, 32 * k + 32)))
+    dma(rowsof("S1", 5, 0, 4096), rowsof("MPT", 5, 0, 4096), "sync", "mp"); dma(rowsof("S1", 6, 0, 4096), rowsof("MPT", 6, 0, 4096), "sync", "mp")
+    ts(c("r12"), c("r8"), 12.0, O.is_lt); act(c("r12b"), c("r12"), scale=-0.5 + 2.0 ** -13)
+    act(A("CO", 224, 240), A("ONE", 0, 16), scale=0.5)
+    scan(A("CO", 0, 16), A("CO", 224, 240), A("MAT", 128 * mn["Z"], 128 * mn["Z"] + 16), O.mult, O.add, 1.0); ts(A("CO", 16, 32), A("IO", 0, 16), c("r8"), O.is_equal)
+    tt(A("CO", 48, 64), A("CO", 0, 16), A("CO", 16, 32), O.mult); red(c("pw"), A("CO", 48, 64), O.add)
+    act(c("p512"), c("p7"), scale=512.0); act(c("pb"), c("p512"), scale=c("pw"))
+    iota(A("TG", 0, 512), [[1, 512]], 0, 0); act(A("TF", 0, 512), A("TG", 0, 512), bias=c("pb"), scale=c("pw"))
+    act(A("TG", 0, 512), A("TF", 0, 512), bias=-0.5 + 2.0 ** -13); act(A("TG", 0, 512), A("TG", 0, 512), bias=12582912.0)
+    act(A("TG", 0, 512), A("TG", 0, 512), bias=-12582912.0); tt(A("TF", 0, 512), A("TF", 0, 512), A("TG", 0, 512), O.subtract)
+    act(A("BT", 0, 512), A("TF", 0, 512), bias=c("r12b"), scale=c("r12"), f=F.Sign)
+    for k in range(8):
+        dma(A("BITS", 0, 4096, p=(16 * k, 16 * k + 16)), A("BT", 0, 512), "sync", "bits")
+    dma(rowsof("BITS", 12, 0, 4096), tb(5), "sync", "bi2"); dma(rowsof("BITS", 13, 0, 4096), tb(6), "sync", "bi2")
+    ts(ci(9), ci(2), float(r), O.add); ts(ci(9), ci(9), 7, O.bitwise_and); ts(c("g8"), ci(9), 8.0, O.mult)
+    iota(A("JK", 0, 512), [[-1, 8], [1, 64]], 0, 0); ts(A("JK", 0, 512), A("JK", 0, 512), c("g8"), O.is_equal)
+    act(A("LP", 0, 512), A("JK", 0, 512), scale=dd(0)); act(A("LM", 0, 512), A("JK", 0, 512), scale=dd(5))
+
+    Qw, S1w, S2w, Bw, CTw = A("Q", 0, TW), A("S1", 0, TW), A("S2", 0, TW), A("BITS", 0, TW), A("CT", 0, 4096)
+    plan = routes(T, topo, r)
+    narr = sum(bin(m if h is None else topo.mask(h, cc)).count("1") for s in range(8) for d, cc, h, m in routes(T, topo, s) if cc == core)
+    nsnt = sum(bin(m).count("1") for d, cc, h, m in plan)
+    big = []
+    for t in range(4):
+        aW = A("aW", 0, 16); L = lambda n, h: A(n, 128 * h, 128 * h + 128); W8 = lambda n, h: A(n, 8 * h, 8 * h + 8)
+        for h in range(2):
+            tc(L("y", h), IX(Qw, W8("aW", h)))
+        act(A("va", 0, 256), IX(Qw, aW))
+        for h in range(2):
+            mm([(PS(2 * h + k, q, 512, 8), M("PERM"), A("va", 128 * h + 64 * k, 128 * h + 64 * k + 64), True, True) for k in range(2) for q in range(8)])
+            act(L("AO", h), PS(2 * h, 0, 1024, 8), bias=c("off")); act(L("AB", h), PS(2 * h, 0, 1024, 8))
+        act(A("BB", 256, 512), IX(Bw, aW)); act(A("S1a", 0, 256), IX(S1w, aW))
+        mm(grp(PS(6, 0, 256), [(M("BDi"), A("BB", 256, 512) if t else A("no", 0, 256))])); act(A("aR", 0, 256), PS(6, 0, 256))
+        mm(grp(PS(7, 0, 16), [(L("va", 0), GG), (L("dR", 0), GD)]) + grp(PS(7, 16, 32), [(L("va", 1), GG), (L("dR", 1), GD)])); act(A("SAT", 0, 32), PS(7, 0, 32))
+        act(A("BL", 256, 512), IX(Bw, aW), bias=c("s2"), scale=c("s1"))
+        for hop in range(4):
+            for h in range(2):
+                Xn, Mn = "X%d" % h, "M%d" % h; uo = W8("uo", h); kb = 4 + h; K = PS(kb, 0, 256)
+                wrap(PS(kb, 256, 264), "Ww" if hop else "Wv", "y", 128 * h, 128 * h + 128)
+                u0, u1 = A("ui", 16 * h, 16 * h + 8), A("ui", 16 * h + 8, 16 * h + 16)
+                ts(u0, PS(kb, 256, 264), c("cw") if hop else 0.0, O.add); ts(u1, u0, 4095, O.bitwise_and); tc(uo, u1)
+                tc(L("co", h), IX(CTw, uo))
+                for a, b in SUB:
+                    big = [act(A(Xn, 16 * a, 16 * b), IX(Qw, A("co", 128 * h + a, 128 * h + b)), after=big)]
+                tt(L("eq", h), IX(CTw, uo), L("aR", h), O.is_equal)
+                act(L("cF", h), IX(CTw, uo), bias=8385.0); act(L("hB", h), IX(CTw, uo), bias=129.0 - 31.5 / 64, scale=1.0 / 64)
+                mm([(K, L("eq", h), A("PI2", 0, 256), True, False), (PS(kb, 0, 128), L("cF", h), A("I32", 0, 128), False, False),
+                    (K, L("hB", h), A("HI2", 0, 256), False, False)])
+                for a, b in SUB:
+                    for q in range(2):
+                        tt(A(Mn, 16 * a + q, 16 * b, 2, reg=Mn + str(q)), A(Xn, 16 * a + q, 16 * b, 2), PS(2 * h, 8 * a, 8 * b), O.max)
+                mm([(PS(kb, i, 256, 16), A(Xn, i, 2048, 16), GN, False, False) for i in range(16)])
+                for q in range(2):
+                    mm([(PS(kb, i, 256, 16), A(Mn, i, 2048, 16, reg=Mn + str(q)), GP, False, i == 15) for i in range(q, 16, 2)])
+                sc = A("SC", 256 * h, 256 * h + 256); scan(sc, A("RK", 0, 256), K, O.add, O.min)
+                ki = A("KI", 32 * hop + 16 * h, 32 * hop + 16 * h + 16)
+                ts(ki, A("SC", 256 * h + 15, 256 * h + 256, 16), 831.0, O.add)
+                if hop < 3:
+                    lo = A("lo", 16 * h, 16 * h + 16); e = A("E", 256 * h, 256 * h + 256)
+                    ts(lo, ki, 63, O.bitwise_and); tt(e, IX(lo, EL), A("MASK", 0, 256), O.mult)
+                    mm(grp(PS(kb, 264, 272), [(A("E", 256 * h, 256 * h + 128), G1), (A("E", 256 * h + 128, 256 * h + 256), G64)]))
+                    tc(W8("cw", h), PS(kb, 264, 272)); tc(L("mg", h), IX(S1w, W8("cw", h)))
+                    wrap(PS(kb, 272, 280), "Wmp", "mg", 128 * h, 128 * h + 128); tc(W8("mo", h), PS(kb, 272, 280))
+                    tt(L("y", h), IX(Qw, W8("mo", h)), L("AO", h), O.add)
+        ts(A("KJ", 0, 96), A("KI", 0, 96), 0xFFFC3F, O.bitwise_and); tt(A("KJ", 0, 96), A("KJ", 0, 96), HC, O.add)
+        tt(A("KI", 0, 32), A("KJ", 0, 32), A("KJ", 32, 64), O.min); tt(A("KI", 32, 64), A("KI", 0, 32), A("KJ", 64, 96), O.min)
+        ts(A("KJ", 96, 128), A("KI", 96, 128), 0xFFFC3F, O.bitwise_and); tt(A("KI", 64, 96), A("KI", 32, 64), A("KJ", 96, 128), O.min)
+        ts(A("lo", 0, 32), A("KI", 64, 96), 63, O.bitwise_and); cw = A("cw", 0, 16)
+        for h in range(2):
+            tt(A("E", 256 * h, 256 * h + 256), IX(A("lo", 16 * h, 16 * h + 16), EL), A("MASK", 0, 256), O.mult)
+        mm(sum((grp(PS(4, 8 * h, 8 * h + 8), [(A("E", 256 * h, 256 * h + 128), G1), (A("E", 256 * h + 128, 256 * h + 256), G64)]) for h in range(2)), []))
+        tc(cw, PS(4, 0, 16)); tt(A("DF", 32, 48), PS(4, 0, 16), DU2, O.subtract)
+        Dd = A("Di", 32, 64); npr = A("DW", 64, 96)
+        ts(A("KI", 0, 32), A("KI", 64, 96), 192.0, O.add); ts(A("Di", 0, 32), A("KI", 0, 32), 10, O.arith_shift_right); tt(Dd, A("Di", 0, 32), A("SAT", 0, 32), O.subtract)
+        ts(A("DW", 0, 32), Dd, 0x7FC0, O.bitwise_and); ts(A("DW", 32, 64), Dd, 63, O.bitwise_and)
+        ts(A("TH", 0, 32), Dd, 256.0, O.mult); tt(A("TH", 0, 32), A("TH", 0, 32), TL, O.add)
+        tc(A("S1c", 0, 256), IX(S1w, cw)); act(A("BB", 0, 256), IX(Bw, cw)); act(A("BL", 0, 256), IX(Bw, cw), bias=c("s2"), scale=c("s1"))
+        mm(grp(PS(5, 0, 16), [(L("S1c", 0), GJ)]) + grp(PS(5, 16, 32), [(L("S1c", 1), GJ)])); tt(npr, Dd, PS(5, 0, 32), O.is_ge)
+        tc(A("E2", 0, 256), IX(A("DW", 0, 104), E2L))
+        ts(A("st", 0, 32), npr, 16777216.0, O.mult); tt(A("TH", 0, 32), A("TH", 0, 32), A("st", 0, 32), O.add)
+        wrap(PS(3, 32, 48), "Wp", "S1c", 0, 256); tt(A("DF", 0, 16), PS(3, 32, 48), DU1, O.subtract)
+        for k in range(2):
+            mm([(PS(6 + k, 0, 256), I12, A("BB", 256 * k, 256 * k + 256), True, False)] + [(PS(6 + k, 128 * h, 128 * h + 128), L("E2", h), Ib, False, h == 1) for h in range(2)])
+        ts(A("RE", 0, 256), PS(6, 0, 256), c("even"), O.mult); act(A("RO", 256, 512), PS(7, 0, 256), scale=c("odd"))
+        ts(A("RE", 256, 512), PS(7, 0, 256), c("even"), O.mult); act(A("RO", 0, 256), PS(6, 0, 256), scale=c("odd"))
+        act(A("vc", 0, 256), IX(Qw, cw)); act(A("S2c", 0, 256), IX(S2w, cw))
+        u = 0
+        for h in range(2):
+            for a in range(4):
+                for par in range(2):
+                    bk = 2 * (u % 4); jk = 768 * (u // 2 % 2); u += 1; R = "RO" if par else "RE"; pp = (32 * a, 32 * a + 32); k = 16 * h + 2 * a + par
+                    mm(grp(PS(bk, 0, 512), [(A("BL", 128 * h, 128 * h + 128, p=pp), A(R, 0, 512, p=pp))])
+                       + grp(PS(bk + 1, 0, 256), [(A("BL", 256 + 128 * h, 384 + 128 * h, p=pp), A(R, 0, 256, p=pp))]))
+                    if (u * NACT) // 16 != ((u - 1) * NACT) // 16:
+                        act(A("JK", jk, jk + 768), PS(bk, 0, 768), bias=A("TH", k, k + 1), scale=-1.0, f=F.Relu, acc=A("LS", k, k + 1))
+                    else:
+                        red(A("MN", k, k + 1), PS(bk, 0, 768), O.min)
+        mm(grp(PS(0, 0, 256), [(M("MI"), A("S1c", 0, 256)), (M("Mup"), A("S1c", 0, 256))]))
+        mm(grp(PS(0, 256, 512), [(M("Mdn"), A("S1c", 0, 256)), (M("Mk"), A("S1a", 0, 256)), (M("M56"), A("S2c", 0, 256)), (M("Md"), A("RE", 0, 256)), (M("Md"), A("RO", 0, 256))]))
+        mm(grp(PS(1, 0, 256), [(M("Mdn"), A("S1a", 0, 256)), (M("M56"), A("S1a", 0, 256)), (M("Mk"), A("S1c", 0, 256)), (M("Md"), A("RE", 0, 256)), (M("Md"), A("RO", 0, 256))]))
+        act(A("VAL", 0, 256), PS(0, 0, 256), bias=c("thb")); act(A("VAL", 256, 768), PS(0, 256, 768))
+        tt(A("st", 0, 32), A("TH", 0, 32), A("MN", 0, 32), O.subtract); tt(A("st", 32, 64), A("st", 0, 32), A("LS", 0, 32), O.max)
+        tt(A("E", 0, 256), IX(A("st", 32, 64), EH), A("MNG", 0, 256), O.is_le)
+        mm([(PS(4, 16 * k + 8 * h, 16 * k + 8 * h + 8), L("E", h), G1, True, True) for k in range(3) for h in range(2)])
+        tt(A("OT", 0, 48), PS(4, 0, 48), A("DF", 0, 48), O.mult); tt(A("OT", 64, 112), A("OT", 0, 48), A("BA", 0, 48), O.add); tc(A("OF", 0, 48), A("OT", 64, 112))
+        tc(IX(S1w, A("OF", 0, 16)), A("VAL", 0, 256)); tc(IX(S1w, A("OF", 16, 48)), A("VAL", 256, 768))
+        tc(A("no", 0, 256), IX(S1w, aW)); scan(A("no", 256, 512), A("CS", 0, 256), A("no", 0, 256), O.mult, O.add)
+        wrap(PS(5, 0, 16), "Wg", "no", 256, 512)
+        tt(A("OT", 0, 16), PS(5, 0, 16), L257, O.max); ts(A("po", 0, 16), A("OT", 0, 16), -257.0, O.add)
+        b0 = 512 * t
+        tc(IX(A("SB", b0, b0 + 512), A("po", 0, 16)), A("va", 0, 256))
+
+        def send(e, t=t, b0=b0):
+            trs = []
+            for d, cc, h, m in plan:
+                rid, pid = topo.addr(cc if h is None else h, core); k = 112 * t + 16 * (d - 1)
+                trs.append(RemoteDMATransfer(dst_ids=[DstId(rid=rid, pnc=pid)], dma_engine_mask=m, remote_sem=T.sem[("arr%d" if h is None else "hin%d") % t],
+                                             src=T.SB[:, b0 + 240 + 16 * d:b0 + 256 + 16 * d], dst=T.RB[:, k:k + 16] if h is None else T.HB[:, 16 * t:16 * t + 16]))
+            e.remote_dma_fused(trs, local_sem=T.sem.snt)
+        snd = op("pool", send, [], [A("SB", b0 + 256, b0 + 368)], 0.5, WAY, "rem")
+        tc(IX(A("SA", b0, b0 + 512), A("po", 0, 16)), A("no", 0, 256)); ms(A("SA", b0 + 368, b0 + 384), 0.0)
+        mm(grp(PS(1, 256, 512), [(Ib, A("AB", 0, 256)), (M("In"), A("vc", 0, 256))])); act(A("dn", 0, 256), PS(1, 256, 512), f=F.Sign)
+        mm(grp(PS(0, 0, 256), [(Ib, A("va", 0, 256)), (M("PERMn"), A("dn", 0, 256))]) + grp(PS(0, 256, 512), [(Ib, A("vc", 0, 256)), (Ib, A("dn", 0, 256))]))
+        act(A("QV", 0, 512), PS(0, 0, 512))
+        tc(IX(Qw, A("OF", 16, 32)), A("QV", 0, 256), after=[snd - 1]); tc(IX(Qw, A("OF", 32, 48)), A("QV", 256, 512), after=[snd - 1])
+        if t < 3:
+            lanes(t + 1)
+        else:
+            mm(grp(PS(0, 0, 512, p=(0, 64)), [(A("LP", 64 * k, 64 * k + 64), A("S1", 512 * k, 512 * k + 512)) for k in range(8)]))
+            act(A("YO", 0, 512, p=(0, 64)), PS(0, 0, 512, p=(0, 64))); dma(X(T.yp[:]), A("YO", 0, 512, p=(0, 64)), "act")
+        s0 = b0 + 256
+        for k, (W, od) in enumerate((("Wix", False), ("Wmp", False), ("Wf", False), ("Wf", True))):
+            wrap(PS(3, 8 * k, 8 * k + 8), W, "SA", s0, s0 + 128, od)
+        p6 = lambda a, b: A("P6", a, b)
+        tt(p6(0, 16), PS(3, 0, 16), DB, O.subtract); tc(p6(16, 24), PS(3, 24, 32)); tt(p6(32, 40), p6(0, 8), PS(3, 16, 24), O.mult)
+        act(p6(40, 48), p6(16, 24), scale=c("pd")); tt(p6(48, 56), p6(8, 16), p6(16, 24), O.mult); tt(p6(56, 64), p6(0, 8), p6(16, 24), O.mult)
+        tt(p6(64, 96), p6(32, 64), OB, O.add); tc(A("O2", 0, 32), p6(64, 96))
+        mm([(PS(2, 128 * k + e, 128 * k + 128, 2), M("M56" if k == 1 else "M7"), A("SA", s0 + 1 - e, s0 + 128, 2), True, True) for k in range(3) for e in range(2)])
+        act(A("V2", 0, 384), PS(2, 0, 384)); tc(IX(S2w, A("O2", 16, 32)), A("V2", 0, 256))
+        g6 = lambda k, a=0, s=1: A("G6", 128 * k + a, 128 * k + 128, s)
+        if t < 3:
+            act(g6(0), IX(S1w, A("O2", 16, 24))); wrap(PS(3, 32, 40), "Wp", "G6", 0, 128)
+            tt(p6(24, 32), PS(3, 32, 40), A("CO", 136, 144), O.subtract); tt(p6(24, 32), p6(24, 32), p6(16, 24), O.mult)
+            tt(p6(24, 32), p6(24, 32), A("CO", 136, 144), O.add); tc(A("O2", 32, 40), p6(24, 32))
+            act(A("G6", 128, 384), IX(S1w, A("O2", 24, 40)), scale=c("keep")); tt(IX(S1w, A("O2", 24, 40)), A("G6", 128, 384), A("V2", 128, 384), O.add)
+            act(g6(3), IX(Qw, A("O2", 16, 24))); act(g6(4), g6(3), scale=c("lo"))
+            act(g6(5, 0, 2), g6(3, 1, 2), scale=c("hi")); act(g6(5, 1, 2), g6(3, 0, 2), scale=c("hi"))
+            tt(IX(Qw, A("O2", 16, 24)), g6(4), g6(5), O.add)
+        else:
+            mm(grp(PS(1, 0, 256, p=(0, 64)), [(A("LM", 64 * k, 64 * k + 64), A("S2", 256 * k, 256 * k + 256)) for k in range(8)]))
+            act(A("YO", 512, 768, p=(0, 64)), PS(1, 0, 256, p=(0, 64))); dma(X(T.ym[:]), A("YO", 512, 768, p=(0, 64)), "act")
+        r6 = lambda k: A("R6", 128 * k, 128 * k + 112); pm = A("O2", 8, 15); rb = A("RB", 112 * t, 112 * t + 112)
+        act(r6(0), IX(A("SB", s0, s0 + 128), pm), bias=1.0, scale=c("hi")); act(r6(1), A("SB", s0, s0 + 112), scale=c("lo")); tt(r6(0), r6(0), r6(1), O.add)
+        ex = ("arr%d" % t, narr)
+        ts(r6(2), IX(rb, pm), c("hi"), O.mult, c("nlo"), O.add, ext=ex, after=[snd]); act(r6(3), rb, bias=c("nhi"), scale=c("lo"), ext=ex, after=[snd])
+        tt(r6(4), r6(2), r6(3), O.max); ts(r6(5), r6(4), 0.0, O.is_lt); tt(r6(5), r6(5), r6(0), O.mult)
+        tt(IX(Qw, A("O2", 0, 7)), r6(4), r6(5), O.add)
+    for k in range(len(cut) - 1):
+        a, b = cut[k], cut[k + 1]; ra = (a + 16 * r) % 128
+        dma(X(T.yq[ra:ra + b - a, :]), A("Q", 0, 2048, p=(a, b)), "act" if k % 2 else "sync", None, 3.5)
+    emit(g, T, ops, 4 * nsnt, r)
+
+
+def emit(g, T, ops, nsnt, r):
+    n = len(ops); use = [[] for _ in ops]
+    gap = lambda i, j: (GAP if ops[i]["deps"][j] else 0.0) + ops[j]["lat"]
+    for i, o in enumerate(ops):
+        for j in o["deps"]:
+            use[j].append(i)
+    pri = [0.0] * n
+    for i in range(n - 1, -1, -1):
+        pri[i] = ops[i]["cost"] + max([ops[i]["lat"]] + [gap(k, i) + pri[k] for k in use[i]])
+    qs = ("pe", "dve", "act", "pool", "sync")
+    pre = [[(j, gap(i, j)) for j in o["deps"]] for i, o in enumerate(ops)]; post = [[(k, gap(k, i)) for k in use[i]] for i in range(n)]
+
+    def place(pre, post, pri, head):
+        left = [len(x) for x in pre]; rdy = list(head); fin = [0.0] * n
+        cand = {q: [] for q in qs}; free = {q: 0.0 for q in qs}; order = []
+        for i in range(n):
+            if not left[i]:
+                cand[ops[i]["q"]].append(i)
+        while len(order) < n:
+            st, q = min((max(free[q], min(rdy[i] for i in cand[q])), q) for q in qs if cand[q])
+            i = max((i for i in cand[q] if rdy[i] <= st + LOOK), key=lambda i: pri[i])
+            cand[q].remove(i); fin[i] = max(st, rdy[i]) + ops[i]["cost"]; free[q] = fin[i]; order.append(i)
+            for k, w in post[i]:
+                rdy[k] = max(rdy[k], fin[i] + w); left[k] -= 1
+                if not left[k]:
+                    cand[ops[k]["q"]].append(k)
+        return max(fin[i] + ops[i]["lat"] for i in range(n)), order, fin
+    best = None; rng = np.random.default_rng(r)
+    for it in range(ITER):
+        f = place(pre, post, pri, [0.0] * n)
+        if best is None or f[0] < best[0]:
+            best = f
+        pri = place(post, pre, (f if it % 4 < 3 else best)[2], [o["lat"] for o in ops])[2]
+        if it % 4 == 3:
+            pri = [p + NOISE * float(z) for p, z in zip(pri, rng.random(n))]
+    order, fin = best[1], best[2]
+    INFO[r] = (best[0], {q: sum(o["cost"] for o in ops if o["q"] == q) for q in qs}, n,
+               [(ops[i]["q"], i, fin[i] - ops[i]["cost"], fin[i]) for i in order])
+    eng = dict(pe=g.tensor, dve=g.vector, act=g.scalar, pool=g, sync=g.sync)
+    sig = {}; cnt = {q: 0 for q in qs}; seen = {q: {} for q in qs}; nd = 0; last = {}
+    for i in order:
+        o = ops[i]; q = o["q"]; e = eng[q]; need = {}
+        for j, sm in o["deps"].items():
+            if sm and ops[j]["kind"] != "rem":
+                need[sig[j][0]] = max(need.get(sig[j][0], 0), sig[j][1])
+        if o["ext"]:
+            need[o["ext"][0]] = o["ext"][1]
+        if q == "pool" and cnt[q]:
+            need[q] = cnt[q]
+        for s, v in need.items():
+            if seen[q].get(s, 0) < v:
+                e.wait_ge(T.sem[s], v); seen[q][s] = v
+        ins = o["fn"](e)
+        if o["kind"] == "dma":
+            sig[i] = ("d%d" % nd, 16); nd += 1; ins.then_inc(T.sem[sig[i][0]], 16); last[sig[i][0]] = 16
+        elif o["kind"] == "c" and (q == "pool" or any(ops[k]["deps"][i] for k in use[i])):
+            cnt[q] += 1; sig[i] = (q, cnt[q]); ins.then_inc(T.sem[q], 1); last[q] = cnt[q]
+    for s, v in last.items():
+        if max(seen[q].get(s, 0) for q in qs) < v:
+            g.sync.wait_ge(T.sem[s], v)
+    g.wait_ge(T.sem.snt, nsnt)

@@ -2,30 +2,38 @@ import numpy as np
 from concourse.bass import DstId, RemoteDMATransfer
 from concourse.mybir import AluOpType as O, AxisListType, ActivationFunctionType as F
 
-TW, D1, D2 = 4608, 4096, 4352
+TW, D1, D2, DUM = 4624, 4096, 4352, 4608
+KW, KN = 19, 304
 B, H16, F4, I4, U2 = "bfloat16", "float16", "float32", "int32", "uint16"
 _S = dict(
     Q=(TW, B), S1=(TW, B), S2=(TW, B), BITS=(TW, B), CT=(4096, F4), MPT=(4096, B), VT=(2048, B), UR=(4096, H16),
-    X0=(2048, B), X1=(2048, B), M0=(2048, B), M1=(2048, B), IND=(2048, B), SB=(2048, B), SA=(2048, B), RB=(448, B), HB=(64, B),
-    CF=(64, F4), CI=(32, I4), OH=(16, F4), DD=(16, F4), IO=(160, F4), IW=(160, B), WB=(144, B), Wp=(144, B), Wmp=(144, B), Wix=(144, B),
-    Wf=(144, B), Wg=(144, B), Ww=(144, H16), Wv=(144, H16), MAT=(2304, B), I32=(128, F4), I16=(256, H16), PI2=(256, B), HI2=(256, B), GM=(128, B),
-    I16c=(256, B), MASK=(256, B), MNG=(256, B), CS=(256, B), RK=(256, F4), RS=(256, B), IL=(256, B), ONE=(256, B), LW=(16, F4), KC=(16, H16), KL=(128, H16),
+    X0=(2048, B), X1=(2048, B), M0=(2048, B), M1=(2048, B), IND=(256, B), SB=(2048, B), SA=(2048, B), RB=(448, B), HB=(64, B),
+    CF=(80, F4), CI=(32, I4), OH=(16, F4), DD=(16, F4), IO=(160, F4), IW=(160, B), WW=(144 * 12, B), WH=(144 * 3, H16),
+    MAT=(2688, B), I32=(152, F4), I16=(256, H16), PI2=(KN, B), HI2=(KN, B), GM=(128, B), KIX=(2 * KN, B),
+    I16c=(256, B), MASK=(256, B), MNG=(128, B), CS=(256, B), RK=(KN, F4), IL=(256, B), ONE=(256, B), LW=(16, F4), KC=(16, H16), KL=(128, H16),
     CO=(256, F4), UL=(64, U2), TI=(256, I4), TJ=(512, I4), TF=(512, F4), TG=(512, F4), TB=(2048, B), TM=(512, B), TU=(256, H16), BT=(512, B),
     PLi=(256, I4), MTi=(128, I4), MTu=(128, U2), PWu=(256, U2), NB=(1024, B), LP=(512, B), LM=(512, B), YO=(768, F4),
-    FWb=(128, B), CE=(128, F4), C3=(136, F4), SM=(256, F4), SS=(256, F4), SW=(128, F4), cu=(16, U2), aW=(16, U2), dR=(256, B), XI=(256, B),
-    va=(256, B), y=(256, H16), AO=(256, F4), AB=(256, B), aR=(256, F4), SAT=(32, F4), S1a=(256, B), S1c=(256, B), S2c=(256, B), vc=(256, B),
-    BB=(512, B), BL=(512, B), ui=(32, I4), uo=(16, U2), co=(256, U2), cF=(256, F4), hB=(256, B), eq=(256, B), SC=(512, F4), KI=(128, I4),
-    KJ=(128, I4), lo=(32, I4), E=(512, B), cw=(16, U2), mg=(256, B), mo=(16, U2), DW=(104, I4), Di=(64, I4), TH=(32, F4), MN=(32, F4), LS=(32, F4),
-    st=(64, F4), E2=(256, B), RE=(512, B), RO=(512, B), JK=(1536, B), BA=(48, F4), DF=(48, F4), OT=(128, F4), OF=(48, U2),
-    no=(512, B), po=(16, U2), VAL=(768, B), QV=(512, B), dn=(256, B), P6=(96, F4), O2=(40, U2), V2=(384, B), G6=(768, B), R6=(768, B))
+    FWb=(128, B), CE=(144, H16), C3=(136, F4), SS=(16, F4), SW=(128, F4), cu=(32, U2), aW=(16, U2), XI=(768, B),
+    va=(512, B), y=(256, H16), AO=(256, F4), AB=(256, B), AT=(1024, B), aR=(256, F4), SAT=(32, F4), S1a=(256, B), S1c=(256, B), S2c=(256, B), vc=(256, B),
+    BB=(512, B), BL=(1024, B), ui=(32, I4), uo=(16, U2), co=(256, U2), cF=(256, F4), hB=(256, B), eq=(256, B), SC=(8 * KN, F4), KI=(128, I4),
+    KJ=(128, I4), lo=(32, I4), lof=(32, F4), E=(512, B), cw=(16, U2), mg=(256, B), mo=(16, U2), DW=(104, I4), Di=(64, I4), TH=(96, F4), ML=(64, F4),
+    st=(64, F4), E2=(256, H16), R=(512, B), Z=(256, B), JK=(768, B), BA=(48, F4), DX=(96, F4), OT=(128, F4), OF=(48, U2),
+    no=(512, B), po=(16, U2), VAL=(768, B), QV=(512, B), dn=(256, B), P6=(96, F4), O2=(40, U2), V2=(384, B), G6=(768, B), R6=(512, B))
+_S.update(S2=(4096, B), SA=(2048, F4), SP=(336, B), S1f=(256, F4), LB=(16, B), MAT=(128 * 24, B), CF=(96, F4)); del _S["S2c"]
 SCRATCH = {k: ("sbuf", [128, n], d) for k, (n, d) in _S.items()}
-SCRATCH["PS"] = ("psum", [128, 4096], F4)
+SCRATCH["PS"] = ("psum", [128, 2048], F4)
+SCRATCH["PB"] = ("psum", [128, 2048, 2], B)
+PSUM = {"PS": 512, "PB": 1024}
 NDMA = 60
 SEMAPHORES = ["pe", "dve", "act", "pool", "snt"] + ["arr%d" % t for t in range(4)] + ["hin%d" % t for t in range(4)] + ["d%d" % i for i in range(NDMA)]
-INFO = {}
-GA, SCA, FIX, GAP, PEC, WAY = 1.56, 3.8, 0.06, 0.15, 0.5e-3, 7.0
-LOOK, ITER, NOISE, NACT = 0.1, 24, 1.0, 8
-SUB = ((0, 32), (32, 64), (64, 96), (96, 128))
+INFO = {}; PLAN = {}
+SWAPS, DRIFT, NEAR, TEMP, APART, GREED, TABU = 4500, 50.0, 0.02, 0.15, 3.0, 5.0, 4
+GA, SCA, CYC, FIX, GAP, PEC, WAY = 1.3, 3.15, 0.83, 0.05, 0.1, 0.48e-3, 6.0
+LOOK, ITER, NOISE, ND, MGA, TTH, PCS = 0.05, 8, 1.0, ((0, 5), (0, 7)), 1, 0.75, 4
+SUBS = {None: ((0, 16, 1), (16, 56, 0), (56, 96, 0), (96, 128, 0)), (0, 0): ((0, 32, 1), (32, 56, 1), (56, 96, 0), (96, 128, 0)),
+        (3, 1): ((0, 32, 0), (32, 64, 0), (64, 96, 0), (96, 128, 0))}
+SUM = (("X", 0, 128), ("M", 0, 128))
+MIX, SAS, MPV, TRANS, NOA, SCA1, CTV, QAF = 1, 1, 3, 1, 0, 1, 2, 1
 
 
 def routes(T, topo, r):
@@ -71,9 +79,13 @@ def rank_program(g, core, T, topo):
     ops = []; hist = {}
 
     def A(n, a, b, s=1, p=(0, 128), reg=None):
-        ap = T[n][p[0]:p[1], a:b:s] if s > 1 else T[n][p[0]:p[1], a:b]
-        if n == "PS":
-            return (ap, [(n, a // 512 * 512, (b + 511) // 512 * 512)], [], len(range(a, b, s)), False, True)
+        if n == "PB":
+            ap = T[n][p[0]:p[1], a // 2:b // 2:s // 2, :] if s > 1 else T[n][p[0]:p[1], a // 2:b // 2, :]
+        else:
+            ap = T[n][p[0]:p[1], a:b:s] if s > 1 else T[n][p[0]:p[1], a:b]
+        if n in PSUM:
+            w = PSUM[n]
+            return (ap, [(n, a // w * w, (b + w - 1) // w * w)], [], len(range(a, b, s)), n == "PB", True)
         return (ap, [(reg or n, a, b)], [], len(range(a, b, s)), _S[n][1] in (B, H16, U2), False)
 
     def IX(w, o):
@@ -94,15 +106,15 @@ def rank_program(g, core, T, topo):
                 acc += [(x, False) for x in v[1] + v[2]]
         for (n, a, b), w in acc:
             for (a2, b2, j, w2) in hist.get(n, []):
-                if a < b2 and a2 < b and (w or w2 or n == "PS"):
+                if a < b2 and a2 < b and (w or w2 or n in PSUM):
                     o = ops[j]
                     if tag is not None and o["tag"] == tag:
                         continue
-                    sem = o["kind"] != "c" or o["q"] != q or (q != "pe" and n != "PS")
+                    sem = o["kind"] != "c" or o["q"] != q or (q != "pe" and n not in PSUM)
                     deps[j] = deps.get(j, False) or sem
         for (n, a, b), w in acc:
             h = hist.setdefault(n, [])
-            if (w and tag is None) or n == "PS":
+            if (w and tag is None) or n in PSUM:
                 h[:] = [e for e in h if not (a <= e[0] and e[1] <= b)]
             h.append((a, b, i, w))
         for j in after:
@@ -115,47 +127,62 @@ def rank_program(g, core, T, topo):
             return FIX + o[3] * SCA * 1e-3
         if any(isop(v) and v[2] for v in ins):
             return FIX + o[3] * GA * 1e-3
-        return FIX + max(64, max(v[3] for v in ins + [o] if isop(v)) * base) * 1e-3
+        return FIX + max(64, max(v[3] for v in ins + [o] if isop(v)) * base) * CYC * 1e-3
     half = lambda *v: 0.5 if all(x[4] for x in v) else 1.0
 
     def tc(o, a, **k): return op("dve", lambda e: e.tensor_copy(o[0], a[0]), [o], [a], vc_(o, [a], half(o, a)), **k)
-    def tt(o, a, b, f, **k): return op("dve", lambda e: e.tensor_tensor(o[0], a[0], b[0], f), [o], [a, b], vc_(o, [a, b], 1 if a[5] or b[5] else 2 * half(o, a, b)), **k)
+    def tt(o, a, b, f, **k): return op("dve", lambda e: e.tensor_tensor(o[0], a[0], b[0], f), [o], [a, b], vc_(o, [a, b], (TTH if half(o, a, b) < 1 else 1) if a[5] or b[5] else 2 * half(o, a, b)), **k)
 
     def ts(o, a, s1, f0, s2=None, f1=None, **k):
         fn = (lambda e: e.tensor_scalar(o[0], a[0], ap(s1), None, f0)) if f1 is None else (lambda e: e.tensor_scalar(o[0], a[0], ap(s1), ap(s2), f0, f1))
         return op("dve", fn, [o], [a, s1, s2], vc_(o, [a], half(o, a)), **k)
     def scan(o, a, b, f0, f1, init=0.0): return op("dve", lambda e: e.tensor_tensor_scan(o[0], a[0], b[0], init, f0, f1), [o], [a, b], vc_(o, [a], half(o, a, b)))
+    def nmin(o, a): return op("dve", lambda e: e.tensor_reduce(o[0], a[0], AxisListType.X, O.min, negate=True), [o], [a], vc_(o, [a], 1))
     def red(o, a, f): return op("dve", lambda e: e.tensor_reduce(o[0], a[0], AxisListType.X, f), [o], [a], vc_(o, [a], 1))
     def ms(o, c): return op("dve", lambda e: e.memset(o[0], c), [o], [], vc_(o, [], half(o)))
 
     def act(o, a, bias=0.0, scale=1.0, f=F.Identity, acc=None, **k):
         fn = ((lambda e: e.activation(o[0], a[0], f, bias=ap(bias), scale=ap(scale))) if acc is None else
               (lambda e: e.activation(o[0], a[0], f, bias=ap(bias), scale=ap(scale), accum_out=acc[0])))
-        return op("act", fn, [o] + ([acc] if acc else []), [a, bias, scale], vc_(o, [a], 1), **k)
+        return op("act", fn, [o] + ([acc] if acc else []), [a, bias, scale], vc_(o, [a], 1) + (0.02 if acc else 0.0), **k)
+
+    def silu(o, a): return op("act", lambda e: e.activation(o[0], a[0], F.Silu), [o], [a], vc_(o, [a], 1))
 
     def mm(lst):
         def fn(e):
             for o, l, rr, s0, s1 in lst:
                 i = e.matmul(o[0], l[0], rr[0], s0, s1)
             return i
-        c = sum(max(min(64, l[3]), rr[3]) * (1 if l[4] else 4) for o, l, rr, s0, s1 in lst) * PEC + FIX
+        c = sum(max(min(64, l[3]), rr[3]) * (1 if l[4] else 4) for o, l, rr, s0, s1 in lst) * PEC
         return op("pe", fn, [x[0] for x in lst], [x[1] for x in lst] + [x[2] for x in lst], c)
     grp = lambda o, prs: [(o, l, rr, i == 0, i == len(prs) - 1) for i, (l, rr) in enumerate(prs)]
 
-    def wrap(o, W, n, a, b, odd=False):
-        return mm(grp(o, [(A(W, 15 - x, 143 - x), A(n, a + ((x | 1) if odd else x), b, 16)) for x in range(16)]))
+    def trs(lst):
+        def fn(e):
+            for o, a, idn in lst:
+                i = e.transpose(o[0], a[0], idn[0])
+            return i
+        return op("pe", fn, [x[0] for x in lst], [x[1] for x in lst] + [x[2] for x in lst], sum(max(64, x[2][3]) for x in lst) * PEC + 0.02)
+    wn = {"WW": {}, "WH": {}}
+
+    def W(n, x=None):
+        buf = "WH" if n in ("Ww", "Wv", "W1") else "WW"; k = 144 * wn[buf].setdefault(n, len(wn[buf]))
+        return A(buf, k, k + 144) if x is None else A(buf, k + 15 - x, k + 143 - x)
+
+    def wrap(o, w, n, a, b, odd=False):
+        return mm(grp(o, [(W(w, x), A(n, a + ((x | 1) if odd else x), b, 16)) for x in range(16)]))
 
     def iota(o, pat, base, cm):
         fl = _S[o[1][0][0]][1] != I4
         fn = (lambda e: e.iota(o[0], pat, base, cm, allow_small_or_imprecise_dtypes=True)) if fl else (lambda e: e.iota(o[0], pat, base, cm))
-        return op("pool", fn, [o], [], 0.25 + o[3] * 2e-3)
+        return op("pool", fn, [o], [], 0.25 + o[3] * 2 * CYC * 1e-3)
 
     def dma(o, a, q="sync", tag=None, lat=2.5): return op(q, lambda e: e.dma_start(o[0], a[0]), [o], [a], 0.1, lat, "dma", tag)
 
     def load(n, a, b, src, dr, sr, q):
-        dma(A(n, a, b, p=(0, dr * (8 - r))), X(src[sr * r:sr * 8, :]), q, "ld" + n)
-        if r:
-            dma(A(n, a, b, p=(dr * (8 - r), dr * 8)), X(src[0:sr * r, :]), q, "ld" + n)
+        for x, y in ((0, cut[1] // 16), (cut[1] // 16, 8)):
+            dma(A(n, a, b, p=(dr * x, dr * y)), X(src[sr * ((x + r) % 8):sr * ((x + r) % 8 + y - x), :]), q, "ld" + n)
+    cut = (0, 128 - 16 * r if r else 64, 128)
     rowsof = lambda n, row, a, b: (T[n][row:128:16, a:b], [(n, a, b)], [], 0, False, False)
     PS = lambda bank, a, b, s=1, p=(0, 128): A("PS", 512 * bank + a, 512 * bank + b, s, p)
     cn = {}
@@ -165,101 +192,126 @@ def rank_program(g, core, T, topo):
     ci = lambda k: A("CI", k, k + 1)
     oh = lambda k: A("OH", k, k + 1)
     dd = lambda k: A("DD", k, k + 1)
-    cut = sorted({0, 64, 128 - 16 * r, 128})
 
     load("PLi", 0, 256, T.pr, 16, 1, "sync"); load("MTi", 0, 128, T.mt, 16, 1, "act")
     load("CI", 16, 17, T.kk, 16, 16, "sync"); load("CI", 20, 21, T.w, 16, 16, "act"); load("CI", 24, 25, T.th, 1, 1, "sync")
     for k in range(len(cut) - 1):
         a, b = cut[k], cut[k + 1]; ra = (a + 16 * r) % 128
         dma(A("Q", 0, 4096, p=(a, b)), X(T.rec[ra:ra + b - a, :]), "act" if k % 2 else "sync", "ldQ", 6.0)
-    ms(A("S1", 0, TW), 0.0)
+    ms(A("S1", 0, 2048), 0.0); ms(A("S1", 2048, 4096), 0.0)
     iota(ci(0), [[0, 1]], 0, 1); iota(A("IO", 0, 160), [[1, 160]], 0, 0); iota(A("I16c", 0, 256), [[0, 16], [1, 16]], 0, 0)
     iota(A("IL", 0, 256), [[1, 256]], 0, 0); iota(A("ONE", 0, 256), [[0, 256]], 1, 0)
     ts(ci(1), ci(0), 15, O.bitwise_and); ts(ci(2), ci(0), 4, O.arith_shift_right); ts(ci(3), ci(0), 1, O.bitwise_and)
     ts(ci(4), ci(0), 4, O.arith_shift_right, 1, O.bitwise_and); ts(ci(5), ci(0), 3, O.arith_shift_right); ts(ci(6), ci(0), 7, O.bitwise_and)
-    tc(A("CF", 0, 7), A("CI", 0, 7))
-    for n in ("p", "x", "b", "p1", "odd", "r8", "p7"):
+    ts(ci(7), ci(0), 15, O.bitwise_and, 1, O.arith_shift_right)
+    tc(A("CF", 0, 8), A("CI", 0, 8))
+    for n in ("p", "x", "b", "p1", "odd", "r8", "p7", "x2"):
         c(n)
     ts(A("OH", 0, 16), A("IO", 0, 16), c("x"), O.is_equal)
-    act(A("DD", 0, 15), A("OH", 0, 15), scale=64.0); tt(A("DD", 0, 15), A("DD", 0, 15), A("OH", 1, 16), O.add)
+    act(A("DD", 0, 15), A("OH", 0, 15), scale=256.0); tt(A("DD", 0, 15), A("DD", 0, 15), A("OH", 1, 16), O.add)
     act(c("b15"), c("b"), bias=15.0, scale=16.0); act(c("p16"), c("p"), bias=16.0)
-    ts(A("WB", 0, 144), A("IO", 0, 144), c("b15"), O.is_equal); ts(A("IW", 0, 160), A("IO", 0, 160), c("p16"), O.is_equal)
-    act(c("wg"), oh(7), bias=oh(4), scale=512.0); act(c("f47"), oh(7), bias=oh(4))
-    for n, s in (("Wf", oh(4)), ("Wp", dd(0)), ("Wmp", dd(5)), ("Wix", dd(12)), ("Wg", c("wg"))):
-        act(A(n, 0, 144), A("WB", 0, 144), scale=s)
-    sh = lambda k: A("IW", 16 - k, 144 - k)
+    ts(W("WB"), A("IO", 0, 144), c("b15"), O.is_equal); ts(A("IW", 0, 160), A("IO", 0, 160), c("p16"), O.is_equal)
     ts(c("hi"), c("x"), 8.0, O.is_ge); act(c("lo"), c("hi"), bias=1.0, scale=-1.0); ts(c("l12"), c("x"), 12.0, O.is_lt)
-    ts(A("MASK", 0, 256), A("I16c", 0, 256), c("x"), O.is_equal); act(A("RS", 0, 256), A("I16c", 0, 256), f=F.Sign)
-    act(A("RK", 0, 256), A("RS", 0, 256), bias=33554432.0, scale=-33554496.0)
-    act(A("MNG", 0, 256), A("MASK", 0, 256), bias=-2.0 ** 30, scale=2.0 ** 30); act(A("CS", 0, 256), A("ONE", 0, 256), scale=oh(4))
+    act(c("wg"), oh(12), bias=oh(4), scale=512.0); act(c("w3a"), oh(8), scale=-2048.0); act(c("w3"), oh(7), bias=c("w3a"), scale=8192.0)
+    for n, s in (("Wf", oh(4)), ("Wp", dd(0)), ("Wmp", dd(5)), ("Wg", c("wg")), ("W8", c("lo"))):
+        act(W(n), W("WB"), scale=s)
+    ts(W("W1"), W("WB"), oh(0), O.mult)
+    sh = lambda k: A("IW", 16 - k, 144 - k)
+    ts(A("MASK", 0, 256), A("I16c", 0, 256), c("x"), O.is_equal)
+    act(A("MNG", 0, 128), A("MASK", 0, 128), bias=-2.0 ** 30, scale=2.0 ** 30); act(A("CS", 0, 256), A("ONE", 0, 256), scale=oh(4))
     iota(M("Z"), [[0, 128]], 0, 0); iota(M("t0"), [[1, 8], [0, 16]], 0, 0); ts(M("BD"), M("t0"), c("b"), O.is_equal)
     ts(M("t1"), A("IO", 0, 128), c("p"), O.is_ge); tt(M("TRI"), M("t1"), M("BD"), O.mult)
     act(M("t0"), sh(8), scale=c("lo")); act(M("t1"), sh(-8), scale=c("hi")); tt(M("PERM"), M("t0"), M("t1"), O.add)
     act(M("PERMn"), M("PERM"), scale=-1.0); act(M("N4096"), sh(0), scale=-4096.0); act(M("BDi"), M("BD"), scale=dd(12)); act(M("In"), sh(0), scale=-1.0)
-    act(A("I32", 0, 128), sh(0)); tc(A("I16", 0, 128), sh(0)); tc(A("I16", 128, 256), M("PERM"))
-    act(A("PI2", 0, 128), sh(0), scale=8388608.0); act(A("PI2", 128, 256), sh(0), scale=8388608.0)
-    act(A("HI2", 0, 128), sh(0), scale=-64.0); act(A("HI2", 128, 256), sh(0))
+    tc(A("I16", 0, 128), sh(0)); tc(A("I16", 128, 256), M("PERM"))
+    tt(M("t1"), M("PERM"), sh(0), O.add); act(M("Msel"), M("t1"), scale=oh(4))
+    act(c("nj"), dd(2), scale=-1.0); act(M("MJ"), A("WW", 0, 128), scale=c("nj"))
+    iota(A("KIX", 0, KN), [[0, 2], [32, 8], [1, KW]], 0, 0); act(c("k32"), c("b"), bias=c("x"), scale=32.0); act(c("k48"), c("k32"), bias=16.0)
+    ts(A("PI2", 0, KN), A("KIX", 0, KN), c("k32"), O.is_equal, 2.0 ** 23, O.mult); ts(A("KIX", KN, 2 * KN), A("KIX", 0, KN), c("k48"), O.is_equal, 2.0 ** 26, O.mult)
+    act(A("HI2", 0, KN // 2), A("PI2", 0, KN // 2), scale=-2.0 ** -17); act(A("HI2", KN // 2, KN), A("PI2", KN // 2, KN), scale=2.0 ** -23)
+    tt(A("HI2", 0, KN), A("HI2", 0, KN), A("KIX", KN, 2 * KN), O.add); act(A("I32", 0, KN // 2), A("PI2", 0, KN // 2), scale=2.0 ** -23)
+    ms(A("RK", 0, KN), -64.0)
+    for k, v in ((0, 2.0 ** 25), (16, -8387040.5), (17, 1.5 * 2.0 ** 29), (18, -1.5 * 2.0 ** 29)):
+        ms(A("RK", k, KN, KW), v)
     act(c("m01"), oh(0), bias=oh(1)); act(c("m56"), oh(5), bias=oh(6)); act(c("mk"), oh(12), bias=oh(13)); act(c("m4"), c("m01"), bias=c("m56"))
-    act(c("keep"), c("m56"), bias=1.0, scale=-1.0); act(c("md"), oh(13), bias=oh(14), scale=1.0 / 64)
-    for n, k, s in (("MI", 0, "m4"), ("Mup", 12, "m01"), ("Mdn", -12, "mk"), ("Mk", 0, "mk"), ("M56", 0, "m56"), ("Md", -11, "md"), ("M7", -7, "mk")):
-        act(M(n), sh(k), scale=c(s))
+    act(c("keep"), c("m56"), bias=1.0, scale=-1.0); act(c("md"), oh(13), bias=oh(14), scale=1.0 / 256); act(c("m89"), oh(8), bias=oh(9))
+    act(c("own"), c("mk"), bias=c("m89")); act(c("k89"), c("m89"), bias=1.0, scale=-1.0); act(c("kx"), c("m89"), bias=c("keep"), scale=-1.0)
+    for n, prs in (("Mo", ((0, "m4"), (12, "m01"), (3, "m56"))), ("Mx", ((-12, "mk"), (-3, "m89"))), ("Mk", ((0, "own"),)), ("Md", ((-11, "md"),)),
+                   ("M7", ((-7, "mk"),)), ("M4", ((-4, "mk"),)), ("K89", ((0, "k89"),)), ("Kx", ((0, "kx"),)), ("Mz", ((0, "m56"), (3, "m56")))):
+        for j, (k, s) in enumerate(prs):
+            act(M("t2" if j else n), sh(k), scale=c(s))
+            if j:
+                tt(M(n), M(n), M("t2"), O.add)
     act(M("t0"), sh(0), scale=c("l12")); I12 = M("t0"); Ib = sh(0)
-    GG, GN, GP, GJ, GD, G64 = (A("GM", 16 * k, 16 * k + 16) for k in range(6))
+    GG, GN, GP, G15, GD, G64, G1x = (A("GM", 16 * k, 16 * k + 16) for k in range(7))
     ts(A("GM", 0, 8), A("IO", 0, 8), c("b"), O.is_equal); act(A("GM", 8, 16), A("GM", 0, 8))
-    act(GN, GG, scale=-1024.0); act(GP, GG, scale=2048.0); act(GJ, GG, scale=dd(2)); act(GD, GG, scale=-512.0); act(G64, GG, scale=64.0)
+    act(c("g15"), oh(15), scale=-2.0 ** 40); act(c("gd"), oh(7), scale=-8192.0)
+    act(GN, GG, scale=-1024.0); act(GP, GG, scale=2048.0); act(G15, GG, scale=c("g15")); act(GD, GG, scale=c("gd")); act(G64, GG, scale=64.0)
     G1 = A("GM", 0, 8); G64 = A("GM", 80, 88)
+    act(G1x, GG, scale=0.0); act(A("GM", 97, 112, 2), G1)
     act(c("pd"), c("p1"), bias=1.0, scale=-2.0); act(c("off"), c("pd"), bias=-0.5, scale=3072.0); act(c("even"), c("odd"), bias=1.0, scale=-1.0)
     act(c("s1"), c("l12"), scale=-1048576.0); act(c("s4"), oh(13), bias=oh(14)); act(c("s3"), c("s4"), bias=oh(12), scale=256.0)
-    act(c("s2"), oh(15), bias=c("s3"), scale=2097152.0); act(c("nlo"), c("lo"), scale=-512.0); act(c("nhi"), c("hi"), scale=-512.0)
+    act(c("s2"), oh(15), bias=c("s3"), scale=2097152.0)
+    for n in ("even", "odd"):
+        act(c("s1" + n), c("s1"), scale=c(n)); act(c("s2" + n), c("s2"), scale=c(n))
+    act(c("r1"), oh(15), scale=2049.0); act(c("r2"), oh(15), bias=-1.0)
+    act(c("tl0"), c("p"), bias=-12582912.0); act(c("tl1"), c("p"), bias=-12582912.0 + 128)
     iota(A("CO", 208, 224), [[16, 16]], 0, 0); act(A("LW", 0, 16), A("CO", 208, 224), bias=c("x"))
     DU1, DU2, L257 = A("BA", 0, 16), A("BA", 32, 48), A("CO", 32, 48)
     act(L257, A("LW", 0, 16), bias=257.0)
-    TL = A("CO", 64, 96); iota(TL, [[128, 2], [0, 16]], -12582912, 1)
-    OB = A("CO", 96, 128)
-    for k, bs in enumerate((D1, 0, D2, D1)):
-        act(A("CO", 96 + 8 * k, 104 + 8 * k), A("LW", 0, 8), bias=float(bs))
-    DB = A("CO", 128, 144); act(A("CO", 128, 136), A("LW", 0, 8), bias=float(D1)); act(A("CO", 136, 144), A("LW", 0, 8), bias=float(D2))
-    for k in range(3):
-        act(A("BA", 16 * k, 16 * k + 16), A("LW", 0, 16), bias=float(D2 if k == 2 else D1))
+    OB = A("CO", 96, 126)
+    for k, bs in ((0, D1), (8, 0), (16, D1 + 128), (23, D1)):
+        act(A("CO", 96 + k, 104 + k), A("LW", 0, 8), bias=float(bs))
+    act(A("LB", 0, 7), A("LW", 0, 7), bias=128.0); act(A("LB", 7, 14), A("LW", 0, 7))
+    act(c("np1"), c("p1"), bias=1.0, scale=-1.0); act(A("CO", 64, 80), A("LW", 0, 16))
+    act(A("CO", 80, 88), A("LW", 0, 8), bias=c("np1")); act(A("CO", 87, 95), A("LW", 0, 8), bias=c("np1"))
+    act(c("b5"), dd(5), scale=-12582912.0 - 128); act(c("b12"), dd(12), scale=-12582912.0 - 128); act(M("BD4"), M("BD"), scale=oh(4))
+    for k, bs in enumerate((D1, D2, D1)):
+        act(A("BA", 16 * k, 16 * k + 16), A("LW", 0, 16), bias=float(bs))
+    act(A("DX", 1, 96, 2), A("BA", 0, 48))
     iota(A("CO", 144, 160), [[16, 2], [1, 8]], 0, 0); iota(A("CO", 160, 176), [[1, 2], [0, 8]], 0, 0)
-    EL, EH, E2L = A("UL", 0, 16), A("UL", 16, 32), A("UL", 32, 48)
-    tc(EL, A("IO", 0, 16)); tc(EH, A("CO", 144, 160))
+    EL, L2, E2L = A("UL", 0, 16), A("UL", 16, 17), A("UL", 32, 48)
+    tc(EL, A("IO", 0, 16)); tc(L2, c("x2"))
     ts(c("c1"), c("x"), 13.0, O.is_ge); act(c("c4"), oh(14), scale=32.0); act(c("c2"), oh(15), bias=c("c4"), scale=64.0)
     act(c("c3"), oh(12), bias=c("c2"), scale=96.0); act(c("c5"), c("l12"), bias=c("c3"), scale=98.0)
     act(A("CO", 176, 192), A("CO", 144, 160), bias=c("c5"), scale=c("c1")); act(A("CO", 192, 208), A("CO", 160, 176), scale=oh(12))
     tt(A("CO", 176, 192), A("CO", 176, 192), A("CO", 192, 208), O.add); tc(E2L, A("CO", 176, 192))
-    iota(A("DW", 96, 98), [[128, 2]], 0, 1); iota(A("DW", 98, 104), [[0, 6]], 0, 0)
+    iota(A("DW", 0, 104), [[0, 104]], 0, 0); iota(A("DW", 96, 98), [[128, 2]], 0, 1)
     HC = A("TJ", 384, 480); iota(HC, [[64, 3], [0, 32]], -192, 0)
-    for n, a, b, v in (("MN", 0, 32, 8000000), ("LS", 0, 32, 0), ("C3", 128, 136, 0), ("Q", 4096, TW, 0), ("BITS", 4096, TW, 0), ("S2", 4096, TW, 0)):
+    for n, a, b, v in (("ML", 0, 64, 0), ("TH", 0, 96, 0), ("C3", 128, 136, 4096), ("SS", 8, 16, 4096), ("Q", 4096, TW, 0), ("BITS", 4096, TW, 0), ("S1", 4096, TW, 0),
+                       ("Z", 0, 256, 0), ("P6", 0, 96, 0)):
         iota(A(n, a, b), [[0, b - a]], v, 0)
-    ms(A("S2", 0, 2048), 0.0); ms(A("VT", 0, 2048), 0.0)
+    ts(A("CE", 0, 16), A("ONE", 0, 16), 0.0, O.mult)
     for t in range(4):
-        iota(A("SB", 512 * t + 256, 512 * t + 384), [[0, 128]], -1, 0); iota(A("SA", 512 * t + 256, 512 * t + 384), [[0, 128]], 0, 0)
+        iota(A("SB", 512 * t + 256, 512 * t + 368), [[0, 112]], 1000, 0); iota(A("SA", 512 * t + 256, 512 * t + 368), [[0, 112]], 128 * SAS, 0)
     p8 = (0, 8)
-    ts(A("CI", 25, 26, p=p8), A("CI", 24, 25, p=p8), 6, O.arith_shift_right); ts(A("CI", 26, 27, p=p8), A("CI", 24, 25, p=p8), 63, O.bitwise_and)
+    ts(A("CI", 25, 26, p=p8), A("CI", 24, 25, p=p8), 8, O.arith_shift_right); ts(A("CI", 26, 27, p=p8), A("CI", 24, 25, p=p8), 255, O.bitwise_and)
     tc(A("TM", 384, 386, p=p8), A("CI", 25, 27, p=p8)); iota(A("TM", 256, 384, p=p8), [[1, 8], [0, 16]], 0, -1)
     ts(A("TM", 256, 384, p=p8), A("TM", 256, 384, p=p8), 0.0, O.is_equal)
-    mm(grp(PS(7, 0, 2), [(A("TM", 256, 384, p=p8), A("TM", 384, 386, p=p8))])); c("th0"); c("th1")
-    act(A("CF", cn["th0"], cn["th1"] + 1), PS(7, 0, 2))
-    act(c("t2"), oh(2), bias=c("f47"), scale=c("th0")); act(c("thb"), oh(3), bias=c("t2"), scale=c("th1"))
+    mm(grp(PS(3, 0, 2), [(A("TM", 256, 384, p=p8), A("TM", 384, 386, p=p8))])); c("th0"); c("th1")
+    act(A("CF", cn["th0"], cn["th1"] + 1), PS(3, 0, 2))
+    act(c("t2"), oh(2), bias=oh(4), scale=c("th0")); act(c("thb"), oh(3), bias=c("t2"), scale=c("th1"))
     tb = lambda k: A("TB", 256 * k, 256 * k + 256)
-    act(c("x256"), c("x"), scale=256.0); act(c("x4"), c("x"), scale=4.0); act(A("TF", 0, 256), A("IL", 0, 256), bias=c("x256"))
-    tt(tb(4), A("PLi", 0, 256), A("TF", 0, 256), O.is_equal); dma(rowsof("S1", 4, 0, 4096), tb(4), "sync", "s1")
-    ts(A("TJ", 0, 256), A("PLi", 0, 256), 6, O.arith_shift_right); tc(tb(0), A("TJ", 0, 256))
-    ts(A("TI", 0, 256), A("PLi", 0, 256), 63, O.bitwise_and); tc(tb(1), A("TI", 0, 256))
-    iota(tb(2), [[1, 4], [0, 64]], 0, 0); act(tb(5), tb(2), bias=c("x4")); iota(tb(6), [[0, 4], [1, 64]], 0, 0)
-    act(tb(2), A("ONE", 0, 256), scale=c("th0")); act(tb(3), A("ONE", 0, 256), scale=c("th1"))
-    for k, row in ((0, 0), (1, 1), (5, 12), (6, 13), (2, 2), (3, 3), (4, 7)):
-        dma(rowsof("S1", row, 0, 4096), tb(k), "sync", "s1")
+    act(c("x256"), c("x"), scale=256.0); ts(A("TF", 0, 256), A("PLi", 0, 256), c("x256"), O.subtract)
+    tt(tb(4), A("TF", 0, 256), A("IL", 0, 256), O.is_equal); dma(rowsof("S1", 4, 0, 4096), tb(4), "sync", "s1")
+    ts(tb(0), A("PLi", 0, 256), 1.0 / 256, O.mult, 129.0 - 127.5 / 256, O.add); act(tb(0), tb(0), bias=-129.0)
+    ts(A("TI", 0, 256), A("PLi", 0, 256), 255, O.bitwise_and); tc(tb(1), A("TI", 0, 256))
+    act(tb(5), A("ONE", 0, 256), scale=c("x")); act(tb(2), A("ONE", 0, 256), scale=c("th0")); act(tb(3), A("ONE", 0, 256), scale=c("th1"))
+    m8, m9 = A("TB", 1792, 1920), A("TB", 1920, 2048)
+    ts(m8, A("MTi", 0, 128), 1.0 / 256, O.mult, 128.0 - 127.5 / 256, O.add); act(m8, m8, bias=-128.0)
+    ts(A("TJ", 256, 384), A("MTi", 0, 128), 255, O.bitwise_and); tc(m9, A("TJ", 256, 384))
+    dma(rowsof("S1", 8, 0, 2048), m8, "sync", "s1"); dma(rowsof("S1", 9, 0, 2048), m9, "sync", "s1")
+    for src, row in ((tb(0), 0), (tb(1), 1), (tb(5), 12), (A("IL", 0, 256), 13)):
+        dma(rowsof("S1", row, 0, 4096), src, "sync", "s1")
     ts(A("MTu", 0, 128), A("MTi", 0, 128), -2048.0, O.add)
-    iota(A("TM", 0, 128), [[0, 8], [2, 16]], 0, 0); act(A("TM", 0, 128), A("TM", 0, 128), bias=c("hi"))
-    iota(A("TM", 128, 256), [[1, 8], [0, 16]], 0, 0); act(c("x8"), c("p7"), scale=8.0); act(A("TM", 128, 256), A("TM", 128, 256), bias=c("x8"))
-    dma(rowsof("VT", 5, 0, 2048), A("TM", 0, 128), "sync", "VT"); dma(rowsof("VT", 6, 0, 2048), A("TM", 128, 256), "sync", "VT")
-    ts(A("TJ", 256, 384), A("MTi", 0, 128), 6, O.arith_shift_right); tc(A("TB", 1792, 1920), A("TJ", 256, 384))
-    ts(A("TJ", 256, 384), A("MTi", 0, 128), 63, O.bitwise_and); tc(A("TB", 1920, 2048), A("TJ", 256, 384))
-    dma(rowsof("S2", 5, 0, 2048), A("TB", 1792, 1920), "sync", "S2"); dma(rowsof("S2", 6, 0, 2048), A("TB", 1920, 2048), "sync", "S2")
+    iota(A("TM", 0, 256), [[0, 16], [1, 8], [0, 2]], 0, 0); iota(A("VT", 256, 512), [[1, 16], [0, 8], [128, 2]], 0, 0)
+    act(A("TM", 0, 256), A("TM", 0, 256), scale=oh(8)); act(A("VT", 256, 512), A("VT", 256, 512), scale=oh(9)); tt(A("VT", 0, 256), A("VT", 256, 512), A("TM", 0, 256), O.add)
+    act(c("o9"), oh(9), scale=16.0); act(A("CO", 240, 248), A("IO", 0, 8), scale=c("o9"))
     for k in range(8):
+        if k:
+            act(A("VT", 256 * k, 256 * k + 256), A("VT", 0, 256), bias=A("CO", 240 + k, 241 + k))
         tc(IX(A("S2", 2048, 4096), A("MTu", 16 * k, 16 * k + 16)), A("VT", 256 * k, 256 * k + 256))
+    dma(A("S2", 0, 2048), A("S1", 0, 2048), "sync", None, 4.0)
     kj = lambda a, b: A("KJ", 0, 128, p=(a, b))
     iota(kj(0, 32), [[1, 2], [0, 64]], 0, 2); iota(kj(32, 64), [[0, 2], [1, 64]], 0, 0); iota(kj(64, 96), [[1, 128]], 0, 128); iota(kj(96, 128), [[1, 128]], 0, 128)
     tt(kj(64, 128), kj(64, 128), kj(64, 128), O.mult)
@@ -267,165 +319,199 @@ def rank_program(g, core, T, topo):
     tc(A("TU", 0, 128), kj(0, 128)); dma(A("UR", 0, 4096, p=(0, 4)), A("TU", 0, 128), "sync")
     ts(ci(8), ci(16), 63, O.bitwise_and); ts(A("KC", 0, 1), ci(8), 64.0, O.mult); tc(A("KC", 1, 2), ci(16))
     ts(A("KC", 2, 3), A("ONE", 0, 1), 64.0, O.mult); tc(A("KC", 3, 4), A("ONE", 0, 1))
-    mm(grp(PS(6, 0, 128, p=(0, 4)), [(A("KC", 0, 4), A("I16", 0, 128))])); tc(A("KL", 0, 128, p=(0, 4)), PS(6, 0, 128, p=(0, 4)))
-    for k in range(8):
-        pr = (A("KL", 0, 128, p=(0, 4)), A("UR", 512 * k, 512 * k + 512, p=(0, 4))); nb = A("NB", 512 * (k % 2), 512 * (k % 2) + 512)
-        mm(grp(PS(k % 2, 0, 512), [pr])); act(nb, PS(k % 2, 0, 512), bias=129.0 - 4095.0 / 8192, scale=1.0 / 4096)
-        mm(grp(PS(2 + k % 2, 0, 512), [pr, (M("N4096"), nb)]))
-        if k % 2:
-            ts(A("CT", 512 * k, 512 * k + 512), PS(2 + k % 2, 0, 512), 528384.0, O.add)
-        else:
-            act(A("CT", 512 * k, 512 * k + 512), PS(2 + k % 2, 0, 512), bias=528384.0)
-    tc(A("KC", 4, 5), ci(20)); ts(c("w2"), ci(20), 0.5, O.mult); ts(A("Ww", 0, 144), A("WB", 0, 144), c("w2"), O.mult)
+    mm(grp(PS(3, 128, 256, p=(0, 4)), [(A("KC", 0, 4), A("I16", 0, 128))])); tc(A("KL", 0, 128, p=(0, 4)), PS(3, 128, 256, p=(0, 4)))
+    tc(A("KC", 4, 5), ci(20)); ts(c("w2"), ci(20), 0.5, O.mult); ts(W("Ww"), W("WB"), c("w2"), O.mult)
     ts(A("KC", 6, 7), ci(20), c("pd"), O.mult); tc(A("TU", 128, 256), M("BD"))
-    mm(grp(PS(7, 8, 9), [(A("I16", 128, 256), A("KC", 4, 5))]) + grp(PS(7, 9, 10), [(A("TU", 128, 256), A("KC", 6, 7))]))
-    act(c("wv"), PS(7, 8, 9)); act(c("cw"), PS(7, 9, 10), scale=-1536.0); ts(A("Wv", 0, 144), A("WB", 0, 144), c("wv"), O.mult)
+    mm(grp(PS(3, 8, 9), [(A("I16", 128, 256), A("KC", 4, 5))]) + grp(PS(3, 9, 10), [(A("TU", 128, 256), A("KC", 6, 7))]))
+    act(c("wv"), PS(3, 8, 9)); act(c("cw"), PS(3, 9, 10), scale=-1536.0); ts(W("Wv"), W("WB"), c("wv"), O.mult)
+    for t in range(4):
+        ts(c("wt%d" % t), c("x"), float((2047 - 341 * t) % 16), O.is_le); act(W("WT%d" % t), W("WB"), scale=c("wt%d" % t))
 
     def lanes(t):
-        s = (341 * t) % 2048; lst = [(PS(6, 0, 128), M("Z"), Ib, True, False)]
+        s = 341 * t; lst = [(PS(2, 0, 128), M("Z"), Ib, True, False)]
         for x in range(16):
-            f = s + x; n1 = min(128, (2048 - f + 15) // 16); W = A("Wf", 15 - x, 143 - x)
-            lst.append((PS(6, 0, n1), W, A("S1", f, 2048, 16), False, x == 15 and n1 == 128))
+            f = s + x; n1 = min(128, (2048 - f + 15) // 16); Wx = W("Wf", x)
+            lst.append((PS(2, 0, n1), Wx, A("S1", f, 2048, 16), False, x == 15 and n1 == 128))
             if n1 < 128:
                 f2 = f + 16 * n1 - 2048
-                lst.append((PS(6, n1, 128), W, A("S1", f2, f2 + 16 * (128 - n1), 16), False, x == 15))
+                lst.append((PS(2, n1, 128), Wx, A("S1", f2, f2 + 16 * (128 - n1), 16), False, x == 15))
             if x % 4 == 3:
                 mm(lst); lst = []
-        act(A("FWb", 0, 128), PS(6, 0, 128))
-        mm(grp(PS(7, 128, 256), [(M("BD"), A("FWb", 0, 128))]) + grp(PS(7, 0, 128), [(M("TRI"), A("FWb", 0, 128))]))
-        scan(A("CE", 0, 128), A("ONE", 0, 128), PS(7, 128, 256), O.mult, O.add)
-        tt(A("SM", 0, 128), A("CE", 0, 128), A("MASK", 0, 128), O.mult); scan(A("SS", 0, 128), A("RS", 0, 128), A("SM", 0, 128), O.mult, O.add)
-        act(A("SW", 112, 116), A("SS", 15, 64, 16), bias=0.5, scale=-1.0)
-        tt(A("SM", 128, 256), A("CE", 0, 128), PS(7, 128, 256), O.subtract); tt(A("C3", 0, 128), A("SM", 128, 256), PS(7, 0, 128), O.add)
-        for j in (4, 0, 5, 1, 6, 2, 7, 3):
-            if j < 4:
-                act(A("IND", 256 * j, 256 * j + 256), A("IL", 0, 256), bias=A("SW", 112 + j, 113 + j), f=F.Sign)
-            else:
-                ts(A("IND", 256 * j, 256 * j + 256), A("IL", 0, 256), A("SS", 16 * j + 15, 16 * j + 16), O.is_ge, 2.0, O.mult)
-            mm([(PS(6, 256, 512), M("BD"), A("IND", 256 * j, 256 * j + 256), j == 4, j == 3)])
-        tt(A("SM", 0, 256), PS(6, 256, 512), A("MASK", 0, 256), O.mult); scan(A("SS", 0, 256), A("RS", 0, 256), A("SM", 0, 256), O.mult, O.add)
-        cw = A("SS", 15, 256, 16); w = lambda k: A("SW", 16 * k, 16 * k + 16)
-        ts(A("cu", 0, 16), cw, 0.5, O.mult, 32.0, O.add); tt(A("XI", 0, 256), IX(A("C3", 0, 136), A("cu", 0, 16)), A("IL", 0, 256), O.is_le)
-        wrap(PS(7, 256, 272), "WB", "XI", 0, 256)
-        act(w(0), cw, bias=512.0 + s, scale=8.0); act(w(1), cw, bias=-191.0, f=F.Relu); act(A("dR", 0, 256), PS(6, 256, 512), bias=-191.0, f=F.Relu)
-        tt(w(2), w(1), DU1, O.mult)
-        tt(w(3), w(0), PS(7, 256, 272), O.add); ts(w(4), w(3), 2048.0, O.is_ge, -2048.0, O.mult); tt(w(3), w(3), w(4), O.add)
-        tt(w(5), w(3), w(2), O.max); tc(A("aW", 0, 16), w(5)); tt(A("DF", 16, 32), w(5), DU1, O.subtract)
+        FW = A("FWb", 0, 128); IL = A("IL", 0, 256); w = lambda k: A("SW", 16 * k, 16 * k + 16); c0 = (2047 - s) // 16
+        act(FW, PS(2, 0, 128)); mm(grp(PS(2, 128, 256), [(M("BD"), FW)]))
+        scan(A("CE", 16, 144), A("ONE", 0, 128), PS(2, 128, 256), O.mult, O.add)
+        mm(grp(PS(2, 384, 385), [(W("W1", x), A("CE", 31 + 16 * x, 32 + 16 * x)) for x in range(8)]
+               + [(W("W1", 8), A("CE", 15 + c0, 16 + c0)), (W("WT%d" % t, 8), A("FWb", c0, c0 + 1))]))
+        ts(A("IND", 0, 256), IL, PS(2, 384, 385), O.is_ge)
+        wrap(PS(3, 400, 408), "W1", "CE", 16, 144); act(A("SS", 0, 8), PS(3, 400, 408))
+        wrap(PS(2, 400, 416), "W8", "IND", 0, 256); tc(A("cu", 0, 16), PS(2, 400, 416)); act(w(0), PS(2, 400, 416), scale=16.0)
+        mm(grp(PS(3, 256, 384), [(M("TRI"), FW), (A("I16", 0, 128), A("CE", 15, 143))])); act(A("C3", 0, 128), PS(3, 256, 384))
+        act(A("XI", 256, 512), A("IND", 0, 256), scale=c("w3"))
+        tt(A("XI", 0, 256), IX(A("SS", 0, 16), A("cu", 0, 16)), IL, O.is_le)
+        wrap(PS(2, 416, 448), "WB", "XI", 0, 512); tt(w(1), PS(2, 416, 432), w(0), O.add); tc(A("cu", 16, 32), w(1))
+        act(w(2), w(1), bias=float(s), scale=16.0); tt(w(3), PS(2, 432, 448), w(2), O.add)
+        tt(A("XI", 512, 768), IX(A("C3", 0, 136), A("cu", 16, 32)), IL, O.is_le)
+        wrap(PS(2, 448, 464), "WB", "XI", 512, 768); tt(w(4), PS(2, 448, 464), w(3), O.add)
+        ts(A("aW", 0, 16), w(4), float(DUM), O.min); tt(A("DX", 64, 96, 2), w(4), DU1, O.subtract)
 
-    lanes(0); act(A("no", 0, 256), IX(A("S1", 0, TW), A("aW", 0, 16)))
-    wrap(PS(4, 0, 256), "Wp", "S1", 0, 4096); tc(A("PWu", 0, 256), PS(4, 0, 256))
+    for k in range(4):
+        mm([(PS(3, 0, 256), W("Wp", x), A("S1", x, 4096, 16), x == 0, x == 15) for x in range(4 * k, 4 * k + 4)])
+    tc(A("PWu", 0, 256), PS(3, 0, 256))
     for k in range(8):
-        act(A("MPT", 512 * k, 512 * k + 512), IX(A("S2", 0, 4096), A("PWu", 32 * k, 32 * k + 32)))
-    dma(rowsof("S1", 5, 0, 4096), rowsof("MPT", 5, 0, 4096), "sync", "mp"); dma(rowsof("S1", 6, 0, 4096), rowsof("MPT", 6, 0, 4096), "sync", "mp")
-    ts(c("r12"), c("r8"), 12.0, O.is_lt); act(c("r12b"), c("r12"), scale=-0.5 + 2.0 ** -13)
+        pr = (A("KL", 0, 128, p=(0, 4)), A("UR", 512 * k, 512 * k + 512, p=(0, 4))); nb = A("NB", 512 * (k % 2), 512 * (k % 2) + 512)
+        mm(grp(PS(0, 0, 512), [pr])); act(nb, PS(0, 0, 512), bias=129.0 - 4095.0 / 8192, scale=1.0 / 4096)
+        mm(grp(PS(1, 0, 512), [pr, (M("N4096"), nb)]))
+        if k % CTV == CTV - 1:
+            ts(A("CT", 512 * k, 512 * k + 512), PS(1, 0, 512), 528384.0, O.add)
+        else:
+            act(A("CT", 512 * k, 512 * k + 512), PS(1, 0, 512), bias=528384.0)
+    lanes(0); act(A("no", 0, 256), IX(A("S1", 0, TW), A("aW", 0, 16)))
+    for k in range(8):
+        (tc if k < MPV else act)(A("MPT", 512 * k, 512 * k + 512), IX(A("S2", 0, 4096), A("PWu", 32 * k, 32 * k + 32)))
+    dma(rowsof("S1", 8, 2048, 4096), rowsof("S2", 8, 2048, 4096), "sync", "mp"); dma(rowsof("S1", 9, 2048, 4096), rowsof("S2", 9, 2048, 4096), "sync", "mp")
+    dma(rowsof("S1", 2, 0, 4096), tb(2), "sync", "mp"); dma(rowsof("S1", 3, 0, 4096), tb(3), "sync", "mp")
+    dma(rowsof("S1", 5, 0, 4096), rowsof("MPT", 8, 0, 4096), "sync", "mp"); dma(rowsof("S1", 6, 0, 4096), rowsof("MPT", 9, 0, 4096), "sync", "mp")
+    ts(c("r12"), c("r8"), 12.0, O.is_lt)
     act(A("CO", 224, 240), A("ONE", 0, 16), scale=0.5)
     scan(A("CO", 0, 16), A("CO", 224, 240), A("MAT", 128 * mn["Z"], 128 * mn["Z"] + 16), O.mult, O.add, 1.0); ts(A("CO", 16, 32), A("IO", 0, 16), c("r8"), O.is_equal)
     tt(A("CO", 48, 64), A("CO", 0, 16), A("CO", 16, 32), O.mult); red(c("pw"), A("CO", 48, 64), O.add)
-    act(c("p512"), c("p7"), scale=512.0); act(c("pb"), c("p512"), scale=c("pw"))
+    act(c("p512"), c("p7"), scale=512.0); act(c("pb"), c("p512"), bias=2.0 ** -13, scale=c("pw"))
     iota(A("TG", 0, 512), [[1, 512]], 0, 0); act(A("TF", 0, 512), A("TG", 0, 512), bias=c("pb"), scale=c("pw"))
-    act(A("TG", 0, 512), A("TF", 0, 512), bias=-0.5 + 2.0 ** -13); act(A("TG", 0, 512), A("TG", 0, 512), bias=12582912.0)
-    act(A("TG", 0, 512), A("TG", 0, 512), bias=-12582912.0); tt(A("TF", 0, 512), A("TF", 0, 512), A("TG", 0, 512), O.subtract)
-    act(A("BT", 0, 512), A("TF", 0, 512), bias=c("r12b"), scale=c("r12"), f=F.Sign)
+    act(A("TG", 0, 512), A("TF", 0, 512), bias=12582912.0); act(A("TG", 0, 512), A("TG", 0, 512), bias=-12582912.0)
+    tt(A("TF", 0, 512), A("TG", 0, 512), A("TF", 0, 512), O.subtract); act(A("BT", 0, 512), A("TF", 0, 512), scale=c("r12"), f=F.Sign)
     for k in range(8):
         dma(A("BITS", 0, 4096, p=(16 * k, 16 * k + 16)), A("BT", 0, 512), "sync", "bits")
-    dma(rowsof("BITS", 12, 0, 4096), tb(5), "sync", "bi2"); dma(rowsof("BITS", 13, 0, 4096), tb(6), "sync", "bi2")
+    dma(rowsof("BITS", 12, 0, 4096), tb(5), "sync", "bi2"); dma(rowsof("BITS", 13, 0, 4096), A("IL", 0, 256), "sync", "bi2")
     ts(ci(9), ci(2), float(r), O.add); ts(ci(9), ci(9), 7, O.bitwise_and); ts(c("g8"), ci(9), 8.0, O.mult)
     iota(A("JK", 0, 512), [[-1, 8], [1, 64]], 0, 0); ts(A("JK", 0, 512), A("JK", 0, 512), c("g8"), O.is_equal)
-    act(A("LP", 0, 512), A("JK", 0, 512), scale=dd(0)); act(A("LM", 0, 512), A("JK", 0, 512), scale=dd(5))
+    act(A("LP", 0, 512), A("JK", 0, 512), scale=dd(0)); act(A("LM", 0, 512), A("JK", 0, 512), scale=dd(8))
 
-    Qw, S1w, S2w, Bw, CTw = A("Q", 0, TW), A("S1", 0, TW), A("S2", 0, TW), A("BITS", 0, TW), A("CT", 0, 4096)
+    Qw, S1w, Bw, CTw = A("Q", 0, TW), A("S1", 0, TW), A("BITS", 0, TW), A("CT", 0, 4096)
     plan = routes(T, topo, r)
     narr = sum(bin(m if h is None else topo.mask(h, cc)).count("1") for s in range(8) for d, cc, h, m in routes(T, topo, s) if cc == core)
     nsnt = sum(bin(m).count("1") for d, cc, h, m in plan)
-    big = []
+    big = []; unit = [0, 0]
+    L = lambda n, h, k=0: A(n, 256 * k + 128 * h, 256 * k + 128 * h + 128)
+    W8 = lambda n, h: A(n, 8 * h, 8 * h + 8)
+    W16 = lambda n, h, k=0: A(n, k + 16 * h, k + 16 * h + 16)
+
+    def contest(hl, hm):
+        for k in range(8):
+            z = int(k >= ND[hl][hm]); bk = 2 * z + unit[z] % 2; jk = 384 * (unit[z] % 2); unit[z] += 1; pp = (32 * (k // 2), 32 * (k // 2) + 32)
+            lc, la = (A("BL", 256 * (z + k % 2) + 128 * hl, 256 * (z + k % 2) + 128 * hl + 128, p=pp) for z in (0, 2))
+            mm(grp(PS(bk, 0, 256), [(lc, A("R", 256 * hm, 256 * hm + 256, p=pp))]) + grp(PS(bk, 256, 384), [(la, A("R", 256 * hm, 256 * hm + 128, p=pp))]))
+            ml = A("ML", 16 * hl + 8 * hm + k, 16 * hl + 8 * hm + k + 1)
+            if k < ND[hl][hm]:
+                nmin(ml, PS(bk, 0, 384))
+            else:
+                act(A("JK", jk, jk + 384), PS(bk, 0, 384), bias=A("TH", 16 * hl + k, 16 * hl + k + 1), scale=-1.0, f=F.Relu, acc=ml)
+
+    def choose(h):
+        cw = W8("cw", h); bst = W16("KI", h, 64); Dd = W16("Di", h, 32); nd = ND[h]; k0 = 16 * h
+        ts(W16("KI", h, 96), A("SC", (6 + h) * KN + 15, (7 + h) * KN, KW), 831.0, O.add); ts(W16("KJ", h, 96), W16("KI", h, 96), 0xFFFC3F, O.bitwise_and)
+        tt(bst, W16("KI", h, 32), W16("KJ", h, 96), O.min); ts(W16("lo", h), bst, 63, O.bitwise_and)
+        tt(A("E", 256 * h, 256 * h + 256), IX(W16("lo", h), EL), A("MASK", 0, 256), O.mult)
+        mm(grp(PS(h, 312, 320), [(A("E", 256 * h, 256 * h + 128), G1), (A("E", 256 * h + 128, 256 * h + 256), G64)]))
+        tc(cw, PS(h, 312, 320)); tt(A("DX", 32 + k0, 48 + k0, 2), PS(h, 312, 320), A("BA", 16 + 8 * h, 24 + 8 * h), O.subtract)
+        ts(W16("Di", h), bst, 1.0 / 1024, O.mult); tt(Dd, W16("Di", h), W16("SAT", h), O.subtract)
+        ts(W16("DW", h), Dd, 0x7F00, O.bitwise_and); ts(W16("DW", h, 32), Dd, 255, O.bitwise_and); ts(W16("DW", h, 64), Dd, -2048.0, O.add)
+        tc(L("E2", h), IX(A("DW", 0, 104), A("UL", 32 + 8 * h, 40 + 8 * h)))
+        ts(W16("TH", h), Dd, 256.0, O.mult, c("tl%d" % h), O.add)
+        for hm in range(2):
+            if nd[hm]:
+                act(A("TH", 32 + k0 + 8 * hm, 32 + k0 + 8 * hm + nd[hm]), A("TH", k0, k0 + nd[hm]))
+        act(L("BB", h), IX(Bw, cw)); (act if SCA1 else tc)(L("S1c", h), IX(S1w, cw))
+        for k, n in enumerate(("even", "odd")):
+            act(L("BL", h, k), L("BB", h), bias=c("s2" + n), scale=c("s1" + n))
+        mm(sum((grp(PS(h, 128 * k, 128 * k + 128), [(I12, L("BB", h, k)), (L("E2", h), A("I16", 0, 128)), (M("MJ"), L("S1c", h))]) for k in range(2)), []))
+        Rh = A("R", 256 * h, 256 * h + 256); Rc = A("R", 256 * h, 256 * h + 128)
+        ts(Rh, PS(h, 0, 256), c("r1"), O.add, c("r2"), O.max)
+        mm(grp(PS(h, 328, 344), [(Rc, G15)])); tt(W16("TH", h, 64), PS(h, 328, 344), W16("TH", h, 32), O.subtract)
+        wrap(PS(h, 344, 352), "Wp", "S1c", 128 * h, 128 * h + 128); tt(A("DX", k0, 16 + k0, 2), PS(h, 344, 352), A("BA", 8 * h, 8 * h + 8), O.subtract)
+        act(L("vc", h), IX(Qw, cw))
+
+    def values(h, bk):
+        sc, sa, Rc = L("S1c", h), L("S1a", h), A("R", 256 * h, 256 * h + 128)
+        mm(grp(PS(bk, 0, 128), [(M("Mo"), sc)]) + grp(PS(bk, 128, 256), [(M("Mx"), sa), (M("Mk"), sc), (M("Md"), Rc)])
+           + grp(PS(bk, 256, 384), [(M("Mx"), sc), (M("Mk"), sa), (M("Md"), Rc)]))
+        act(L("VAL", h), PS(bk, 0, 128), bias=c("thb")); act(L("VAL", h, 1), PS(bk, 128, 256)); act(L("VAL", h, 2), PS(bk, 256, 384))
+
+    def stands(h):
+        tt(W16("st", h), W16("ML", h), W16("TH", h, 64), O.subtract); tt(A("st", 32 + 16 * h, 40 + 16 * h), A("st", 16 * h, 16 * h + 8), A("st", 16 * h + 8, 16 * h + 16), O.max)
+        sw = A("st", 32 + 16 * h, 40 + 16 * h)
+        tt(L("E", h), IX(sw, A("UL", 0, 8)), A("MNG", 0, 128), O.is_le); ts(A("Z", 128 * h + 4, 128 * h + 128, 8), IX(sw, L2), 0.0, O.is_le)
+
     for t in range(4):
-        aW = A("aW", 0, 16); L = lambda n, h: A(n, 128 * h, 128 * h + 128); W8 = lambda n, h: A(n, 8 * h, 8 * h + 8)
+        aW = A("aW", 0, 16)
         for h in range(2):
-            tc(L("y", h), IX(Qw, W8("aW", h)))
-        act(A("va", 0, 256), IX(Qw, aW))
-        for h in range(2):
-            mm([(PS(2 * h + k, q, 512, 8), M("PERM"), A("va", 128 * h + 64 * k, 128 * h + 64 * k + 64), True, True) for k in range(2) for q in range(8)])
-            act(L("AO", h), PS(2 * h, 0, 1024, 8), bias=c("off")); act(L("AB", h), PS(2 * h, 0, 1024, 8))
-        act(A("BB", 256, 512), IX(Bw, aW)); act(A("S1a", 0, 256), IX(S1w, aW))
-        mm(grp(PS(6, 0, 256), [(M("BDi"), A("BB", 256, 512) if t else A("no", 0, 256))])); act(A("aR", 0, 256), PS(6, 0, 256))
-        mm(grp(PS(7, 0, 16), [(L("va", 0), GG), (L("dR", 0), GD)]) + grp(PS(7, 16, 32), [(L("va", 1), GG), (L("dR", 1), GD)])); act(A("SAT", 0, 32), PS(7, 0, 32))
-        act(A("BL", 256, 512), IX(Bw, aW), bias=c("s2"), scale=c("s1"))
+            act(L("va", h), IX(Qw, W8("aW", h)))
+            if not MIX:
+                tc(L("y", h), IX(Qw, W8("aW", h)))
+            for e in range(2):
+                act(A("AT", 512 * h + e, 512 * h + 256, 2), L("va", h))
+            mm(sum((grp(PS(2 + h, 128 * k, 128 * k + 128), [(A("AT", 512 * h + 128 * k, 512 * h + 128 * k + 128), M("PERM"))]) for k in range(2)), []))
+            act(A("AT", 512 * h + 256, 512 * h + 512), PS(2 + h, 0, 256))
+            for k in range(2):
+                b0 = 2048 * h + 1024 * k
+                trs([(A("PB", b0 + 2 * q, b0 + 1024, 16), A("AT", 512 * h + 256 + 128 * k, 512 * h + 384 + 128 * k), Ib) for q in range(8)])
+            mm(grp(PS(2 + h, 128, 256), [(M("PERM"), L("va", h))])); act(L("AO", h), PS(2 + h, 128, 256), bias=c("off")); act(L("AB", h), PS(2 + h, 128, 256))
+        act(A("BB", 256, 512), IX(Bw, aW))
+        mm(grp(PS(2, 256, 512), [(M("BDi"), A("BB", 256, 512) if t else A("no", 0, 256))])); act(A("aR", 0, 256), PS(2, 256, 512))
+        mm(grp(PS(3, 256, 272), [(L("va", 0), GG), (L("IND", 0), GD)]) + grp(PS(3, 272, 288), [(L("va", 1), GG), (L("IND", 1), GD)])); act(A("SAT", 0, 32), PS(3, 256, 288))
+        act(A("S1a", 0, 256), IX(S1w, aW)); act(A("va", 256, 512), A("va", 0, 256), scale=-1.0)
+        if SAS:
+            act(A("S1f", 0, 256), A("S1a", 0, 256), bias=128.0)
+        for k, n in enumerate(("even", "odd")):
+            act(A("BL", 512 + 256 * k, 768 + 256 * k), A("BB", 256, 512), bias=c("s2" + n), scale=c("s1" + n))
         for hop in range(4):
             for h in range(2):
-                Xn, Mn = "X%d" % h, "M%d" % h; uo = W8("uo", h); kb = 4 + h; K = PS(kb, 0, 256)
-                wrap(PS(kb, 256, 264), "Ww" if hop else "Wv", "y", 128 * h, 128 * h + 128)
+                Xn, Mn = "X%d" % h, "M%d" % h; uo = W8("uo", h); K = PS(h, 0, KN)
+                wrap(PS(h, 304, 312), "Ww" if hop else "Wv", "y" if hop or not MIX else "va", 128 * h, 128 * h + 128)
+                SUB = SUBS.get((hop, h), SUBS[None])
                 u0, u1 = A("ui", 16 * h, 16 * h + 8), A("ui", 16 * h + 8, 16 * h + 16)
-                ts(u0, PS(kb, 256, 264), c("cw") if hop else 0.0, O.add); ts(u1, u0, 4095, O.bitwise_and); tc(uo, u1)
+                ts(u0, PS(h, 304, 312), c("cw") if hop else 0.0, O.add); ts(u1, u0, 4095, O.bitwise_and); tc(uo, u1)
                 tc(L("co", h), IX(CTw, uo))
-                for a, b in SUB:
-                    big = [act(A(Xn, 16 * a, 16 * b), IX(Qw, A("co", 128 * h + a, 128 * h + b)), after=big)]
-                tt(L("eq", h), IX(CTw, uo), L("aR", h), O.is_equal)
-                act(L("cF", h), IX(CTw, uo), bias=8385.0); act(L("hB", h), IX(CTw, uo), bias=129.0 - 31.5 / 64, scale=1.0 / 64)
-                mm([(K, L("eq", h), A("PI2", 0, 256), True, False), (PS(kb, 0, 128), L("cF", h), A("I32", 0, 128), False, False),
-                    (K, L("hB", h), A("HI2", 0, 256), False, False)])
-                for a, b in SUB:
-                    for q in range(2):
-                        tt(A(Mn, 16 * a + q, 16 * b, 2, reg=Mn + str(q)), A(Xn, 16 * a + q, 16 * b, 2), PS(2 * h, 8 * a, 8 * b), O.max)
-                mm([(PS(kb, i, 256, 16), A(Xn, i, 2048, 16), GN, False, False) for i in range(16)])
-                for q in range(2):
-                    mm([(PS(kb, i, 256, 16), A(Mn, i, 2048, 16, reg=Mn + str(q)), GP, False, i == 15) for i in range(q, 16, 2)])
-                sc = A("SC", 256 * h, 256 * h + 256); scan(sc, A("RK", 0, 256), K, O.add, O.min)
-                ki = A("KI", 32 * hop + 16 * h, 32 * hop + 16 * h + 16)
-                ts(ki, A("SC", 256 * h + 15, 256 * h + 256, 16), 831.0, O.add)
-                if hop < 3:
-                    lo = A("lo", 16 * h, 16 * h + 16); e = A("E", 256 * h, 256 * h + 256)
-                    ts(lo, ki, 63, O.bitwise_and); tt(e, IX(lo, EL), A("MASK", 0, 256), O.mult)
-                    mm(grp(PS(kb, 264, 272), [(A("E", 256 * h, 256 * h + 128), G1), (A("E", 256 * h + 128, 256 * h + 256), G64)]))
-                    tc(W8("cw", h), PS(kb, 264, 272)); tc(L("mg", h), IX(S1w, W8("cw", h)))
-                    wrap(PS(kb, 272, 280), "Wmp", "mg", 128 * h, 128 * h + 128); tc(W8("mo", h), PS(kb, 272, 280))
-                    tt(L("y", h), IX(Qw, W8("mo", h)), L("AO", h), O.add)
-        ts(A("KJ", 0, 96), A("KI", 0, 96), 0xFFFC3F, O.bitwise_and); tt(A("KJ", 0, 96), A("KJ", 0, 96), HC, O.add)
-        tt(A("KI", 0, 32), A("KJ", 0, 32), A("KJ", 32, 64), O.min); tt(A("KI", 32, 64), A("KI", 0, 32), A("KJ", 64, 96), O.min)
-        ts(A("KJ", 96, 128), A("KI", 96, 128), 0xFFFC3F, O.bitwise_and); tt(A("KI", 64, 96), A("KI", 32, 64), A("KJ", 96, 128), O.min)
-        ts(A("lo", 0, 32), A("KI", 64, 96), 63, O.bitwise_and); cw = A("cw", 0, 16)
-        for h in range(2):
-            tt(A("E", 256 * h, 256 * h + 256), IX(A("lo", 16 * h, 16 * h + 16), EL), A("MASK", 0, 256), O.mult)
-        mm(sum((grp(PS(4, 8 * h, 8 * h + 8), [(A("E", 256 * h, 256 * h + 128), G1), (A("E", 256 * h + 128, 256 * h + 256), G64)]) for h in range(2)), []))
-        tc(cw, PS(4, 0, 16)); tt(A("DF", 32, 48), PS(4, 0, 16), DU2, O.subtract)
-        Dd = A("Di", 32, 64); npr = A("DW", 64, 96)
-        ts(A("KI", 0, 32), A("KI", 64, 96), 192.0, O.add); ts(A("Di", 0, 32), A("KI", 0, 32), 10, O.arith_shift_right); tt(Dd, A("Di", 0, 32), A("SAT", 0, 32), O.subtract)
-        ts(A("DW", 0, 32), Dd, 0x7FC0, O.bitwise_and); ts(A("DW", 32, 64), Dd, 63, O.bitwise_and)
-        ts(A("TH", 0, 32), Dd, 256.0, O.mult); tt(A("TH", 0, 32), A("TH", 0, 32), TL, O.add)
-        tc(A("S1c", 0, 256), IX(S1w, cw)); act(A("BB", 0, 256), IX(Bw, cw)); act(A("BL", 0, 256), IX(Bw, cw), bias=c("s2"), scale=c("s1"))
-        mm(grp(PS(5, 0, 16), [(L("S1c", 0), GJ)]) + grp(PS(5, 16, 32), [(L("S1c", 1), GJ)])); tt(npr, Dd, PS(5, 0, 32), O.is_ge)
-        tc(A("E2", 0, 256), IX(A("DW", 0, 104), E2L))
-        ts(A("st", 0, 32), npr, 16777216.0, O.mult); tt(A("TH", 0, 32), A("TH", 0, 32), A("st", 0, 32), O.add)
-        wrap(PS(3, 32, 48), "Wp", "S1c", 0, 256); tt(A("DF", 0, 16), PS(3, 32, 48), DU1, O.subtract)
-        for k in range(2):
-            mm([(PS(6 + k, 0, 256), I12, A("BB", 256 * k, 256 * k + 256), True, False)] + [(PS(6 + k, 128 * h, 128 * h + 128), L("E2", h), Ib, False, h == 1) for h in range(2)])
-        ts(A("RE", 0, 256), PS(6, 0, 256), c("even"), O.mult); act(A("RO", 256, 512), PS(7, 0, 256), scale=c("odd"))
-        ts(A("RE", 256, 512), PS(7, 0, 256), c("even"), O.mult); act(A("RO", 0, 256), PS(6, 0, 256), scale=c("odd"))
-        act(A("vc", 0, 256), IX(Qw, cw)); act(A("S2c", 0, 256), IX(S2w, cw))
-        u = 0
-        for h in range(2):
-            for a in range(4):
-                for par in range(2):
-                    bk = 2 * (u % 4); jk = 768 * (u // 2 % 2); u += 1; R = "RO" if par else "RE"; pp = (32 * a, 32 * a + 32); k = 16 * h + 2 * a + par
-                    mm(grp(PS(bk, 0, 512), [(A("BL", 128 * h, 128 * h + 128, p=pp), A(R, 0, 512, p=pp))])
-                       + grp(PS(bk + 1, 0, 256), [(A("BL", 256 + 128 * h, 384 + 128 * h, p=pp), A(R, 0, 256, p=pp))]))
-                    if (u * NACT) // 16 != ((u - 1) * NACT) // 16:
-                        act(A("JK", jk, jk + 768), PS(bk, 0, 768), bias=A("TH", k, k + 1), scale=-1.0, f=F.Relu, acc=A("LS", k, k + 1))
+                for a, b, q in SUB:
+                    if q:
+                        tc(A(Xn, 16 * a, 16 * b), IX(Qw, A("co", 128 * h + a, 128 * h + b)))
                     else:
-                        red(A("MN", k, k + 1), PS(bk, 0, 768), O.min)
-        mm(grp(PS(0, 0, 256), [(M("MI"), A("S1c", 0, 256)), (M("Mup"), A("S1c", 0, 256))]))
-        mm(grp(PS(0, 256, 512), [(M("Mdn"), A("S1c", 0, 256)), (M("Mk"), A("S1a", 0, 256)), (M("M56"), A("S2c", 0, 256)), (M("Md"), A("RE", 0, 256)), (M("Md"), A("RO", 0, 256))]))
-        mm(grp(PS(1, 0, 256), [(M("Mdn"), A("S1a", 0, 256)), (M("M56"), A("S1a", 0, 256)), (M("Mk"), A("S1c", 0, 256)), (M("Md"), A("RE", 0, 256)), (M("Md"), A("RO", 0, 256))]))
-        act(A("VAL", 0, 256), PS(0, 0, 256), bias=c("thb")); act(A("VAL", 256, 768), PS(0, 256, 768))
-        tt(A("st", 0, 32), A("TH", 0, 32), A("MN", 0, 32), O.subtract); tt(A("st", 32, 64), A("st", 0, 32), A("LS", 0, 32), O.max)
-        tt(A("E", 0, 256), IX(A("st", 32, 64), EH), A("MNG", 0, 256), O.is_le)
-        mm([(PS(4, 16 * k + 8 * h, 16 * k + 8 * h + 8), L("E", h), G1, True, True) for k in range(3) for h in range(2)])
-        tt(A("OT", 0, 48), PS(4, 0, 48), A("DF", 0, 48), O.mult); tt(A("OT", 64, 112), A("OT", 0, 48), A("BA", 0, 48), O.add); tc(A("OF", 0, 48), A("OT", 64, 112))
-        tc(IX(S1w, A("OF", 0, 16)), A("VAL", 0, 256)); tc(IX(S1w, A("OF", 16, 48)), A("VAL", 256, 768))
-        tc(A("no", 0, 256), IX(S1w, aW)); scan(A("no", 256, 512), A("CS", 0, 256), A("no", 0, 256), O.mult, O.add)
-        wrap(PS(5, 0, 16), "Wg", "no", 256, 512)
-        tt(A("OT", 0, 16), PS(5, 0, 16), L257, O.max); ts(A("po", 0, 16), A("OT", 0, 16), -257.0, O.add)
+                        big = [act(A(Xn, 16 * a, 16 * b), IX(Qw, A("co", 128 * h + a, 128 * h + b)), after=big)]
+                tt(L("eq", h), IX(CTw, uo), L("aR", h), O.is_equal)
+                act(L("cF", h), IX(CTw, uo), bias=8385.0); act(L("hB", h), L("cF", h), bias=129.0 - (8385 + 31.5) / 64, scale=1.0 / 64)
+                mm([(K, L("eq", h), A("PI2", 0, KN), True, False), (PS(h, 0, KN // 2), L("cF", h), A("I32", 0, KN // 2), False, False),
+                    (K, L("hB", h), A("HI2", 0, KN), False, False)])
+                for a, b, q in SUB:
+                    tt(A(Mn, 16 * a, 16 * b), A(Xn, 16 * a, 16 * b), A("PB", 2048 * h + 16 * a, 2048 * h + 16 * b), O.max)
+                for nm, a, b in SUM:
+                    for i0 in range(0, 16, PCS):
+                        mm([(PS(h, i, KN, KW, p=(a, b)), A(nm + str(h), 16 * a + i, 16 * b, 16), GN if nm == "X" else GP, False, nm == "M" and i == 15) for i in range(i0, i0 + PCS)])
+                s0 = (2 * hop + h) * KN; scan(A("SC", s0, s0 + KN), A("RK", 0, KN), K, O.add, O.min)
+                if hop < 3:
+                    lo = W16("lof", h); e = A("E", 256 * h, 256 * h + 256)
+                    tt(lo, A("SC", s0 + 16, s0 + KN, KW), A("SC", s0 + 18, s0 + KN, KW), O.subtract); tt(e, IX(lo, EL), A("MASK", 0, 256), O.mult)
+                    mm(grp(PS(h, 312, 320), [(A("E", 256 * h, 256 * h + 128), G1), (A("E", 256 * h + 128, 256 * h + 256), G64)]))
+                    ts(W8("cw", h), PS(h, 312, 320), 2047.5, O.add); (act if MGA else tc)(L("mg", h), IX(S1w, W8("cw", h)))
+                    wrap(PS(h, 320, 328), "Wmp", "mg", 128 * h, 128 * h + 128); tc(W8("mo", h), PS(h, 320, 328))
+                    tt(L("y", h), IX(Qw, W8("mo", h)), L("AO", h), O.add)
+                else:
+                    choose(h)
+                    if h == 0:
+                        contest(0, 0)
+            if hop == 2:
+                ts(A("KI", 0, 96), A("SC", 15, 6 * KN, KW), 831.0, O.add)
+                ts(A("KJ", 0, 96), A("KI", 0, 96), 0xFFFC3F, O.bitwise_and); tt(A("KJ", 0, 96), A("KJ", 0, 96), HC, O.add)
+                tt(A("KI", 0, 32), A("KJ", 0, 32), A("KJ", 32, 64), O.min); tt(A("KI", 32, 64), A("KI", 0, 32), A("KJ", 64, 96), O.min)
+        contest(1, 0); contest(0, 1); stands(0); contest(1, 1); values(0, 2); values(1, 3); stands(1)
+        mm([(PS(1, 32 * k + 16 * h, 32 * k + 16 * h + 16), L("E", h), G1x, True, True) for k in range(3) for h in range(2)])
+        scan(A("OT", 0, 96), PS(1, 0, 96), A("DX", 0, 96), O.mult, O.add); tc(A("OF", 0, 48), A("OT", 1, 96, 2))
+        tc(IX(S1w, A("OF", 0, 16)), A("VAL", 0, 256)); tc(IX(S1w, A("OF", 16, 32)), A("VAL", 256, 512))
+        (act if NOA else tc)(A("no", 0, 256), IX(S1w, aW)); tc(IX(S1w, A("OF", 32, 48)), A("VAL", 512, 768))
+        mm([(PS(0, 256, 512), M("Msel"), A("no", 0, 256), True, False)] + [(PS(0, 256 + 128 * h, 384 + 128 * h), L("Z", h), M("In"), False, h == 1) for h in range(2)])
+        scan(A("no", 256, 512), A("CS", 0, 256), PS(0, 256, 512), O.mult, O.add)
+        wrap(PS(0, 0, 16), "Wg", "no", 256, 512)
+        tt(A("OT", 96, 112), PS(0, 0, 16), L257, O.max); ts(A("po", 0, 16), A("OT", 96, 112), -257.0, O.add)
         b0 = 512 * t
-        tc(IX(A("SB", b0, b0 + 512), A("po", 0, 16)), A("va", 0, 256))
+        tc(IX(A("SB", b0, b0 + 512), A("po", 0, 16)), A("va", 256, 512))
 
         def send(e, t=t, b0=b0):
             trs = []
@@ -435,43 +521,52 @@ def rank_program(g, core, T, topo):
                                              src=T.SB[:, b0 + 240 + 16 * d:b0 + 256 + 16 * d], dst=T.RB[:, k:k + 16] if h is None else T.HB[:, 16 * t:16 * t + 16]))
             e.remote_dma_fused(trs, local_sem=T.sem.snt)
         snd = op("pool", send, [], [A("SB", b0 + 256, b0 + 368)], 0.5, WAY, "rem")
-        tc(IX(A("SA", b0, b0 + 512), A("po", 0, 16)), A("no", 0, 256)); ms(A("SA", b0 + 368, b0 + 384), 0.0)
+        sa = A("SP", 0, 112)
+        if SAS:
+            silu(IX(A("SA", b0, b0 + 512), A("po", 0, 16)), A("S1f", 0, 256)); act(A("TF", 0, 112), A("SA", b0 + 256, b0 + 368), bias=12582912.0)
+            act(A("SP", 112, 224), A("TF", 0, 112), bias=c("b5"), scale=dd(5)); act(A("SP", 224, 336), A("TF", 0, 112), bias=c("b12"), scale=dd(12))
+            act(sa, A("TF", 0, 112), bias=-12582912.0 - 128)
+        mm(grp(PS(0, 16, 17), [(M("BD4"), A("no", 511, 512))])); ts(A("P6", 0, 30), A("CO", 64, 94), PS(0, 16, 17), O.is_lt)
         mm(grp(PS(1, 256, 512), [(Ib, A("AB", 0, 256)), (M("In"), A("vc", 0, 256))])); act(A("dn", 0, 256), PS(1, 256, 512), f=F.Sign)
-        mm(grp(PS(0, 0, 256), [(Ib, A("va", 0, 256)), (M("PERMn"), A("dn", 0, 256))]) + grp(PS(0, 256, 512), [(Ib, A("vc", 0, 256)), (Ib, A("dn", 0, 256))]))
-        act(A("QV", 0, 512), PS(0, 0, 512))
-        tc(IX(Qw, A("OF", 16, 32)), A("QV", 0, 256), after=[snd - 1]); tc(IX(Qw, A("OF", 32, 48)), A("QV", 256, 512), after=[snd - 1])
+        mm(grp(PS(1, 0, 256), [(Ib, A("va", 0, 256)), (M("PERMn"), A("dn", 0, 256))]) + grp(PS(1, 256, 512), [(Ib, A("vc", 0, 256)), (Ib, A("dn", 0, 256))]))
+        act(A("QV", 0, 512), PS(1, 0, 512))
+        tc(IX(Qw, A("OF", 32, 48)), A("QV", 0, 256), after=[snd - 1][:QAF]); tc(IX(Qw, A("OF", 16, 32)), A("QV", 256, 512), after=[snd - 1][:QAF])
         if t < 3:
             lanes(t + 1)
         else:
-            mm(grp(PS(0, 0, 512, p=(0, 64)), [(A("LP", 64 * k, 64 * k + 64), A("S1", 512 * k, 512 * k + 512)) for k in range(8)]))
-            act(A("YO", 0, 512, p=(0, 64)), PS(0, 0, 512, p=(0, 64))); dma(X(T.yp[:]), A("YO", 0, 512, p=(0, 64)), "act")
-        s0 = b0 + 256
-        for k, (W, od) in enumerate((("Wix", False), ("Wmp", False), ("Wf", False), ("Wf", True))):
-            wrap(PS(3, 8 * k, 8 * k + 8), W, "SA", s0, s0 + 128, od)
-        p6 = lambda a, b: A("P6", a, b)
-        tt(p6(0, 16), PS(3, 0, 16), DB, O.subtract); tc(p6(16, 24), PS(3, 24, 32)); tt(p6(32, 40), p6(0, 8), PS(3, 16, 24), O.mult)
-        act(p6(40, 48), p6(16, 24), scale=c("pd")); tt(p6(48, 56), p6(8, 16), p6(16, 24), O.mult); tt(p6(56, 64), p6(0, 8), p6(16, 24), O.mult)
-        tt(p6(64, 96), p6(32, 64), OB, O.add); tc(A("O2", 0, 32), p6(64, 96))
-        mm([(PS(2, 128 * k + e, 128 * k + 128, 2), M("M56" if k == 1 else "M7"), A("SA", s0 + 1 - e, s0 + 128, 2), True, True) for k in range(3) for e in range(2)])
-        act(A("V2", 0, 384), PS(2, 0, 384)); tc(IX(S2w, A("O2", 16, 32)), A("V2", 0, 256))
-        g6 = lambda k, a=0, s=1: A("G6", 128 * k + a, 128 * k + 128, s)
+            for k in range(8):
+                mm([(PS(2, 0, 512, p=(0, 64)), A("LP", 64 * k, 64 * k + 64), A("S1", 512 * k, 512 * k + 512), k == 0, k == 7)])
+            act(A("YO", 0, 512, p=(0, 64)), PS(2, 0, 512, p=(0, 64))); dma(X(T.yp[:]), A("YO", 0, 512, p=(0, 64)), "act")
+        s0 = b0 + 256; p6 = lambda a, b: A("P6", a, b); sp = lambda x: A("SP", x, 112, 16)
+        spare = lambda o, a, b: [(o, M("N4096"), A("ONE", a, b), True, False), (o, M("In"), A("LB", a, b), False, False)]
+        act(p6(40, 47), p6(16, 23), scale=c("pd"))
+        mm(spare(PS(1, 384, 398), 0, 14) + [(PS(1, 384, 398), W("WB", x), A("SP", 112 + x, 336, 16), False, x == 15) for x in range(16)])
+        tt(p6(32, 39), PS(1, 391, 398), p6(0, 7), O.mult); tt(p6(48, 62), PS(1, 384, 398), p6(16, 30), O.mult)
+        tt(p6(64, 94), p6(32, 62), OB, O.add); tc(A("O2", 0, 30), p6(64, 94))
+        g6 = lambda k, a=0, s=1: A("G6", 128 * k + a, 128 * k + 112, s); om = A("O2", 16, 23)
+        pair = lambda k, m, s0, s1: [(PS(1, 112 * k + e, 112 * k + 112, 2), M(m), A("SP", 1 - e, 112, 2), s0 and e == 0, s1 and e == 1) for e in range(2)]
         if t < 3:
-            act(g6(0), IX(S1w, A("O2", 16, 24))); wrap(PS(3, 32, 40), "Wp", "G6", 0, 128)
-            tt(p6(24, 32), PS(3, 32, 40), A("CO", 136, 144), O.subtract); tt(p6(24, 32), p6(24, 32), p6(16, 24), O.mult)
-            tt(p6(24, 32), p6(24, 32), A("CO", 136, 144), O.add); tc(A("O2", 32, 40), p6(24, 32))
-            act(A("G6", 128, 384), IX(S1w, A("O2", 24, 40)), scale=c("keep")); tt(IX(S1w, A("O2", 24, 40)), A("G6", 128, 384), A("V2", 128, 384), O.add)
-            act(g6(3), IX(Qw, A("O2", 16, 24))); act(g6(4), g6(3), scale=c("lo"))
+            act(g6(0), IX(S1w, om))
+            mm(pair(2, "M7", True, True) + [(PS(1, 112, 224), M("Kx"), sa, True, False)] + pair(1, "Mz", False, False) + pair(0, "M4", False, False))
+            mm([(PS(1, 0, 112), M("K89"), g6(0), False, True)])
+            act(A("V2", 0, 336), PS(1, 0, 336)); tc(IX(S1w, A("O2", 16, 30)), A("V2", 0, 224))
+            mm(spare(PS(0, 64, 71), 7, 14) + [(PS(0, 64, 71), W("Wp", x), A("G6", x, 112, 16), False, x == 15) for x in range(16)])
+            tt(p6(8, 15), PS(0, 64, 71), p6(16, 23), O.mult); tt(p6(8, 15), p6(8, 15), A("CO", 96, 103), O.add); tc(A("O2", 32, 39), p6(8, 15))
+            act(g6(1), IX(S1w, A("O2", 32, 39)), scale=c("keep")); tt(IX(S1w, A("O2", 32, 39)), g6(1), A("V2", 224, 336), O.add)
+            act(g6(3), IX(Qw, om)); act(g6(4), g6(3), scale=c("lo"))
             act(g6(5, 0, 2), g6(3, 1, 2), scale=c("hi")); act(g6(5, 1, 2), g6(3, 0, 2), scale=c("hi"))
-            tt(IX(Qw, A("O2", 16, 24)), g6(4), g6(5), O.add)
+            tt(IX(Qw, om), g6(4), g6(5), O.add)
         else:
-            mm(grp(PS(1, 0, 256, p=(0, 64)), [(A("LM", 64 * k, 64 * k + 64), A("S2", 256 * k, 256 * k + 256)) for k in range(8)]))
-            act(A("YO", 512, 768, p=(0, 64)), PS(1, 0, 256, p=(0, 64))); dma(X(T.ym[:]), A("YO", 512, 768, p=(0, 64)), "act")
-        r6 = lambda k: A("R6", 128 * k, 128 * k + 112); pm = A("O2", 8, 15); rb = A("RB", 112 * t, 112 * t + 112)
-        act(r6(0), IX(A("SB", s0, s0 + 128), pm), bias=1.0, scale=c("hi")); act(r6(1), A("SB", s0, s0 + 112), scale=c("lo")); tt(r6(0), r6(0), r6(1), O.add)
-        ex = ("arr%d" % t, narr)
-        ts(r6(2), IX(rb, pm), c("hi"), O.mult, c("nlo"), O.add, ext=ex, after=[snd]); act(r6(3), rb, bias=c("nhi"), scale=c("lo"), ext=ex, after=[snd])
-        tt(r6(4), r6(2), r6(3), O.max); ts(r6(5), r6(4), 0.0, O.is_lt); tt(r6(5), r6(5), r6(0), O.mult)
-        tt(IX(Qw, A("O2", 0, 7)), r6(4), r6(5), O.add)
+            mm(pair(1, "Mz", True, False) + pair(0, "M4", False, True))
+            act(A("V2", 0, 224), PS(1, 0, 224)); tc(IX(S1w, A("O2", 16, 30)), A("V2", 0, 224))
+            for k in range(8):
+                mm([(PS(3, 0, 256, p=(0, 64)), A("LM", 64 * k, 64 * k + 64), A("S1", 256 * k, 256 * k + 256), k == 0, k == 7)])
+            act(A("YO", 512, 768, p=(0, 64)), PS(3, 0, 256, p=(0, 64))); dma(X(T.ym[:]), A("YO", 512, 768, p=(0, 64)), "act")
+        r6 = lambda k: A("R6", 128 * k, 128 * k + 112)
+        act(r6(0), A("SB", s0, s0 + 112), scale=-1.0)
+        tt(r6(1), A("RB", 112 * t, 112 * t + 112), r6(0), O.min, ext=("arr%d" % t, narr), after=[snd])
+        act(r6(2), IX(r6(1), A("O2", 8, 15)), scale=c("hi"), f=F.Abs); act(r6(3), r6(1), scale=c("lo"), f=F.Abs)
+        tt(IX(Qw, A("O2", 0, 7)), r6(2), r6(3), O.add)
     for k in range(len(cut) - 1):
         a, b = cut[k], cut[k + 1]; ra = (a + 16 * r) % 128
         dma(X(T.yq[ra:ra + b - a, :]), A("Q", 0, 2048, p=(a, b)), "act" if k % 2 else "sync", None, 3.5)
@@ -505,19 +600,96 @@ def emit(g, T, ops, nsnt, r):
                 if not left[k]:
                     cand[ops[k]["q"]].append(k)
         return max(fin[i] + ops[i]["lat"] for i in range(n)), order, fin
-    best = None; rng = np.random.default_rng(r)
-    for it in range(ITER):
-        f = place(pre, post, pri, [0.0] * n)
-        if best is None or f[0] < best[0]:
-            best = f
-        pri = place(post, pre, (f if it % 4 < 3 else best)[2], [o["lat"] for o in ops])[2]
-        if it % 4 == 3:
-            pri = [p + NOISE * float(z) for p, z in zip(pri, rng.random(n))]
-    order, fin = best[1], best[2]
-    INFO[r] = (best[0], {q: sum(o["cost"] for o in ops if o["q"] == q) for q in qs}, n,
-               [(ops[i]["q"], i, fin[i] - ops[i]["cost"], fin[i]) for i in order])
+
+    cost = [o["cost"] for o in ops]; lat = [o["lat"] for o in ops]
+
+    def times(prv, nxt):
+        left = [len(pre[i]) + (prv[i] >= 0) for i in range(n)]; st = [0.0] * n; order = [i for i in range(n) if not left[i]]
+        for i in order:
+            f = st[i] + cost[i]
+            for k, w in post[i]:
+                if st[k] < f + w:
+                    st[k] = f + w
+                left[k] -= 1
+                if not left[k]:
+                    order.append(k)
+            k = nxt[i]
+            if k >= 0:
+                if st[k] < f:
+                    st[k] = f
+                left[k] -= 1
+                if not left[k]:
+                    order.append(k)
+        tl = [0.0] * n
+        for i in reversed(order):
+            z = lat[i]
+            for k, w in post[i]:
+                if z < tl[k] + w:
+                    z = tl[k] + w
+            k = nxt[i]
+            if k >= 0 and z < tl[k]:
+                z = tl[k]
+            tl[i] = z + cost[i]
+        return max(tl) if len(order) == n else 1e9, st, tl
+
+    def improve(order, rng):
+        prv = [-1] * n; nxt = [-1] * n; end = {}
+        for i in order:
+            q = ops[i]["q"]
+            if q in end:
+                prv[i] = end[q]; nxt[end[q]] = i
+            end[q] = i
+        best = None; tabu = {}
+        for it in range(SWAPS):
+            T0, st, tl = times(prv, nxt)
+            if best is None or T0 < best[0] - 1e-9:
+                best = (T0, list(prv), list(nxt), st)
+            elif T0 > best[0] + DRIFT:
+                prv, nxt = list(best[1]), list(best[2]); continue
+            pick = {}
+            for u in range(n):
+                v = nxt[u]
+                if v >= 0 and st[u] + cost[u] + tl[v] > T0 - NEAR and st[v] < st[u] + cost[u] + 1e-9 and u not in ops[v]["deps"] and tabu.get((v, u), -1) < it:
+                    a = prv[u]; b = nxt[v]
+                    rv = max([st[j] + cost[j] + w for j, w in pre[v]] + [st[a] + cost[a] if a >= 0 else 0.0])
+                    if rv >= st[u] + cost[u] - 1e-9:
+                        continue
+                    ru = max([st[j] + cost[j] + w for j, w in pre[u]] + [rv + cost[v]])
+                    qu = cost[u] + max([tl[k] + w for k, w in post[u]] + [lat[u], tl[b] if b >= 0 else 0.0])
+                    qv = cost[v] + max([tl[k] + w for k, w in post[v]] + [lat[v], qu])
+                    e = max(rv + qv, ru + qu) - T0; z = max(e, 0.0) * GREED + float(rng.random()); w = int(st[u] / APART + it % 2 * 0.5)
+                    if w not in pick or z < pick[w][3]:
+                        pick[w] = (e, u, v, z)
+            for w, (e, u, v, z) in pick.items():
+                if w % 2 == it // 2 % 2 and e < TEMP * (1 - it / SWAPS) * float(rng.exponential()) + 1e-6:
+                    a = prv[u]; b = nxt[v]; tabu[(u, v)] = it + TABU
+                    if a >= 0:
+                        nxt[a] = v
+                    if b >= 0:
+                        prv[b] = u
+                    prv[v] = a; nxt[v] = u; prv[u] = v; nxt[u] = b
+        st = best[3]; rank = {}; left = [len(pre[i]) + (best[1][i] >= 0) for i in range(n)]; todo = [i for i in range(n) if not left[i]]
+        for i in todo:
+            rank[i] = len(rank)
+            for k in [k for k, w in post[i]] + [best[2][i]] * (best[2][i] >= 0):
+                left[k] -= 1
+                if not left[k]:
+                    todo.append(k)
+        return best[0], todo, [st[i] + cost[i] for i in range(n)]
+    if n not in PLAN:
+        best = None; rng = np.random.default_rng(1)
+        for it in range(ITER):
+            f = place(pre, post, pri, [0.0] * n)
+            if best is None or f[0] < best[0]:
+                best = f
+            pri = place(post, pre, (f if it % 4 < 3 else best)[2], lat)[2]
+            if it % 4 == 3:
+                pri = [p + NOISE * float(z) for p, z in zip(pri, rng.random(n))]
+        PLAN[n] = improve(best[1], rng) if SWAPS else best
+    best = PLAN[n]; order, fin = best[1], best[2]
+    INFO[r] = (best[0], {q: sum(o["cost"] for o in ops if o["q"] == q) for q in qs}, n)
     eng = dict(pe=g.tensor, dve=g.vector, act=g.scalar, pool=g, sync=g.sync)
-    sig = {}; cnt = {q: 0 for q in qs}; seen = {q: {} for q in qs}; nd = 0; last = {}
+    sig = {}; cnt = {q: 0 for q in qs}; seen = {q: {} for q in qs}; nd = 0; last = {}; knew = {}; waited = {}
     for i in order:
         o = ops[i]; q = o["q"]; e = eng[q]; need = {}
         for j, sm in o["deps"].items():
@@ -527,15 +699,19 @@ def emit(g, T, ops, nsnt, r):
             need[o["ext"][0]] = o["ext"][1]
         if q == "pool" and cnt[q]:
             need[q] = cnt[q]
-        for s, v in need.items():
+        for s, v in sorted(need.items(), key=lambda z: -knew.get(z, (0,))[0]):
             if seen[q].get(s, 0) < v:
-                e.wait_ge(T.sem[s], v); seen[q][s] = v
+                e.wait_ge(T.sem[s], v); seen[q][s] = v; waited[s] = max(waited.get(s, 0), v)
+                for s2, v2 in (knew.get((s, v), (0, {}))[1].items() if TRANS else ()):
+                    seen[q][s2] = max(seen[q].get(s2, 0), v2)
         ins = o["fn"](e)
         if o["kind"] == "dma":
             sig[i] = ("d%d" % nd, 16); nd += 1; ins.then_inc(T.sem[sig[i][0]], 16); last[sig[i][0]] = 16
         elif o["kind"] == "c" and (q == "pool" or any(ops[k]["deps"][i] for k in use[i])):
             cnt[q] += 1; sig[i] = (q, cnt[q]); ins.then_inc(T.sem[q], 1); last[q] = cnt[q]
+        if i in sig:
+            knew[sig[i]] = (fin[i] + o["lat"], dict(seen[q]))
     for s, v in last.items():
-        if max(seen[q].get(s, 0) for q in qs) < v:
+        if waited.get(s, 0) < v:
             g.sync.wait_ge(T.sem[s], v)
     g.wait_ge(T.sem.snt, nsnt)

import numpy as np
from concourse.bass import DstId, RemoteDMATransfer
from concourse.mybir import AluOpType as O, AxisListType, ActivationFunctionType as F

TW, D1, D2, DUM = 4624, 4096, 4352, 4608
KW, KN = 19, 304
B, H16, F4, I4, U2 = "bfloat16", "float16", "float32", "int32", "uint16"
_S = dict(
    Q=(TW, B), S1=(TW, B), S2=(TW, B), BITS=(TW, B), CT=(4096, F4), MPT=(4096, B), VT=(2048, B), UR=(4096, H16),
    X0=(2048, B), X1=(2048, B), M0=(2048, B), M1=(2048, B), IND=(256, B), SB=(2048, B), SA=(2048, B), RB=(448, B), HB=(64, B),
    CF=(80, F4), CI=(32, I4), OH=(16, F4), DD=(16, F4), IO=(160, F4), IW=(160, B), WW=(144 * 12, B), WH=(144 * 3, H16),
    MAT=(2688, B), I32=(152, F4), I16=(256, H16), PI2=(KN, B), HI2=(KN, B), GM=(128, B), KIX=(2 * KN, B),
    I16c=(256, B), MASK=(256, B), MNG=(128, B), CS=(256, B), RK=(KN, F4), IL=(256, B), ONE=(256, B), LW=(16, F4), KC=(16, H16), KL=(128, H16),
    CO=(256, F4), UL=(64, U2), TI=(256, I4), TJ=(512, I4), TF=(512, F4), TG=(512, F4), TB=(2048, B), TM=(512, B), TU=(256, H16), BT=(512, B),
    PLi=(256, I4), MTi=(128, I4), MTu=(128, U2), PWu=(256, U2), NB=(1024, B), LP=(512, B), LM=(512, B), YO=(768, F4),
    FWb=(128, B), CE=(144, H16), C3=(136, F4), SS=(16, F4), SW=(128, F4), cu=(32, U2), aW=(16, U2), XI=(768, B),
    va=(512, B), y=(256, H16), AO=(256, F4), AB=(256, B), AT=(1024, B), aR=(256, F4), SAT=(32, F4), S1a=(256, B), S1c=(256, B), S2c=(256, B), vc=(256, B),
    BB=(512, B), BL=(1024, B), ui=(32, I4), uo=(16, U2), co=(256, U2), cF=(256, F4), hB=(256, B), eq=(256, B), SC=(8 * KN, F4), KI=(128, I4),
    KJ=(128, I4), lo=(32, I4), lof=(32, F4), E=(512, B), cw=(16, U2), mg=(256, B), mo=(16, U2), DW=(104, I4), Di=(64, I4), TH=(96, F4), ML=(64, F4),
    st=(64, F4), E2=(256, H16), R=(512, B), Z=(256, B), JK=(768, B), BA=(48, F4), DX=(96, F4), OT=(128, F4), OF=(48, U2),
    no=(512, B), po=(16, U2), VAL=(768, B), QV=(512, B), dn=(256, B), P6=(96, F4), O2=(40, U2), V2=(384, B), G6=(768, B), R6=(512, B))
_S.update(S2=(4096, B), SA=(2048, F4), SP=(336, B), S1f=(256, F4), LB=(16, B), MAT=(128 * 24, B), CF=(96, F4)); del _S["S2c"]
SCRATCH = {k: ("sbuf", [128, n], d) for k, (n, d) in _S.items()}
SCRATCH["PS"] = ("psum", [128, 2048], F4)
SCRATCH["PB"] = ("psum", [128, 2048, 2], B)
PSUM = {"PS": 512, "PB": 1024}
NDMA = 60
SEMAPHORES = ["pe", "dve", "act", "pool", "snt"] + ["arr%d" % t for t in range(4)] + ["hin%d" % t for t in range(4)] + ["d%d" % i for i in range(NDMA)]
INFO = {}; PLAN = {}
SWAPS, DRIFT, NEAR, TEMP, APART, GREED, TABU = 4500, 50.0, 0.02, 0.15, 3.0, 5.0, 4
GA, SCA, CYC, FIX, GAP, PEC, WAY = 1.3, 3.15, 0.83, 0.05, 0.1, 0.48e-3, 6.0
LOOK, ITER, NOISE, ND, MGA, TTH, PCS = 0.05, 8, 1.0, ((0, 5), (0, 7)), 1, 0.75, 4
SUBS = {None: ((0, 16, 1), (16, 56, 0), (56, 96, 0), (96, 128, 0)), (0, 0): ((0, 32, 1), (32, 56, 1), (56, 96, 0), (96, 128, 0)),
        (3, 1): ((0, 32, 0), (32, 64, 0), (64, 96, 0), (96, 128, 0))}
SUM = (("X", 0, 128), ("M", 0, 128))
MIX, SAS, MPV, TRANS, NOA, SCA1, CTV, QAF = 1, 1, 3, 1, 0, 1, 2, 1


def routes(T, topo, r):
    me = T.cores[r]; n = len(T.cores); direct = []; far = []
    for d in range(1, n):
        c = T.cores[(r + d) % n]
        (direct if topo.may_write(me, c) else far).append((d, c))
    off = topo.engines(me, direct[0][1])
    hs = [h for h in topo.cores_of(me) if h != me and all(topo.may_write(h, c) for _, c in far)]
    hs.sort(key=lambda h: topo.die(h) != topo.die(me))
    on = [e for e in topo.engines(me, hs[0]) if e not in off]

    def deal(es, k):
        sz = [1] * k
        while sum(sz) + min(sz) <= len(es):
            j = sz.index(min(sz)); sz[j] *= 2
        out = []; p = 0
        for z in sorted(sz, reverse=True):
            out.append(sum(1 << e for e in es[p:p + z])); p += z
        return out
    return ([(d, c, None, m) for (d, c), m in zip(direct, deal(off, len(direct)))]
            + [(d, c, h, m) for (d, c), h, m in zip(far, hs, deal(on, len(far)))])


def relay(g, core, T, topo):
    for r in range(len(T.cores)):
        for d, c, h, m in routes(T, topo, r):
            if h == core:
                rid, pid = topo.addr(c, core); mk = topo.mask(core, c)
                for t in range(4):
                    g.wait_ge(T.sem["hin%d" % t], bin(m).count("1"))
                    k = 112 * t + 16 * (d - 1)
                    g.remote_dma_fused([RemoteDMATransfer(dst_ids=[DstId(rid=rid, pnc=pid)], dma_engine_mask=mk, remote_sem=T.sem["arr%d" % t],
                                                          src=T.HB[:, 16 * t:16 * t + 16], dst=T.RB[:, k:k + 16])], local_sem=T.sem.snt)
                g.wait_ge(T.sem.snt, 4 * bin(mk).count("1"))


def rank_program(g, core, T, topo):
    r = T.rank_of(core)
    if r is None:
        relay(g, core, T, topo)
        return
    ops = []; hist = {}

    def A(n, a, b, s=1, p=(0, 128), reg=None):
        if n == "PB":
            ap = T[n][p[0]:p[1], a // 2:b // 2:s // 2, :] if s > 1 else T[n][p[0]:p[1], a // 2:b // 2, :]
        else:
            ap = T[n][p[0]:p[1], a:b:s] if s > 1 else T[n][p[0]:p[1], a:b]
        if n in PSUM:
            w = PSUM[n]
            return (ap, [(n, a // w * w, (b + w - 1) // w * w)], [], len(range(a, b, s)), n == "PB", True)
        return (ap, [(reg or n, a, b)], [], len(range(a, b, s)), _S[n][1] in (B, H16, U2), False)

    def IX(w, o):
        return (w[0].indirect(o[0]), w[1], o[1], 16 * o[3], False, False)

    def X(ap):
        return (ap, [], [], 0, False, False)
    isop = lambda v: isinstance(v, tuple)
    ap = lambda v: v[0] if isop(v) else v

    def op(q, fn, outs, ins, cost, lat=0.0, kind="c", tag=None, ext=None, after=()):
        i = len(ops); deps = {}
        acc = []
        for v in outs:
            acc += [(x, True) for x in v[1]] + [(x, False) for x in v[2]]
        for v in ins:
            if isop(v):
                acc += [(x, False) for x in v[1] + v[2]]
        for (n, a, b), w in acc:
            for (a2, b2, j, w2) in hist.get(n, []):
                if a < b2 and a2 < b and (w or w2 or n in PSUM):
                    o = ops[j]
                    if tag is not None and o["tag"] == tag:
                        continue
                    sem = o["kind"] != "c" or o["q"] != q or (q != "pe" and n not in PSUM)
                    deps[j] = deps.get(j, False) or sem
        for (n, a, b), w in acc:
            h = hist.setdefault(n, [])
            if (w and tag is None) or n in PSUM:
                h[:] = [e for e in h if not (a <= e[0] and e[1] <= b)]
            h.append((a, b, i, w))
        for j in after:
            deps.setdefault(j, False)
        ops.append(dict(q=q, fn=fn, deps=deps, cost=cost, lat=lat, kind=kind, tag=tag, ext=ext))
        return i

    def vc_(o, ins, base):
        if o[2]:
            return FIX + o[3] * SCA * 1e-3
        if any(isop(v) and v[2] for v in ins):
            return FIX + o[3] * GA * 1e-3
        return FIX + max(64, max(v[3] for v in ins + [o] if isop(v)) * base) * CYC * 1e-3
    half = lambda *v: 0.5 if all(x[4] for x in v) else 1.0

    def tc(o, a, **k): return op("dve", lambda e: e.tensor_copy(o[0], a[0]), [o], [a], vc_(o, [a], half(o, a)), **k)
    def tt(o, a, b, f, **k): return op("dve", lambda e: e.tensor_tensor(o[0], a[0], b[0], f), [o], [a, b], vc_(o, [a, b], (TTH if half(o, a, b) < 1 else 1) if a[5] or b[5] else 2 * half(o, a, b)), **k)

    def ts(o, a, s1, f0, s2=None, f1=None, **k):
        fn = (lambda e: e.tensor_scalar(o[0], a[0], ap(s1), None, f0)) if f1 is None else (lambda e: e.tensor_scalar(o[0], a[0], ap(s1), ap(s2), f0, f1))
        return op("dve", fn, [o], [a, s1, s2], vc_(o, [a], half(o, a)), **k)
    def scan(o, a, b, f0, f1, init=0.0): return op("dve", lambda e: e.tensor_tensor_scan(o[0], a[0], b[0], init, f0, f1), [o], [a, b], vc_(o, [a], half(o, a, b)))
    def nmin(o, a): return op("dve", lambda e: e.tensor_reduce(o[0], a[0], AxisListType.X, O.min, negate=True), [o], [a], vc_(o, [a], 1))
    def red(o, a, f): return op("dve", lambda e: e.tensor_reduce(o[0], a[0], AxisListType.X, f), [o], [a], vc_(o, [a], 1))
    def ms(o, c): return op("dve", lambda e: e.memset(o[0], c), [o], [], vc_(o, [], half(o)))

    def act(o, a, bias=0.0, scale=1.0, f=F.Identity, acc=None, **k):
        fn = ((lambda e: e.activation(o[0], a[0], f, bias=ap(bias), scale=ap(scale))) if acc is None else
              (lambda e: e.activation(o[0], a[0], f, bias=ap(bias), scale=ap(scale), accum_out=acc[0])))
        return op("act", fn, [o] + ([acc] if acc else []), [a, bias, scale], vc_(o, [a], 1) + (0.02 if acc else 0.0), **k)

    def silu(o, a): return op("act", lambda e: e.activation(o[0], a[0], F.Silu), [o], [a], vc_(o, [a], 1))

    def mm(lst):
        def fn(e):
            for o, l, rr, s0, s1 in lst:
                i = e.matmul(o[0], l[0], rr[0], s0, s1)
            return i
        c = sum(max(min(64, l[3]), rr[3]) * (1 if l[4] else 4) for o, l, rr, s0, s1 in lst) * PEC
        return op("pe", fn, [x[0] for x in lst], [x[1] for x in lst] + [x[2] for x in lst], c)
    grp = lambda o, prs: [(o, l, rr, i == 0, i == len(prs) - 1) for i, (l, rr) in enumerate(prs)]

    def trs(lst):
        def fn(e):
            for o, a, idn in lst:
                i = e.transpose(o[0], a[0], idn[0])
            return i
        return op("pe", fn, [x[0] for x in lst], [x[1] for x in lst] + [x[2] for x in lst], sum(max(64, x[2][3]) for x in lst) * PEC + 0.02)
    wn = {"WW": {}, "WH": {}}

    def W(n, x=None):
        buf = "WH" if n in ("Ww", "Wv", "W1") else "WW"; k = 144 * wn[buf].setdefault(n, len(wn[buf]))
        return A(buf, k, k + 144) if x is None else A(buf, k + 15 - x, k + 143 - x)

    def wrap(o, w, n, a, b, odd=False):
        return mm(grp(o, [(W(w, x), A(n, a + ((x | 1) if odd else x), b, 16)) for x in range(16)]))

    def iota(o, pat, base, cm):
        fl = _S[o[1][0][0]][1] != I4
        fn = (lambda e: e.iota(o[0], pat, base, cm, allow_small_or_imprecise_dtypes=True)) if fl else (lambda e: e.iota(o[0], pat, base, cm))
        return op("pool", fn, [o], [], 0.25 + o[3] * 2 * CYC * 1e-3)

    def dma(o, a, q="sync", tag=None, lat=2.5): return op(q, lambda e: e.dma_start(o[0], a[0]), [o], [a], 0.1, lat, "dma", tag)

    def load(n, a, b, src, dr, sr, q):
        for x, y in ((0, cut[1] // 16), (cut[1] // 16, 8)):
            dma(A(n, a, b, p=(dr * x, dr * y)), X(src[sr * ((x + r) % 8):sr * ((x + r) % 8 + y - x), :]), q, "ld" + n)
    cut = (0, 128 - 16 * r if r else 64, 128)
    rowsof = lambda n, row, a, b: (T[n][row:128:16, a:b], [(n, a, b)], [], 0, False, False)
    PS = lambda bank, a, b, s=1, p=(0, 128): A("PS", 512 * bank + a, 512 * bank + b, s, p)
    cn = {}
    def c(n): return A("CF", cn.setdefault(n, len(cn)), cn[n] + 1)
    mn = {}
    def M(n): return A("MAT", 128 * mn.setdefault(n, len(mn)), 128 * mn[n] + 128)
    ci = lambda k: A("CI", k, k + 1)
    oh = lambda k: A("OH", k, k + 1)
    dd = lambda k: A("DD", k, k + 1)

    load("PLi", 0, 256, T.pr, 16, 1, "sync"); load("MTi", 0, 128, T.mt, 16, 1, "act")
    load("CI", 16, 17, T.kk, 16, 16, "sync"); load("CI", 20, 21, T.w, 16, 16, "act"); load("CI", 24, 25, T.th, 1, 1, "sync")
    for k in range(len(cut) - 1):
        a, b = cut[k], cut[k + 1]; ra = (a + 16 * r) % 128
        dma(A("Q", 0, 4096, p=(a, b)), X(T.rec[ra:ra + b - a, :]), "act" if k % 2 else "sync", "ldQ", 6.0)
    ms(A("S1", 0, 2048), 0.0); ms(A("S1", 2048, 4096), 0.0)
    iota(ci(0), [[0, 1]], 0, 1); iota(A("IO", 0, 160), [[1, 160]], 0, 0); iota(A("I16c", 0, 256), [[0, 16], [1, 16]], 0, 0)
    iota(A("IL", 0, 256), [[1, 256]], 0, 0); iota(A("ONE", 0, 256), [[0, 256]], 1, 0)
    ts(ci(1), ci(0), 15, O.bitwise_and); ts(ci(2), ci(0), 4, O.arith_shift_right); ts(ci(3), ci(0), 1, O.bitwise_and)
    ts(ci(4), ci(0), 4, O.arith_shift_right, 1, O.bitwise_and); ts(ci(5), ci(0), 3, O.arith_shift_right); ts(ci(6), ci(0), 7, O.bitwise_and)
    ts(ci(7), ci(0), 15, O.bitwise_and, 1, O.arith_shift_right)
    tc(A("CF", 0, 8), A("CI", 0, 8))
    for n in ("p", "x", "b", "p1", "odd", "r8", "p7", "x2"):
        c(n)
    ts(A("OH", 0, 16), A("IO", 0, 16), c("x"), O.is_equal)
    act(A("DD", 0, 15), A("OH", 0, 15), scale=256.0); tt(A("DD", 0, 15), A("DD", 0, 15), A("OH", 1, 16), O.add)
    act(c("b15"), c("b"), bias=15.0, scale=16.0); act(c("p16"), c("p"), bias=16.0)
    ts(W("WB"), A("IO", 0, 144), c("b15"), O.is_equal); ts(A("IW", 0, 160), A("IO", 0, 160), c("p16"), O.is_equal)
    ts(c("hi"), c("x"), 8.0, O.is_ge); act(c("lo"), c("hi"), bias=1.0, scale=-1.0); ts(c("l12"), c("x"), 12.0, O.is_lt)
    act(c("wg"), oh(12), bias=oh(4), scale=512.0); act(c("w3a"), oh(8), scale=-2048.0); act(c("w3"), oh(7), bias=c("w3a"), scale=8192.0)
    for n, s in (("Wf", oh(4)), ("Wp", dd(0)), ("Wmp", dd(5)), ("Wg", c("wg")), ("W8", c("lo"))):
        act(W(n), W("WB"), scale=s)
    ts(W("W1"), W("WB"), oh(0), O.mult)
    sh = lambda k: A("IW", 16 - k, 144 - k)
    ts(A("MASK", 0, 256), A("I16c", 0, 256), c("x"), O.is_equal)
    act(A("MNG", 0, 128), A("MASK", 0, 128), bias=-2.0 ** 30, scale=2.0 ** 30); act(A("CS", 0, 256), A("ONE", 0, 256), scale=oh(4))
    iota(M("Z"), [[0, 128]], 0, 0); iota(M("t0"), [[1, 8], [0, 16]], 0, 0); ts(M("BD"), M("t0"), c("b"), O.is_equal)
    ts(M("t1"), A("IO", 0, 128), c("p"), O.is_ge); tt(M("TRI"), M("t1"), M("BD"), O.mult)
    act(M("t0"), sh(8), scale=c("lo")); act(M("t1"), sh(-8), scale=c("hi")); tt(M("PERM"), M("t0"), M("t1"), O.add)
    act(M("PERMn"), M("PERM"), scale=-1.0); act(M("N4096"), sh(0), scale=-4096.0); act(M("BDi"), M("BD"), scale=dd(12)); act(M("In"), sh(0), scale=-1.0)
    tc(A("I16", 0, 128), sh(0)); tc(A("I16", 128, 256), M("PERM"))
    tt(M("t1"), M("PERM"), sh(0), O.add); act(M("Msel"), M("t1"), scale=oh(4))
    act(c("nj"), dd(2), scale=-1.0); act(M("MJ"), A("WW", 0, 128), scale=c("nj"))
    iota(A("KIX", 0, KN), [[0, 2], [32, 8], [1, KW]], 0, 0); act(c("k32"), c("b"), bias=c("x"), scale=32.0); act(c("k48"), c("k32"), bias=16.0)
    ts(A("PI2", 0, KN), A("KIX", 0, KN), c("k32"), O.is_equal, 2.0 ** 23, O.mult); ts(A("KIX", KN, 2 * KN), A("KIX", 0, KN), c("k48"), O.is_equal, 2.0 ** 26, O.mult)
    act(A("HI2", 0, KN // 2), A("PI2", 0, KN // 2), scale=-2.0 ** -17); act(A("HI2", KN // 2, KN), A("PI2", KN // 2, KN), scale=2.0 ** -23)
    tt(A("HI2", 0, KN), A("HI2", 0, KN), A("KIX", KN, 2 * KN), O.add); act(A("I32", 0, KN // 2), A("PI2", 0, KN // 2), scale=2.0 ** -23)
    ms(A("RK", 0, KN), -64.0)
    for k, v in ((0, 2.0 ** 25), (16, -8387040.5), (17, 1.5 * 2.0 ** 29), (18, -1.5 * 2.0 ** 29)):
        ms(A("RK", k, KN, KW), v)
    act(c("m01"), oh(0), bias=oh(1)); act(c("m56"), oh(5), bias=oh(6)); act(c("mk"), oh(12), bias=oh(13)); act(c("m4"), c("m01"), bias=c("m56"))
    act(c("keep"), c("m56"), bias=1.0, scale=-1.0); act(c("md"), oh(13), bias=oh(14), scale=1.0 / 256); act(c("m89"), oh(8), bias=oh(9))
    act(c("own"), c("mk"), bias=c("m89")); act(c("k89"), c("m89"), bias=1.0, scale=-1.0); act(c("kx"), c("m89"), bias=c("keep"), scale=-1.0)
    for n, prs in (("Mo", ((0, "m4"), (12, "m01"), (3, "m56"))), ("Mx", ((-12, "mk"), (-3, "m89"))), ("Mk", ((0, "own"),)), ("Md", ((-11, "md"),)),
                   ("M7", ((-7, "mk"),)), ("M4", ((-4, "mk"),)), ("K89", ((0, "k89"),)), ("Kx", ((0, "kx"),)), ("Mz", ((0, "m56"), (3, "m56")))):
        for j, (k, s) in enumerate(prs):
            act(M("t2" if j else n), sh(k), scale=c(s))
            if j:
                tt(M(n), M(n), M("t2"), O.add)
    act(M("t0"), sh(0), scale=c("l12")); I12 = M("t0"); Ib = sh(0)
    GG, GN, GP, G15, GD, G64, G1x = (A("GM", 16 * k, 16 * k + 16) for k in range(7))
    ts(A("GM", 0, 8), A("IO", 0, 8), c("b"), O.is_equal); act(A("GM", 8, 16), A("GM", 0, 8))
    act(c("g15"), oh(15), scale=-2.0 ** 40); act(c("gd"), oh(7), scale=-8192.0)
    act(GN, GG, scale=-1024.0); act(GP, GG, scale=2048.0); act(G15, GG, scale=c("g15")); act(GD, GG, scale=c("gd")); act(G64, GG, scale=64.0)
    G1 = A("GM", 0, 8); G64 = A("GM", 80, 88)
    act(G1x, GG, scale=0.0); act(A("GM", 97, 112, 2), G1)
    act(c("pd"), c("p1"), bias=1.0, scale=-2.0); act(c("off"), c("pd"), bias=-0.5, scale=3072.0); act(c("even"), c("odd"), bias=1.0, scale=-1.0)
    act(c("s1"), c("l12"), scale=-1048576.0); act(c("s4"), oh(13), bias=oh(14)); act(c("s3"), c("s4"), bias=oh(12), scale=256.0)
    act(c("s2"), oh(15), bias=c("s3"), scale=2097152.0)
    for n in ("even", "odd"):
        act(c("s1" + n), c("s1"), scale=c(n)); act(c("s2" + n), c("s2"), scale=c(n))
    act(c("r1"), oh(15), scale=2049.0); act(c("r2"), oh(15), bias=-1.0)
    act(c("tl0"), c("p"), bias=-12582912.0); act(c("tl1"), c("p"), bias=-12582912.0 + 128)
    iota(A("CO", 208, 224), [[16, 16]], 0, 0); act(A("LW", 0, 16), A("CO", 208, 224), bias=c("x"))
    DU1, DU2, L257 = A("BA", 0, 16), A("BA", 32, 48), A("CO", 32, 48)
    act(L257, A("LW", 0, 16), bias=257.0)
    OB = A("CO", 96, 126)
    for k, bs in ((0, D1), (8, 0), (16, D1 + 128), (23, D1)):
        act(A("CO", 96 + k, 104 + k), A("LW", 0, 8), bias=float(bs))
    act(A("LB", 0, 7), A("LW", 0, 7), bias=128.0); act(A("LB", 7, 14), A("LW", 0, 7))
    act(c("np1"), c("p1"), bias=1.0, scale=-1.0); act(A("CO", 64, 80), A("LW", 0, 16))
    act(A("CO", 80, 88), A("LW", 0, 8), bias=c("np1")); act(A("CO", 87, 95), A("LW", 0, 8), bias=c("np1"))
    act(c("b5"), dd(5), scale=-12582912.0 - 128); act(c("b12"), dd(12), scale=-12582912.0 - 128); act(M("BD4"), M("BD"), scale=oh(4))
    for k, bs in enumerate((D1, D2, D1)):
        act(A("BA", 16 * k, 16 * k + 16), A("LW", 0, 16), bias=float(bs))
    act(A("DX", 1, 96, 2), A("BA", 0, 48))
    iota(A("CO", 144, 160), [[16, 2], [1, 8]], 0, 0); iota(A("CO", 160, 176), [[1, 2], [0, 8]], 0, 0)
    EL, L2, E2L = A("UL", 0, 16), A("UL", 16, 17), A("UL", 32, 48)
    tc(EL, A("IO", 0, 16)); tc(L2, c("x2"))
    ts(c("c1"), c("x"), 13.0, O.is_ge); act(c("c4"), oh(14), scale=32.0); act(c("c2"), oh(15), bias=c("c4"), scale=64.0)
    act(c("c3"), oh(12), bias=c("c2"), scale=96.0); act(c("c5"), c("l12"), bias=c("c3"), scale=98.0)
    act(A("CO", 176, 192), A("CO", 144, 160), bias=c("c5"), scale=c("c1")); act(A("CO", 192, 208), A("CO", 160, 176), scale=oh(12))
    tt(A("CO", 176, 192), A("CO", 176, 192), A("CO", 192, 208), O.add); tc(E2L, A("CO", 176, 192))
    iota(A("DW", 0, 104), [[0, 104]], 0, 0); iota(A("DW", 96, 98), [[128, 2]], 0, 1)
    HC = A("TJ", 384, 480); iota(HC, [[64, 3], [0, 32]], -192, 0)
    for n, a, b, v in (("ML", 0, 64, 0), ("TH", 0, 96, 0), ("C3", 128, 136, 4096), ("SS", 8, 16, 4096), ("Q", 4096, TW, 0), ("BITS", 4096, TW, 0), ("S1", 4096, TW, 0),
                       ("Z", 0, 256, 0), ("P6", 0, 96, 0)):
        iota(A(n, a, b), [[0, b - a]], v, 0)
    ts(A("CE", 0, 16), A("ONE", 0, 16), 0.0, O.mult)
    for t in range(4):
        iota(A("SB", 512 * t + 256, 512 * t + 368), [[0, 112]], 1000, 0); iota(A("SA", 512 * t + 256, 512 * t + 368), [[0, 112]], 128 * SAS, 0)
    p8 = (0, 8)
    ts(A("CI", 25, 26, p=p8), A("CI", 24, 25, p=p8), 8, O.arith_shift_right); ts(A("CI", 26, 27, p=p8), A("CI", 24, 25, p=p8), 255, O.bitwise_and)
    tc(A("TM", 384, 386, p=p8), A("CI", 25, 27, p=p8)); iota(A("TM", 256, 384, p=p8), [[1, 8], [0, 16]], 0, -1)
    ts(A("TM", 256, 384, p=p8), A("TM", 256, 384, p=p8), 0.0, O.is_equal)
    mm(grp(PS(3, 0, 2), [(A("TM", 256, 384, p=p8), A("TM", 384, 386, p=p8))])); c("th0"); c("th1")
    act(A("CF", cn["th0"], cn["th1"] + 1), PS(3, 0, 2))
    act(c("t2"), oh(2), bias=oh(4), scale=c("th0")); act(c("thb"), oh(3), bias=c("t2"), scale=c("th1"))
    tb = lambda k: A("TB", 256 * k, 256 * k + 256)
    act(c("x256"), c("x"), scale=256.0); ts(A("TF", 0, 256), A("PLi", 0, 256), c("x256"), O.subtract)
    tt(tb(4), A("TF", 0, 256), A("IL", 0, 256), O.is_equal); dma(rowsof("S1", 4, 0, 4096), tb(4), "sync", "s1")
    ts(tb(0), A("PLi", 0, 256), 1.0 / 256, O.mult, 129.0 - 127.5 / 256, O.add); act(tb(0), tb(0), bias=-129.0)
    ts(A("TI", 0, 256), A("PLi", 0, 256), 255, O.bitwise_and); tc(tb(1), A("TI", 0, 256))
    act(tb(5), A("ONE", 0, 256), scale=c("x")); act(tb(2), A("ONE", 0, 256), scale=c("th0")); act(tb(3), A("ONE", 0, 256), scale=c("th1"))
    m8, m9 = A("TB", 1792, 1920), A("TB", 1920, 2048)
    ts(m8, A("MTi", 0, 128), 1.0 / 256, O.mult, 128.0 - 127.5 / 256, O.add); act(m8, m8, bias=-128.0)
    ts(A("TJ", 256, 384), A("MTi", 0, 128), 255, O.bitwise_and); tc(m9, A("TJ", 256, 384))
    dma(rowsof("S1", 8, 0, 2048), m8, "sync", "s1"); dma(rowsof("S1", 9, 0, 2048), m9, "sync", "s1")
    for src, row in ((tb(0), 0), (tb(1), 1), (tb(5), 12), (A("IL", 0, 256), 13)):
        dma(rowsof("S1", row, 0, 4096), src, "sync", "s1")
    ts(A("MTu", 0, 128), A("MTi", 0, 128), -2048.0, O.add)
    iota(A("TM", 0, 256), [[0, 16], [1, 8], [0, 2]], 0, 0); iota(A("VT", 256, 512), [[1, 16], [0, 8], [128, 2]], 0, 0)
    act(A("TM", 0, 256), A("TM", 0, 256), scale=oh(8)); act(A("VT", 256, 512), A("VT", 256, 512), scale=oh(9)); tt(A("VT", 0, 256), A("VT", 256, 512), A("TM", 0, 256), O.add)
    act(c("o9"), oh(9), scale=16.0); act(A("CO", 240, 248), A("IO", 0, 8), scale=c("o9"))
    for k in range(8):
        if k:
            act(A("VT", 256 * k, 256 * k + 256), A("VT", 0, 256), bias=A("CO", 240 + k, 241 + k))
        tc(IX(A("S2", 2048, 4096), A("MTu", 16 * k, 16 * k + 16)), A("VT", 256 * k, 256 * k + 256))
    dma(A("S2", 0, 2048), A("S1", 0, 2048), "sync", None, 4.0)
    kj = lambda a, b: A("KJ", 0, 128, p=(a, b))
    iota(kj(0, 32), [[1, 2], [0, 64]], 0, 2); iota(kj(32, 64), [[0, 2], [1, 64]], 0, 0); iota(kj(64, 96), [[1, 128]], 0, 128); iota(kj(96, 128), [[1, 128]], 0, 128)
    tt(kj(64, 128), kj(64, 128), kj(64, 128), O.mult)
    ts(kj(64, 96), kj(64, 96), 11, O.arith_shift_right, 63, O.bitwise_and); ts(kj(96, 128), kj(96, 128), 5, O.arith_shift_right, 63, O.bitwise_and)
    tc(A("TU", 0, 128), kj(0, 128)); dma(A("UR", 0, 4096, p=(0, 4)), A("TU", 0, 128), "sync")
    ts(ci(8), ci(16), 63, O.bitwise_and); ts(A("KC", 0, 1), ci(8), 64.0, O.mult); tc(A("KC", 1, 2), ci(16))
    ts(A("KC", 2, 3), A("ONE", 0, 1), 64.0, O.mult); tc(A("KC", 3, 4), A("ONE", 0, 1))
    mm(grp(PS(3, 128, 256, p=(0, 4)), [(A("KC", 0, 4), A("I16", 0, 128))])); tc(A("KL", 0, 128, p=(0, 4)), PS(3, 128, 256, p=(0, 4)))
    tc(A("KC", 4, 5), ci(20)); ts(c("w2"), ci(20), 0.5, O.mult); ts(W("Ww"), W("WB"), c("w2"), O.mult)
    ts(A("KC", 6, 7), ci(20), c("pd"), O.mult); tc(A("TU", 128, 256), M("BD"))
    mm(grp(PS(3, 8, 9), [(A("I16", 128, 256), A("KC", 4, 5))]) + grp(PS(3, 9, 10), [(A("TU", 128, 256), A("KC", 6, 7))]))
    act(c("wv"), PS(3, 8, 9)); act(c("cw"), PS(3, 9, 10), scale=-1536.0); ts(W("Wv"), W("WB"), c("wv"), O.mult)
    for t in range(4):
        ts(c("wt%d" % t), c("x"), float((2047 - 341 * t) % 16), O.is_le); act(W("WT%d" % t), W("WB"), scale=c("wt%d" % t))

    def lanes(t):
        s = 341 * t; lst = [(PS(2, 0, 128), M("Z"), Ib, True, False)]
        for x in range(16):
            f = s + x; n1 = min(128, (2048 - f + 15) // 16); Wx = W("Wf", x)
            lst.append((PS(2, 0, n1), Wx, A("S1", f, 2048, 16), False, x == 15 and n1 == 128))
            if n1 < 128:
                f2 = f + 16 * n1 - 2048
                lst.append((PS(2, n1, 128), Wx, A("S1", f2, f2 + 16 * (128 - n1), 16), False, x == 15))
            if x % 4 == 3:
                mm(lst); lst = []
        FW = A("FWb", 0, 128); IL = A("IL", 0, 256); w = lambda k: A("SW", 16 * k, 16 * k + 16); c0 = (2047 - s) // 16
        act(FW, PS(2, 0, 128)); mm(grp(PS(2, 128, 256), [(M("BD"), FW)]))
        scan(A("CE", 16, 144), A("ONE", 0, 128), PS(2, 128, 256), O.mult, O.add)
        mm(grp(PS(2, 384, 385), [(W("W1", x), A("CE", 31 + 16 * x, 32 + 16 * x)) for x in range(8)]
               + [(W("W1", 8), A("CE", 15 + c0, 16 + c0)), (W("WT%d" % t, 8), A("FWb", c0, c0 + 1))]))
        ts(A("IND", 0, 256), IL, PS(2, 384, 385), O.is_ge)
        wrap(PS(3, 400, 408), "W1", "CE", 16, 144); act(A("SS", 0, 8), PS(3, 400, 408))
        wrap(PS(2, 400, 416), "W8", "IND", 0, 256); tc(A("cu", 0, 16), PS(2, 400, 416)); act(w(0), PS(2, 400, 416), scale=16.0)
        mm(grp(PS(3, 256, 384), [(M("TRI"), FW), (A("I16", 0, 128), A("CE", 15, 143))])); act(A("C3", 0, 128), PS(3, 256, 384))
        act(A("XI", 256, 512), A("IND", 0, 256), scale=c("w3"))
        tt(A("XI", 0, 256), IX(A("SS", 0, 16), A("cu", 0, 16)), IL, O.is_le)
        wrap(PS(2, 416, 448), "WB", "XI", 0, 512); tt(w(1), PS(2, 416, 432), w(0), O.add); tc(A("cu", 16, 32), w(1))
        act(w(2), w(1), bias=float(s), scale=16.0); tt(w(3), PS(2, 432, 448), w(2), O.add)
        tt(A("XI", 512, 768), IX(A("C3", 0, 136), A("cu", 16, 32)), IL, O.is_le)
        wrap(PS(2, 448, 464), "WB", "XI", 512, 768); tt(w(4), PS(2, 448, 464), w(3), O.add)
        ts(A("aW", 0, 16), w(4), float(DUM), O.min); tt(A("DX", 64, 96, 2), w(4), DU1, O.subtract)

    for k in range(4):
        mm([(PS(3, 0, 256), W("Wp", x), A("S1", x, 4096, 16), x == 0, x == 15) for x in range(4 * k, 4 * k + 4)])
    tc(A("PWu", 0, 256), PS(3, 0, 256))
    for k in range(8):
        pr = (A("KL", 0, 128, p=(0, 4)), A("UR", 512 * k, 512 * k + 512, p=(0, 4))); nb = A("NB", 512 * (k % 2), 512 * (k % 2) + 512)
        mm(grp(PS(0, 0, 512), [pr])); act(nb, PS(0, 0, 512), bias=129.0 - 4095.0 / 8192, scale=1.0 / 4096)
        mm(grp(PS(1, 0, 512), [pr, (M("N4096"), nb)]))
        if k % CTV == CTV - 1:
            ts(A("CT", 512 * k, 512 * k + 512), PS(1, 0, 512), 528384.0, O.add)
        else:
            act(A("CT", 512 * k, 512 * k + 512), PS(1, 0, 512), bias=528384.0)
    lanes(0); act(A("no", 0, 256), IX(A("S1", 0, TW), A("aW", 0, 16)))
    for k in range(8):
        (tc if k < MPV else act)(A("MPT", 512 * k, 512 * k + 512), IX(A("S2", 0, 4096), A("PWu", 32 * k, 32 * k + 32)))
    dma(rowsof("S1", 8, 2048, 4096), rowsof("S2", 8, 2048, 4096), "sync", "mp"); dma(rowsof("S1", 9, 2048, 4096), rowsof("S2", 9, 2048, 4096), "sync", "mp")
    dma(rowsof("S1", 2, 0, 4096), tb(2), "sync", "mp"); dma(rowsof("S1", 3, 0, 4096), tb(3), "sync", "mp")
    dma(rowsof("S1", 5, 0, 4096), rowsof("MPT", 8, 0, 4096), "sync", "mp"); dma(rowsof("S1", 6, 0, 4096), rowsof("MPT", 9, 0, 4096), "sync", "mp")
    ts(c("r12"), c("r8"), 12.0, O.is_lt)
    act(A("CO", 224, 240), A("ONE", 0, 16), scale=0.5)
    scan(A("CO", 0, 16), A("CO", 224, 240), A("MAT", 128 * mn["Z"], 128 * mn["Z"] + 16), O.mult, O.add, 1.0); ts(A("CO", 16, 32), A("IO", 0, 16), c("r8"), O.is_equal)
    tt(A("CO", 48, 64), A("CO", 0, 16), A("CO", 16, 32), O.mult); red(c("pw"), A("CO", 48, 64), O.add)
    act(c("p512"), c("p7"), scale=512.0); act(c("pb"), c("p512"), bias=2.0 ** -13, scale=c("pw"))
    iota(A("TG", 0, 512), [[1, 512]], 0, 0); act(A("TF", 0, 512), A("TG", 0, 512), bias=c("pb"), scale=c("pw"))
    act(A("TG", 0, 512), A("TF", 0, 512), bias=12582912.0); act(A("TG", 0, 512), A("TG", 0, 512), bias=-12582912.0)
    tt(A("TF", 0, 512), A("TG", 0, 512), A("TF", 0, 512), O.subtract); act(A("BT", 0, 512), A("TF", 0, 512), scale=c("r12"), f=F.Sign)
    for k in range(8):
        dma(A("BITS", 0, 4096, p=(16 * k, 16 * k + 16)), A("BT", 0, 512), "sync", "bits")
    dma(rowsof("BITS", 12, 0, 4096), tb(5), "sync", "bi2"); dma(rowsof("BITS", 13, 0, 4096), A("IL", 0, 256), "sync", "bi2")
    ts(ci(9), ci(2), float(r), O.add); ts(ci(9), ci(9), 7, O.bitwise_and); ts(c("g8"), ci(9), 8.0, O.mult)
    iota(A("JK", 0, 512), [[-1, 8], [1, 64]], 0, 0); ts(A("JK", 0, 512), A("JK", 0, 512), c("g8"), O.is_equal)
    act(A("LP", 0, 512), A("JK", 0, 512), scale=dd(0)); act(A("LM", 0, 512), A("JK", 0, 512), scale=dd(8))

    Qw, S1w, Bw, CTw = A("Q", 0, TW), A("S1", 0, TW), A("BITS", 0, TW), A("CT", 0, 4096)
    plan = routes(T, topo, r)
    narr = sum(bin(m if h is None else topo.mask(h, cc)).count("1") for s in range(8) for d, cc, h, m in routes(T, topo, s) if cc == core)
    nsnt = sum(bin(m).count("1") for d, cc, h, m in plan)
    big = []; unit = [0, 0]
    L = lambda n, h, k=0: A(n, 256 * k + 128 * h, 256 * k + 128 * h + 128)
    W8 = lambda n, h: A(n, 8 * h, 8 * h + 8)
    W16 = lambda n, h, k=0: A(n, k + 16 * h, k + 16 * h + 16)

    def contest(hl, hm):
        for k in range(8):
            z = int(k >= ND[hl][hm]); bk = 2 * z + unit[z] % 2; jk = 384 * (unit[z] % 2); unit[z] += 1; pp = (32 * (k // 2), 32 * (k // 2) + 32)
            lc, la = (A("BL", 256 * (z + k % 2) + 128 * hl, 256 * (z + k % 2) + 128 * hl + 128, p=pp) for z in (0, 2))
            mm(grp(PS(bk, 0, 256), [(lc, A("R", 256 * hm, 256 * hm + 256, p=pp))]) + grp(PS(bk, 256, 384), [(la, A("R", 256 * hm, 256 * hm + 128, p=pp))]))
            ml = A("ML", 16 * hl + 8 * hm + k, 16 * hl + 8 * hm + k + 1)
            if k < ND[hl][hm]:
                nmin(ml, PS(bk, 0, 384))
            else:
                act(A("JK", jk, jk + 384), PS(bk, 0, 384), bias=A("TH", 16 * hl + k, 16 * hl + k + 1), scale=-1.0, f=F.Relu, acc=ml)

    def choose(h):
        cw = W8("cw", h); bst = W16("KI", h, 64); Dd = W16("Di", h, 32); nd = ND[h]; k0 = 16 * h
        ts(W16("KI", h, 96), A("SC", (6 + h) * KN + 15, (7 + h) * KN, KW), 831.0, O.add); ts(W16("KJ", h, 96), W16("KI", h, 96), 0xFFFC3F, O.bitwise_and)
        tt(bst, W16("KI", h, 32), W16("KJ", h, 96), O.min); ts(W16("lo", h), bst, 63, O.bitwise_and)
        tt(A("E", 256 * h, 256 * h + 256), IX(W16("lo", h), EL), A("MASK", 0, 256), O.mult)
        mm(grp(PS(h, 312, 320), [(A("E", 256 * h, 256 * h + 128), G1), (A("E", 256 * h + 128, 256 * h + 256), G64)]))
        tc(cw, PS(h, 312, 320)); tt(A("DX", 32 + k0, 48 + k0, 2), PS(h, 312, 320), A("BA", 16 + 8 * h, 24 + 8 * h), O.subtract)
        ts(W16("Di", h), bst, 1.0 / 1024, O.mult); tt(Dd, W16("Di", h), W16("SAT", h), O.subtract)
        ts(W16("DW", h), Dd, 0x7F00, O.bitwise_and); ts(W16("DW", h, 32), Dd, 255, O.bitwise_and); ts(W16("DW", h, 64), Dd, -2048.0, O.add)
        tc(L("E2", h), IX(A("DW", 0, 104), A("UL", 32 + 8 * h, 40 + 8 * h)))
        ts(W16("TH", h), Dd, 256.0, O.mult, c("tl%d" % h), O.add)
        for hm in range(2):
            if nd[hm]:
                act(A("TH", 32 + k0 + 8 * hm, 32 + k0 + 8 * hm + nd[hm]), A("TH", k0, k0 + nd[hm]))
        act(L("BB", h), IX(Bw, cw)); (act if SCA1 else tc)(L("S1c", h), IX(S1w, cw))
        for k, n in enumerate(("even", "odd")):
            act(L("BL", h, k), L("BB", h), bias=c("s2" + n), scale=c("s1" + n))
        mm(sum((grp(PS(h, 128 * k, 128 * k + 128), [(I12, L("BB", h, k)), (L("E2", h), A("I16", 0, 128)), (M("MJ"), L("S1c", h))]) for k in range(2)), []))
        Rh = A("R", 256 * h, 256 * h + 256); Rc = A("R", 256 * h, 256 * h + 128)
        ts(Rh, PS(h, 0, 256), c("r1"), O.add, c("r2"), O.max)
        mm(grp(PS(h, 328, 344), [(Rc, G15)])); tt(W16("TH", h, 64), PS(h, 328, 344), W16("TH", h, 32), O.subtract)
        wrap(PS(h, 344, 352), "Wp", "S1c", 128 * h, 128 * h + 128); tt(A("DX", k0, 16 + k0, 2), PS(h, 344, 352), A("BA", 8 * h, 8 * h + 8), O.subtract)
        act(L("vc", h), IX(Qw, cw))

    def values(h, bk):
        sc, sa, Rc = L("S1c", h), L("S1a", h), A("R", 256 * h, 256 * h + 128)
        mm(grp(PS(bk, 0, 128), [(M("Mo"), sc)]) + grp(PS(bk, 128, 256), [(M("Mx"), sa), (M("Mk"), sc), (M("Md"), Rc)])
           + grp(PS(bk, 256, 384), [(M("Mx"), sc), (M("Mk"), sa), (M("Md"), Rc)]))
        act(L("VAL", h), PS(bk, 0, 128), bias=c("thb")); act(L("VAL", h, 1), PS(bk, 128, 256)); act(L("VAL", h, 2), PS(bk, 256, 384))

    def stands(h):
        tt(W16("st", h), W16("ML", h), W16("TH", h, 64), O.subtract); tt(A("st", 32 + 16 * h, 40 + 16 * h), A("st", 16 * h, 16 * h + 8), A("st", 16 * h + 8, 16 * h + 16), O.max)
        sw = A("st", 32 + 16 * h, 40 + 16 * h)
        tt(L("E", h), IX(sw, A("UL", 0, 8)), A("MNG", 0, 128), O.is_le); ts(A("Z", 128 * h + 4, 128 * h + 128, 8), IX(sw, L2), 0.0, O.is_le)

    for t in range(4):
        aW = A("aW", 0, 16)
        for h in range(2):
            act(L("va", h), IX(Qw, W8("aW", h)))
            if not MIX:
                tc(L("y", h), IX(Qw, W8("aW", h)))
            for e in range(2):
                act(A("AT", 512 * h + e, 512 * h + 256, 2), L("va", h))
            mm(sum((grp(PS(2 + h, 128 * k, 128 * k + 128), [(A("AT", 512 * h + 128 * k, 512 * h + 128 * k + 128), M("PERM"))]) for k in range(2)), []))
            act(A("AT", 512 * h + 256, 512 * h + 512), PS(2 + h, 0, 256))
            for k in range(2):
                b0 = 2048 * h + 1024 * k
                trs([(A("PB", b0 + 2 * q, b0 + 1024, 16), A("AT", 512 * h + 256 + 128 * k, 512 * h + 384 + 128 * k), Ib) for q in range(8)])
            mm(grp(PS(2 + h, 128, 256), [(M("PERM"), L("va", h))])); act(L("AO", h), PS(2 + h, 128, 256), bias=c("off")); act(L("AB", h), PS(2 + h, 128, 256))
        act(A("BB", 256, 512), IX(Bw, aW))
        mm(grp(PS(2, 256, 512), [(M("BDi"), A("BB", 256, 512) if t else A("no", 0, 256))])); act(A("aR", 0, 256), PS(2, 256, 512))
        mm(grp(PS(3, 256, 272), [(L("va", 0), GG), (L("IND", 0), GD)]) + grp(PS(3, 272, 288), [(L("va", 1), GG), (L("IND", 1), GD)])); act(A("SAT", 0, 32), PS(3, 256, 288))
        act(A("S1a", 0, 256), IX(S1w, aW)); act(A("va", 256, 512), A("va", 0, 256), scale=-1.0)
        if SAS:
            act(A("S1f", 0, 256), A("S1a", 0, 256), bias=128.0)
        for k, n in enumerate(("even", "odd")):
            act(A("BL", 512 + 256 * k, 768 + 256 * k), A("BB", 256, 512), bias=c("s2" + n), scale=c("s1" + n))
        for hop in range(4):
            for h in range(2):
                Xn, Mn = "X%d" % h, "M%d" % h; uo = W8("uo", h); K = PS(h, 0, KN)
                wrap(PS(h, 304, 312), "Ww" if hop else "Wv", "y" if hop or not MIX else "va", 128 * h, 128 * h + 128)
                SUB = SUBS.get((hop, h), SUBS[None])
                u0, u1 = A("ui", 16 * h, 16 * h + 8), A("ui", 16 * h + 8, 16 * h + 16)
                ts(u0, PS(h, 304, 312), c("cw") if hop else 0.0, O.add); ts(u1, u0, 4095, O.bitwise_and); tc(uo, u1)
                tc(L("co", h), IX(CTw, uo))
                for a, b, q in SUB:
                    if q:
                        tc(A(Xn, 16 * a, 16 * b), IX(Qw, A("co", 128 * h + a, 128 * h + b)))
                    else:
                        big = [act(A(Xn, 16 * a, 16 * b), IX(Qw, A("co", 128 * h + a, 128 * h + b)), after=big)]
                tt(L("eq", h), IX(CTw, uo), L("aR", h), O.is_equal)
                act(L("cF", h), IX(CTw, uo), bias=8385.0); act(L("hB", h), L("cF", h), bias=129.0 - (8385 + 31.5) / 64, scale=1.0 / 64)
                mm([(K, L("eq", h), A("PI2", 0, KN), True, False), (PS(h, 0, KN // 2), L("cF", h), A("I32", 0, KN // 2), False, False),
                    (K, L("hB", h), A("HI2", 0, KN), False, False)])
                for a, b, q in SUB:
                    tt(A(Mn, 16 * a, 16 * b), A(Xn, 16 * a, 16 * b), A("PB", 2048 * h + 16 * a, 2048 * h + 16 * b), O.max)
                for nm, a, b in SUM:
                    for i0 in range(0, 16, PCS):
                        mm([(PS(h, i, KN, KW, p=(a, b)), A(nm + str(h), 16 * a + i, 16 * b, 16), GN if nm == "X" else GP, False, nm == "M" and i == 15) for i in range(i0, i0 + PCS)])
                s0 = (2 * hop + h) * KN; scan(A("SC", s0, s0 + KN), A("RK", 0, KN), K, O.add, O.min)
                if hop < 3:
                    lo = W16("lof", h); e = A("E", 256 * h, 256 * h + 256)
                    tt(lo, A("SC", s0 + 16, s0 + KN, KW), A("SC", s0 + 18, s0 + KN, KW), O.subtract); tt(e, IX(lo, EL), A("MASK", 0, 256), O.mult)
                    mm(grp(PS(h, 312, 320), [(A("E", 256 * h, 256 * h + 128), G1), (A("E", 256 * h + 128, 256 * h + 256), G64)]))
                    ts(W8("cw", h), PS(h, 312, 320), 2047.5, O.add); (act if MGA else tc)(L("mg", h), IX(S1w, W8("cw", h)))
                    wrap(PS(h, 320, 328), "Wmp", "mg", 128 * h, 128 * h + 128); tc(W8("mo", h), PS(h, 320, 328))
                    tt(L("y", h), IX(Qw, W8("mo", h)), L("AO", h), O.add)
                else:
                    choose(h)
                    if h == 0:
                        contest(0, 0)
            if hop == 2:
                ts(A("KI", 0, 96), A("SC", 15, 6 * KN, KW), 831.0, O.add)
                ts(A("KJ", 0, 96), A("KI", 0, 96), 0xFFFC3F, O.bitwise_and); tt(A("KJ", 0, 96), A("KJ", 0, 96), HC, O.add)
                tt(A("KI", 0, 32), A("KJ", 0, 32), A("KJ", 32, 64), O.min); tt(A("KI", 32, 64), A("KI", 0, 32), A("KJ", 64, 96), O.min)
        contest(1, 0); contest(0, 1); stands(0); contest(1, 1); values(0, 2); values(1, 3); stands(1)
        mm([(PS(1, 32 * k + 16 * h, 32 * k + 16 * h + 16), L("E", h), G1x, True, True) for k in range(3) for h in range(2)])
        scan(A("OT", 0, 96), PS(1, 0, 96), A("DX", 0, 96), O.mult, O.add); tc(A("OF", 0, 48), A("OT", 1, 96, 2))
        tc(IX(S1w, A("OF", 0, 16)), A("VAL", 0, 256)); tc(IX(S1w, A("OF", 16, 32)), A("VAL", 256, 512))
        (act if NOA else tc)(A("no", 0, 256), IX(S1w, aW)); tc(IX(S1w, A("OF", 32, 48)), A("VAL", 512, 768))
        mm([(PS(0, 256, 512), M("Msel"), A("no", 0, 256), True, False)] + [(PS(0, 256 + 128 * h, 384 + 128 * h), L("Z", h), M("In"), False, h == 1) for h in range(2)])
        scan(A("no", 256, 512), A("CS", 0, 256), PS(0, 256, 512), O.mult, O.add)
        wrap(PS(0, 0, 16), "Wg", "no", 256, 512)
        tt(A("OT", 96, 112), PS(0, 0, 16), L257, O.max); ts(A("po", 0, 16), A("OT", 96, 112), -257.0, O.add)
        b0 = 512 * t
        tc(IX(A("SB", b0, b0 + 512), A("po", 0, 16)), A("va", 256, 512))

        def send(e, t=t, b0=b0):
            trs = []
            for d, cc, h, m in plan:
                rid, pid = topo.addr(cc if h is None else h, core); k = 112 * t + 16 * (d - 1)
                trs.append(RemoteDMATransfer(dst_ids=[DstId(rid=rid, pnc=pid)], dma_engine_mask=m, remote_sem=T.sem[("arr%d" if h is None else "hin%d") % t],
                                             src=T.SB[:, b0 + 240 + 16 * d:b0 + 256 + 16 * d], dst=T.RB[:, k:k + 16] if h is None else T.HB[:, 16 * t:16 * t + 16]))
            e.remote_dma_fused(trs, local_sem=T.sem.snt)
        snd = op("pool", send, [], [A("SB", b0 + 256, b0 + 368)], 0.5, WAY, "rem")
        sa = A("SP", 0, 112)
        if SAS:
            silu(IX(A("SA", b0, b0 + 512), A("po", 0, 16)), A("S1f", 0, 256)); act(A("TF", 0, 112), A("SA", b0 + 256, b0 + 368), bias=12582912.0)
            act(A("SP", 112, 224), A("TF", 0, 112), bias=c("b5"), scale=dd(5)); act(A("SP", 224, 336), A("TF", 0, 112), bias=c("b12"), scale=dd(12))
            act(sa, A("TF", 0, 112), bias=-12582912.0 - 128)
        mm(grp(PS(0, 16, 17), [(M("BD4"), A("no", 511, 512))])); ts(A("P6", 0, 30), A("CO", 64, 94), PS(0, 16, 17), O.is_lt)
        mm(grp(PS(1, 256, 512), [(Ib, A("AB", 0, 256)), (M("In"), A("vc", 0, 256))])); act(A("dn", 0, 256), PS(1, 256, 512), f=F.Sign)
        mm(grp(PS(1, 0, 256), [(Ib, A("va", 0, 256)), (M("PERMn"), A("dn", 0, 256))]) + grp(PS(1, 256, 512), [(Ib, A("vc", 0, 256)), (Ib, A("dn", 0, 256))]))
        act(A("QV", 0, 512), PS(1, 0, 512))
        tc(IX(Qw, A("OF", 32, 48)), A("QV", 0, 256), after=[snd - 1][:QAF]); tc(IX(Qw, A("OF", 16, 32)), A("QV", 256, 512), after=[snd - 1][:QAF])
        if t < 3:
            lanes(t + 1)
        else:
            for k in range(8):
                mm([(PS(2, 0, 512, p=(0, 64)), A("LP", 64 * k, 64 * k + 64), A("S1", 512 * k, 512 * k + 512), k == 0, k == 7)])
            act(A("YO", 0, 512, p=(0, 64)), PS(2, 0, 512, p=(0, 64))); dma(X(T.yp[:]), A("YO", 0, 512, p=(0, 64)), "act")
        s0 = b0 + 256; p6 = lambda a, b: A("P6", a, b); sp = lambda x: A("SP", x, 112, 16)
        spare = lambda o, a, b: [(o, M("N4096"), A("ONE", a, b), True, False), (o, M("In"), A("LB", a, b), False, False)]
        act(p6(40, 47), p6(16, 23), scale=c("pd"))
        mm(spare(PS(1, 384, 398), 0, 14) + [(PS(1, 384, 398), W("WB", x), A("SP", 112 + x, 336, 16), False, x == 15) for x in range(16)])
        tt(p6(32, 39), PS(1, 391, 398), p6(0, 7), O.mult); tt(p6(48, 62), PS(1, 384, 398), p6(16, 30), O.mult)
        tt(p6(64, 94), p6(32, 62), OB, O.add); tc(A("O2", 0, 30), p6(64, 94))
        g6 = lambda k, a=0, s=1: A("G6", 128 * k + a, 128 * k + 112, s); om = A("O2", 16, 23)
        pair = lambda k, m, s0, s1: [(PS(1, 112 * k + e, 112 * k + 112, 2), M(m), A("SP", 1 - e, 112, 2), s0 and e == 0, s1 and e == 1) for e in range(2)]
        if t < 3:
            act(g6(0), IX(S1w, om))
            mm(pair(2, "M7", True, True) + [(PS(1, 112, 224), M("Kx"), sa, True, False)] + pair(1, "Mz", False, False) + pair(0, "M4", False, False))
            mm([(PS(1, 0, 112), M("K89"), g6(0), False, True)])
            act(A("V2", 0, 336), PS(1, 0, 336)); tc(IX(S1w, A("O2", 16, 30)), A("V2", 0, 224))
            mm(spare(PS(0, 64, 71), 7, 14) + [(PS(0, 64, 71), W("Wp", x), A("G6", x, 112, 16), False, x == 15) for x in range(16)])
            tt(p6(8, 15), PS(0, 64, 71), p6(16, 23), O.mult); tt(p6(8, 15), p6(8, 15), A("CO", 96, 103), O.add); tc(A("O2", 32, 39), p6(8, 15))
            act(g6(1), IX(S1w, A("O2", 32, 39)), scale=c("keep")); tt(IX(S1w, A("O2", 32, 39)), g6(1), A("V2", 224, 336), O.add)
            act(g6(3), IX(Qw, om)); act(g6(4), g6(3), scale=c("lo"))
            act(g6(5, 0, 2), g6(3, 1, 2), scale=c("hi")); act(g6(5, 1, 2), g6(3, 0, 2), scale=c("hi"))
            tt(IX(Qw, om), g6(4), g6(5), O.add)
        else:
            mm(pair(1, "Mz", True, False) + pair(0, "M4", False, True))
            act(A("V2", 0, 224), PS(1, 0, 224)); tc(IX(S1w, A("O2", 16, 30)), A("V2", 0, 224))
            for k in range(8):
                mm([(PS(3, 0, 256, p=(0, 64)), A("LM", 64 * k, 64 * k + 64), A("S1", 256 * k, 256 * k + 256), k == 0, k == 7)])
            act(A("YO", 512, 768, p=(0, 64)), PS(3, 0, 256, p=(0, 64))); dma(X(T.ym[:]), A("YO", 512, 768, p=(0, 64)), "act")
        r6 = lambda k: A("R6", 128 * k, 128 * k + 112)
        act(r6(0), A("SB", s0, s0 + 112), scale=-1.0)
        tt(r6(1), A("RB", 112 * t, 112 * t + 112), r6(0), O.min, ext=("arr%d" % t, narr), after=[snd])
        act(r6(2), IX(r6(1), A("O2", 8, 15)), scale=c("hi"), f=F.Abs); act(r6(3), r6(1), scale=c("lo"), f=F.Abs)
        tt(IX(Qw, A("O2", 0, 7)), r6(2), r6(3), O.add)
    for k in range(len(cut) - 1):
        a, b = cut[k], cut[k + 1]; ra = (a + 16 * r) % 128
        dma(X(T.yq[ra:ra + b - a, :]), A("Q", 0, 2048, p=(a, b)), "act" if k % 2 else "sync", None, 3.5)
    emit(g, T, ops, 4 * nsnt, r)


def emit(g, T, ops, nsnt, r):
    n = len(ops); use = [[] for _ in ops]
    gap = lambda i, j: (GAP if ops[i]["deps"][j] else 0.0) + ops[j]["lat"]
    for i, o in enumerate(ops):
        for j in o["deps"]:
            use[j].append(i)
    pri = [0.0] * n
    for i in range(n - 1, -1, -1):
        pri[i] = ops[i]["cost"] + max([ops[i]["lat"]] + [gap(k, i) + pri[k] for k in use[i]])
    qs = ("pe", "dve", "act", "pool", "sync")
    pre = [[(j, gap(i, j)) for j in o["deps"]] for i, o in enumerate(ops)]; post = [[(k, gap(k, i)) for k in use[i]] for i in range(n)]

    def place(pre, post, pri, head):
        left = [len(x) for x in pre]; rdy = list(head); fin = [0.0] * n
        cand = {q: [] for q in qs}; free = {q: 0.0 for q in qs}; order = []
        for i in range(n):
            if not left[i]:
                cand[ops[i]["q"]].append(i)
        while len(order) < n:
            st, q = min((max(free[q], min(rdy[i] for i in cand[q])), q) for q in qs if cand[q])
            i = max((i for i in cand[q] if rdy[i] <= st + LOOK), key=lambda i: pri[i])
            cand[q].remove(i); fin[i] = max(st, rdy[i]) + ops[i]["cost"]; free[q] = fin[i]; order.append(i)
            for k, w in post[i]:
                rdy[k] = max(rdy[k], fin[i] + w); left[k] -= 1
                if not left[k]:
                    cand[ops[k]["q"]].append(k)
        return max(fin[i] + ops[i]["lat"] for i in range(n)), order, fin

    cost = [o["cost"] for o in ops]; lat = [o["lat"] for o in ops]

    def times(prv, nxt):
        left = [len(pre[i]) + (prv[i] >= 0) for i in range(n)]; st = [0.0] * n; order = [i for i in range(n) if not left[i]]
        for i in order:
            f = st[i] + cost[i]
            for k, w in post[i]:
                if st[k] < f + w:
                    st[k] = f + w
                left[k] -= 1
                if not left[k]:
                    order.append(k)
            k = nxt[i]
            if k >= 0:
                if st[k] < f:
                    st[k] = f
                left[k] -= 1
                if not left[k]:
                    order.append(k)
        tl = [0.0] * n
        for i in reversed(order):
            z = lat[i]
            for k, w in post[i]:
                if z < tl[k] + w:
                    z = tl[k] + w
            k = nxt[i]
            if k >= 0 and z < tl[k]:
                z = tl[k]
            tl[i] = z + cost[i]
        return max(tl) if len(order) == n else 1e9, st, tl

    def improve(order, rng):
        prv = [-1] * n; nxt = [-1] * n; end = {}
        for i in order:
            q = ops[i]["q"]
            if q in end:
                prv[i] = end[q]; nxt[end[q]] = i
            end[q] = i
        best = None; tabu = {}
        for it in range(SWAPS):
            T0, st, tl = times(prv, nxt)
            if best is None or T0 < best[0] - 1e-9:
                best = (T0, list(prv), list(nxt), st)
            elif T0 > best[0] + DRIFT:
                prv, nxt = list(best[1]), list(best[2]); continue
            pick = {}
            for u in range(n):
                v = nxt[u]
                if v >= 0 and st[u] + cost[u] + tl[v] > T0 - NEAR and st[v] < st[u] + cost[u] + 1e-9 and u not in ops[v]["deps"] and tabu.get((v, u), -1) < it:
                    a = prv[u]; b = nxt[v]
                    rv = max([st[j] + cost[j] + w for j, w in pre[v]] + [st[a] + cost[a] if a >= 0 else 0.0])
                    if rv >= st[u] + cost[u] - 1e-9:
                        continue
                    ru = max([st[j] + cost[j] + w for j, w in pre[u]] + [rv + cost[v]])
                    qu = cost[u] + max([tl[k] + w for k, w in post[u]] + [lat[u], tl[b] if b >= 0 else 0.0])
                    qv = cost[v] + max([tl[k] + w for k, w in post[v]] + [lat[v], qu])
                    e = max(rv + qv, ru + qu) - T0; z = max(e, 0.0) * GREED + float(rng.random()); w = int(st[u] / APART + it % 2 * 0.5)
                    if w not in pick or z < pick[w][3]:
                        pick[w] = (e, u, v, z)
            for w, (e, u, v, z) in pick.items():
                if w % 2 == it // 2 % 2 and e < TEMP * (1 - it / SWAPS) * float(rng.exponential()) + 1e-6:
                    a = prv[u]; b = nxt[v]; tabu[(u, v)] = it + TABU
                    if a >= 0:
                        nxt[a] = v
                    if b >= 0:
                        prv[b] = u
                    prv[v] = a; nxt[v] = u; prv[u] = v; nxt[u] = b
        st = best[3]; rank = {}; left = [len(pre[i]) + (best[1][i] >= 0) for i in range(n)]; todo = [i for i in range(n) if not left[i]]
        for i in todo:
            rank[i] = len(rank)
            for k in [k for k, w in post[i]] + [best[2][i]] * (best[2][i] >= 0):
                left[k] -= 1
                if not left[k]:
                    todo.append(k)
        return best[0], todo, [st[i] + cost[i] for i in range(n)]
    if n not in PLAN:
        best = None; rng = np.random.default_rng(1)
        for it in range(ITER):
            f = place(pre, post, pri, [0.0] * n)
            if best is None or f[0] < best[0]:
                best = f
            pri = place(post, pre, (f if it % 4 < 3 else best)[2], lat)[2]
            if it % 4 == 3:
                pri = [p + NOISE * float(z) for p, z in zip(pri, rng.random(n))]
        PLAN[n] = improve(best[1], rng) if SWAPS else best
    best = PLAN[n]; order, fin = best[1], best[2]
    INFO[r] = (best[0], {q: sum(o["cost"] for o in ops if o["q"] == q) for q in qs}, n)
    eng = dict(pe=g.tensor, dve=g.vector, act=g.scalar, pool=g, sync=g.sync)
    sig = {}; cnt = {q: 0 for q in qs}; seen = {q: {} for q in qs}; nd = 0; last = {}; knew = {}; waited = {}
    for i in order:
        o = ops[i]; q = o["q"]; e = eng[q]; need = {}
        for j, sm in o["deps"].items():
            if sm and ops[j]["kind"] != "rem":
                need[sig[j][0]] = max(need.get(sig[j][0], 0), sig[j][1])
        if o["ext"]:
            need[o["ext"][0]] = o["ext"][1]
        if q == "pool" and cnt[q]:
            need[q] = cnt[q]
        for s, v in sorted(need.items(), key=lambda z: -knew.get(z, (0,))[0]):
            if seen[q].get(s, 0) < v:
                e.wait_ge(T.sem[s], v); seen[q][s] = v; waited[s] = max(waited.get(s, 0), v)
                for s2, v2 in (knew.get((s, v), (0, {}))[1].items() if TRANS else ()):
                    seen[q][s2] = max(seen[q].get(s2, 0), v2)
        ins = o["fn"](e)
        if o["kind"] == "dma":
            sig[i] = ("d%d" % nd, 16); nd += 1; ins.then_inc(T.sem[sig[i][0]], 16); last[sig[i][0]] = 16
        elif o["kind"] == "c" and (q == "pool" or any(ops[k]["deps"][i] for k in use[i])):
            cnt[q] += 1; sig[i] = (q, cnt[q]); ins.then_inc(T.sem[q], 1); last[q] = cnt[q]
        if i in sig:
            knew[sig[i]] = (fin[i] + o["lat"], dict(seen[q]))
    for s, v in last.items():
        if waited.get(s, 0) < v:
            g.sync.wait_ge(T.sem[s], v)
    g.wait_ge(T.sem.snt, nsnt)
